import numpy as np
import ml_dtypes


def mxq(x, axis, fmt="e4m3"):
    dtype, down = {"e4m3": (ml_dtypes.float8_e4m3fn, 7), "e5m2": (ml_dtypes.float8_e5m2, 14)}[fmt]
    v = np.moveaxis(np.asarray(x, np.float32).astype(ml_dtypes.bfloat16).astype(np.float64), axis, -1)
    blocks = v.reshape(v.shape[:-1] + (-1, 32))
    amax = np.abs(blocks).max(-1, keepdims=True)
    byte = np.maximum(np.where(amax > 0, np.frexp(amax)[1] - 1 + 127, 0) - down, 1)
    scale = np.exp2(byte - 127.0)
    codes = (blocks / scale).astype(np.float32).astype(dtype).astype(np.float64)
    return np.moveaxis((codes * scale).reshape(v.shape), -1, axis)


WIDE = False


def mx_kscale(k):
    if not WIDE:
        return np.ones(k)
    levels = np.array([10, -10, 5, -5, 0])
    if k % 512:
        return np.exp2(np.random.permutation(np.resize(levels, k // 32))).repeat(32)
    a = np.empty((k // 512, 16))
    for p in range(k // 512):
        a[p, :8] = np.random.permutation(np.resize(levels, 8))
        for g in range(8):
            far = levels[np.abs(levels - a[p, g]) >= 10]
            a[p, g + 8] = far[np.random.randint(len(far))]
    return np.exp2(a.ravel()).repeat(32)


def f64(x):
    return np.asarray(x).astype(np.float64)


def striped(idx):
    return np.tile(np.asarray(idx).reshape(-1, 16).T, (8, 1)).astype(np.uint16)


def unstriped(offs):
    return offs[:16].T.reshape(-1).astype(np.int64)


E2M1 = np.array([0.0, 0.5, 1.0, 1.5, 2.0, 3.0, 4.0, 6.0, -0.0, -0.5, -1.0, -1.5, -2.0, -3.0, -4.0, -6.0])


def pack_weight(w, fmt):
    k, n = w.shape
    w = f64(np.asarray(w, np.float32).astype(ml_dtypes.bfloat16)).reshape(k // 32, 32, n)
    amax = np.abs(w).max(1)
    if fmt == "e4m3":
        byte = np.frexp(amax)[1] - 1 + 127 - 7
    else:
        mant, ex = np.frexp(amax / 6.0)
        byte = np.where(mant > 0.5, ex, ex - 1) + 127
    byte = np.clip(np.where(amax > 0, byte, 1), 1, 254)
    scaled = (w * np.exp2(127.0 - byte)[:, None, :]).reshape(k, n).astype(np.float32)
    by_word = np.ascontiguousarray(scaled.reshape(k // 512, 128, 4, n).transpose(0, 1, 3, 2))
    if fmt == "e4m3":
        words = by_word.astype(ml_dtypes.float8_e4m3fn).view(np.uint8)
    else:
        c = by_word.astype(ml_dtypes.float4_e2m1fn).view(np.uint8) & 0xF
        words = (c[..., 0::2] | (c[..., 1::2] << 4)).reshape(k // 512, 128, 2 * n)
    return np.ascontiguousarray(words), np.ascontiguousarray(byte.astype(np.uint8).reshape(k // 512, 16, n))


def unpack_weight(words, scales, fmt):
    g, _, n = scales.shape
    words = np.ascontiguousarray(words).reshape(g, 128, n, -1)
    if fmt == "e4m3":
        vals = words.view(ml_dtypes.float8_e4m3fn).astype(np.float64)
    else:
        nib = np.empty((g, 128, n, 4), np.uint8)
        nib[..., 0::2] = words & 0xF
        nib[..., 1::2] = words >> 4
        vals = E2M1[nib]
    vals = vals * np.repeat(np.exp2(scales.astype(np.float64) - 127.0), 8, axis=1)[..., None]
    return vals.transpose(0, 1, 3, 2).reshape(g * 512, n)


D, K, T, I, V, Q = 512, 512, 2048, 512, 1024, 128


def setup_inputs():
    n = np.random.standard_normal
    idx = np.random.permutation(T)[:I]
    idx2 = np.random.permutation(V)[:I]
    fd = mx_kscale(D)
    fk = mx_kscale(K)
    keysp = pack_weight(n((D, T)) / fd[:, None], "e2m1")
    return {
        "query": (n((D, Q)) * 0.5 / np.sqrt(D) * fd[:, None]).astype(np.float32),
        "keys_words": keysp[0],
        "keys_scales": keysp[1],
        "kn": np.tile(np.random.uniform(0.0, 1.0, T), (128, 1)).astype(np.float32),
        "hid": (n((K, Q)) * 1.0 / np.sqrt(K) * fk[:, None]).astype(np.float32),
        "voc": (n((K, V)) / fk[:, None]).astype(np.float32),
        "lam": (np.random.uniform(0.2, 0.8, (Q, 1))).astype(np.float32),
        "offs": striped(idx),
        "offs2": striped(idx2),
    }


def reference(query, keys_words, keys_scales, kn, hid, voc, lam, offs, offs2):
    idx = unstriped(offs)
    idx2 = unstriped(offs2)
    keysu = unpack_weight(keys_words, keys_scales, "e2m1")
    queryq = mxq(f64(query), 0, "e4m3")
    keysidxg = keysu[:, idx]
    a = queryq.T @ keysidxg
    s = 2.0 * a - f64(kn)[:1][:, idx]
    p = np.exp(s - np.max(s, axis=1, keepdims=True))
    w = p / np.sum(p, axis=1, keepdims=True)
    wf = np.zeros((Q, V))
    wf[:, idx2] = w
    hidq = mxq(f64(hid), 0, "e4m3")
    vocq = mxq(f64(voc), 0, "e4m3")
    b = hidq.T @ vocq
    r = np.exp(b - np.max(b, axis=1, keepdims=True))
    y = (f64(lam) * wf + (1.0 - f64(lam)) * r / np.sum(r, axis=1, keepdims=True)) * 512.0
    return y

@@ -1,0 +1,217 @@
+from contextlib import ExitStack
+
+import concourse.mybir as mybir
+from concourse.masks import make_identity
+
+D, K, T, I, V, Q = 512, 512, 2048, 512, 1024, 128
+FLOPS = 2 * D * Q * I + 2 * K * Q * V
+
+F32 = mybir.dt.float32
+BF16 = mybir.dt.bfloat16
+I32 = mybir.dt.int32
+U32 = mybir.dt.uint32
+U16 = mybir.dt.uint16
+U8 = mybir.dt.uint8
+FP8X4 = mybir.dt.float8_e4m3fn_x4
+FP4X4 = mybir.dt.float4_e2m1fn_x4
+ALU = mybir.AluOpType
+ACT = mybir.ActivationFunctionType
+AX = mybir.AxisListType
+
+P = 128
+PACK = 4
+CHUNK = 256
+BANK = 512
+HEAD = 128
+
+
+def tile_attend_knnlm_kernel(tc, query, keys_words, keys_scales, kn, hid, voc, lam, offs, offs2, out):
+    nc = tc.nc
+    with ExitStack() as ctx:
+        sb = ctx.enter_context(tc.tile_pool(name="sb", bufs=1))
+        ps = ctx.enter_context(tc.psum_pool(name="ps", bufs=1))
+
+        def tile(shape, dtype, name, tag=None):
+            return sb.tile(shape, dtype, name=name, tag=tag or name, align_bytes=64)
+
+        slots = tile([P, I // 16], U16, "slots")
+        places = tile([P, I // 16], U16, "places")
+        kn_win = tile([P, T], F32, "kn_win")
+        word_win = tile([P, T], U16, "word_win")
+        scale_win = tile([P, T], U8, "scale_win")
+        mixed = tile([P, V], F32, "mixed")
+        ident = tile([P, P], F32, "ident")
+        warm = tile([P, 1], F32, "warm")
+        lam_sb = tile([P, 1], F32, "lam_sb")
+        q_raw = tile([P, PACK, Q], F32, "q_raw")
+        h_raw = tile([P, PACK, Q], F32, "h_raw")
+        n_chunks = V // CHUNK
+        v_raw = [tile([P, PACK, CHUNK], F32, "v_raw%d" % c) for c in range(n_chunks)]
+
+        nc.vector.memset(scale_win[:].bitcast(I32), 0)
+        nc.vector.memset(kn_win[0 : P - 1, :], 0.0)
+        nc.vector.memset(mixed[:], 0.0)
+        make_identity(nc, ident[:])
+        nc.gpsimd.memset(warm[:], 0.0)
+        warm_out = tile([P, 1], F32, "warm_out")
+        nc.scalar.activation(warm_out[:], warm[:], ACT.Exp)
+
+        voc_r = voc.rearrange("(p j) w -> p j w", j=PACK)
+        nc.sync.dma_start(slots[:], offs)
+        nc.sync.dma_start(kn_win[P - 1 : P, :], kn[0:1, :])
+        nc.sync.dma_start(word_win[:].bitcast(I32), keys_words[0].bitcast(I32))
+        nc.sync.dma_start(q_raw[:], query.rearrange("(p j) w -> p j w", j=PACK))
+        for quad in range(4):
+            nc.sync.dma_start(
+                scale_win[32 * quad : 32 * quad + 4, :].bitcast(I32),
+                keys_scales[0, 4 * quad : 4 * quad + 4, :].bitcast(I32),
+            )
+
+        def load_vocab(c):
+            nc.sync.dma_start(v_raw[c][:], voc_r[:, :, c * CHUNK : (c + 1) * CHUNK])
+
+        nc.sync.dma_start(h_raw[:], hid.rearrange("(p j) w -> p j w", j=PACK))
+        load_vocab(0)
+        load_vocab(1)
+        nc.sync.dma_start(lam_sb[:], lam)
+        load_vocab(2)
+        nc.sync.dma_start(places[:], offs2)
+        load_vocab(3)
+
+        def cast(engine, grouped, raw, lo, hi):
+            dst = grouped[:, lo:hi, :].rearrange("p (c i) t -> p c t i", i=4)
+            src = raw[:, :, lo:hi].rearrange("p t (c i) -> p c t i", i=4)
+            if engine == "scalar":
+                nc.scalar.copy(dst, src)
+            else:
+                nc.vector.tensor_copy(dst, src)
+
+        def quantize(codes, scales, grouped):
+            nc.vector.quantize_mx(out=codes.bitcast(FP8X4), scales=scales, in_=grouped[:].rearrange("p w j -> p (w j)"))
+
+        q_bf = tile([P, Q, PACK], BF16, "q_bf")
+        h_bf = tile([P, Q, PACK], BF16, "h_bf")
+        v_bf = [tile([P, CHUNK, PACK], BF16, "v_bf%d" % c) for c in range(n_chunks)]
+        q_codes = tile([P, Q], U32, "q_codes")
+        q_scales = tile([P, Q], U8, "q_scales")
+        h_codes = tile([P, Q], U32, "h_codes")
+        h_scales = tile([P, Q], U8, "h_scales")
+        v_scales = tile([P, V], U8, "v_scales")
+
+        v_codes = tile([P, V], U32, "v_codes")
+        kn_g = tile([P, I], F32, "kn_g")
+        nc.vector.tensor_copy(kn_g[:], kn_win[:].indirect(slots[:]))
+        word_g = tile([P, I], U16, "word_g")
+        nc.vector.tensor_copy(word_g[:], word_win[:].indirect(slots[:]))
+        scale_g = tile([P, I], U8, "scale_g")
+        nc.vector.tensor_copy(scale_g[:], scale_win[:].indirect(slots[:]))
+
+        kn_ps = ps.tile([P, 4, P], F32, name="kn_ps")
+        for j in range(4):
+            nc.tensor.transpose(kn_ps[:, j, :], kn_g[:, j * P : (j + 1) * P], ident[:])
+        kn_col = tile([P, 4], F32, "kn_col")
+        cast("scalar", q_bf, q_raw, 0, Q)
+        nc.scalar.copy(kn_col[:], kn_ps[:, :, P - 1])
+        cast("scalar", h_bf, h_raw, 0, Q)
+        quantize(q_codes[:], q_scales[:], q_bf)
+        quantize(h_codes[:], h_scales[:], h_bf)
+        cast("scalar", v_bf[0], v_raw[0], 0, CHUNK // 2)
+        cast("vector", v_bf[0], v_raw[0], CHUNK // 2, CHUNK)
+
+        a_ps = ps.tile([P, 4, Q], F32, name="a_ps")
+        word_bytes = word_g[:].bitcast(U8)
+        for j in range(4):
+            nc.tensor.matmul_mx(
+                out=a_ps[:, j, :],
+                lhsT=word_bytes[:, 2 * P * j : 2 * P * (j + 1)].bitcast(FP4X4),
+                lhsT_scale=scale_g[:, P * j : P * (j + 1)],
+                rhs=q_codes[:].bitcast(FP8X4),
+                rhs_scale=q_scales[:],
+                start=True,
+                stop=True,
+            )
+        neg_t = tile([P, 4, Q], F32, "neg_t")
+        neg_ps = ps.tile([P, I], F32, name="neg_ps")
+        for j in range(4):
+            nc.scalar.activation(neg_t[:, j, :], a_ps[:, j, :], ACT.Identity, bias=kn_col[:, j : j + 1], scale=-2.0)
+        for j in range(4):
+            nc.tensor.transpose(neg_ps[:, j * P : (j + 1) * P], neg_t[:, j, :], ident[:])
+
+        b_ps = [ps.tile([P, BANK], F32, name="b_ps%d" % h) for h in range(2)]
+
+        def quantize_vocab(c):
+            cols = slice(c * CHUNK, (c + 1) * CHUNK)
+            quantize(v_codes[:, cols], v_scales[:, cols], v_bf[c])
+
+        def vocab_scores(c):
+            cols = slice(c * CHUNK, (c + 1) * CHUNK)
+            lo = (c % 2) * CHUNK
+            nc.tensor.matmul_mx(
+                out=b_ps[c // 2][:, lo : lo + CHUNK],
+                lhsT=h_codes[:].bitcast(FP8X4),
+                lhsT_scale=h_scales[:],
+                rhs=v_codes[:, cols].bitcast(FP8X4),
+                rhs_scale=v_scales[:, cols],
+                start=True,
+                stop=True,
+            )
+
+        quantize_vocab(0)
+        vocab_scores(0)
+        cast("scalar", v_bf[1], v_raw[1], 0, CHUNK // 2)
+        cast("vector", v_bf[1], v_raw[1], CHUNK // 2, CHUNK)
+        s_min = tile([P, 1], F32, "s_min")
+        nc.vector.tensor_reduce(s_min[:], neg_ps[:], AX.X, ALU.min)
+        p_sum = tile([P, 1], F32, "p_sum")
+        p_sb = tile([P, I], F32, "p_sb")
+        nc.scalar.activation(p_sb[:], neg_ps[:], ACT.Exp, bias=s_min[:], scale=-1.0, accum_out=p_sum[:])
+        quantize_vocab(1)
+        vocab_scores(1)
+        cast("vector", v_bf[2], v_raw[2], 0, CHUNK)
+        quantize_vocab(2)
+        vocab_scores(2)
+        cast("scalar", v_bf[3], v_raw[3], 0, CHUNK // 2)
+        cast("vector", v_bf[3], v_raw[3], CHUNK // 2, CHUNK)
+        b_neg0 = tile([P, 1], F32, "b_neg0")
+        nc.vector.tensor_reduce(b_neg0[:], b_ps[0][:], AX.X, ALU.max, negate=True)
+        quantize_vocab(3)
+        vocab_scores(3)
+
+        share = tile([P, 2], F32, "share")
+        minus_one = tile([P, 1], F32, "minus_one")
+        nc.gpsimd.memset(minus_one[:], -1.0)
+        nc.gpsimd.tensor_scalar(share[:, 0:1], lam_sb[:], 512.0, 0.0, ALU.mult, ALU.add)
+        nc.gpsimd.tensor_scalar(share[:, 1:2], lam_sb[:], -512.0, 512.0, ALU.mult, ALU.add)
+
+        def coefficient(total, col, name):
+            inv = tile([P, 1], F32, name + "_inv")
+            nc.gpsimd.tensor_tensor(inv[:], total[:], minus_one[:], ALU.pow)
+            coef = tile([P, 1], F32, name)
+            nc.gpsimd.tensor_tensor(coef[:], inv[:], share[:, col : col + 1], ALU.mult)
+            return coef
+
+        p_coef = coefficient(p_sum, 0, "p_coef")
+        w_head = tile([P, HEAD], F32, "w_head")
+        nc.scalar.activation(w_head[:], p_sb[:, 0:HEAD], ACT.Copy, scale=p_coef[:])
+        w_tail = tile([P, I - HEAD], F32, "w_tail", tag="v_bf3")
+        nc.scalar.activation(w_tail[:], p_sb[:, HEAD:I], ACT.Copy, scale=p_coef[:])
+
+        nc.vector.tensor_copy(mixed[:].indirect(places[:, 0 : HEAD // 16]), w_head[:])
+        b_bias = tile([P, 1], F32, "b_bias")
+        neg_b1 = tile([P, BANK], F32, "neg_b1")
+        nc.vector.tensor_scalar(neg_b1[:], b_ps[1][:], -1.0, b_neg0[:], ALU.mult, ALU.min, accum_out=b_bias[:])
+        nc.vector.tensor_copy(mixed[:].indirect(places[:, HEAD // 16 : I // 16]), w_tail[:])
+
+        r_sums = tile([P, 2], F32, "r_sums")
+        r_sb = [tile([P, BANK], F32, "r_sb%d" % h) for h in range(2)]
+        nc.scalar.activation(r_sb[0][:], b_ps[0][:], ACT.Exp, bias=b_bias[:], scale=1.0, accum_out=r_sums[:, 0:1])
+        nc.scalar.activation(r_sb[1][:], neg_b1[:], ACT.Exp, bias=b_bias[:], scale=-1.0, accum_out=r_sums[:, 1:2])
+        r_sum = tile([P, 1], F32, "r_sum")
+        nc.scalar.activation(r_sum[:], r_sums[:, 0:1], ACT.Identity, bias=r_sums[:, 1:2], scale=1.0)
+        r_coef = coefficient(r_sum, 1, "r_coef")
+
+        for h in range(2):
+            cols = slice(h * BANK, (h + 1) * BANK)
+            res = tile([P, BANK], F32, "res%d" % h)
+            nc.vector.scalar_tensor_tensor(res[:], r_sb[h][:], r_coef[:], mixed[:, cols], ALU.mult, ALU.add)
+            nc.sync.dma_start(out[:, cols], res[:])

@@ -16,61 +16,78 @@ FP8X4 = mybir.dt.float8_e4m3fn_x4
 FP4X4 = mybir.dt.float4_e2m1fn_x4
 ALU = mybir.AluOpType
 ACT = mybir.ActivationFunctionType
-AX = mybir.AxisListType
 
 P = 128
 PACK = 4
 CHUNK = 256
 BANK = 512
 HEAD = 128
+KN_SPLIT = 896
+KIB = 1024
 
 
 def tile_attend_knnlm_kernel(tc, query, keys_words, keys_scales, kn, hid, voc, lam, offs, offs2, out):
     nc = tc.nc
     with ExitStack() as ctx:
         sb = ctx.enter_context(tc.tile_pool(name="sb", bufs=1))
+        reuse = ctx.enter_context(tc.tile_pool(name="reuse", bufs=1))
         ps = ctx.enter_context(tc.psum_pool(name="ps", bufs=1))
 
-        def tile(shape, dtype, name, tag=None):
-            return sb.tile(shape, dtype, name=name, tag=tag or name, align_bytes=64)
+        def tile(shape, dtype, name):
+            return sb.tile(shape, dtype, name=name, align_bytes=64)
+
+        def tile_at(offset, shape, dtype, name):
+            return reuse.tile(shape, dtype, name=name, align_bytes=64, offset=offset)
+
+        at_kn, at_words, at_scales, at_col, at_s, at_min, at_raw2, at_codes3 = (
+            0, 8 * KIB, 12 * KIB, 26 * KIB, 15 * KIB, 18 * KIB, 20 * KIB, 24 * KIB)
 
         slots = tile([P, I // 16], U16, "slots")
         places = tile([P, I // 16], U16, "places")
-        kn_win = tile([P, T], F32, "kn_win")
-        word_win = tile([P, T], U16, "word_win")
-        scale_win = tile([P, T], U8, "scale_win")
+        kn_win = tile_at(at_kn, [P, T], F32, "kn_win")
+        word_win = tile_at(at_words, [P, T], U16, "word_win")
+        scale_win = tile_at(at_scales, [P, T], U8, "scale_win")
         mixed = tile([P, V], F32, "mixed")
         ident = tile([P, P], F32, "ident")
-        warm = tile([P, 1], F32, "warm")
+        zero = tile([P, 1], F32, "zero")
+        one = tile([P, 1], F32, "one")
         lam_sb = tile([P, 1], F32, "lam_sb")
         q_raw = tile([P, PACK, Q], F32, "q_raw")
         h_raw = tile([P, PACK, Q], F32, "h_raw")
-        n_chunks = V // CHUNK
-        v_raw = [tile([P, PACK, CHUNK], F32, "v_raw%d" % c) for c in range(n_chunks)]
+        v_raw = [
+            tile([P, PACK, CHUNK], F32, "v_raw0"),
+            tile([P, PACK, CHUNK], F32, "v_raw1"),
+            tile_at(at_raw2, [P, PACK, CHUNK], F32, "v_raw2"),
+            tile([P, PACK, CHUNK], F32, "v_raw3"),
+        ]
 
-        nc.vector.memset(scale_win[:].bitcast(I32), 0)
-        nc.vector.memset(kn_win[0 : P - 1, :], 0.0)
-        nc.vector.memset(mixed[:], 0.0)
+        nc.vector.memset(zero[:], 0.0)
+        scale_words = scale_win[:].bitcast(I32)
+        nc.vector.memset(scale_words[:, 0 : T // 4 - 1], 0)
+        nc.vector.memset(scale_words[:, T // 4 - 1 : T // 4], 0)
         make_identity(nc, ident[:])
-        nc.gpsimd.memset(warm[:], 0.0)
-        warm_out = tile([P, 1], F32, "warm_out")
-        nc.scalar.activation(warm_out[:], warm[:], ACT.Exp)
+        nc.vector.memset(kn_win[0 : P - 1, 0 : KN_SPLIT - 1], 0.0)
+        nc.vector.memset(kn_win[0 : P - 1, KN_SPLIT - 1 : KN_SPLIT], 0.0)
+        nc.gpsimd.memset(kn_win[0 : P - 1, KN_SPLIT:T], 0.0)
+        nc.gpsimd.memset(mixed[:], 0.0)
+        nc.scalar.activation(one[:], zero[:], ACT.Exp)
 
-        voc_r = voc.rearrange("(p j) w -> p j w", j=PACK)
+        def by_rows(x):
+            return x.rearrange("(p j) w -> p j w", j=PACK)
+
+        def load_vocab(c):
+            nc.sync.dma_start(v_raw[c][:], by_rows(voc)[:, :, c * CHUNK : (c + 1) * CHUNK])
+
         nc.sync.dma_start(slots[:], offs)
         nc.sync.dma_start(kn_win[P - 1 : P, :], kn[0:1, :])
+        nc.sync.dma_start(q_raw[:], by_rows(query))
         nc.sync.dma_start(word_win[:].bitcast(I32), keys_words[0].bitcast(I32))
-        nc.sync.dma_start(q_raw[:], query.rearrange("(p j) w -> p j w", j=PACK))
+        nc.sync.dma_start(h_raw[:], by_rows(hid))
         for quad in range(4):
             nc.sync.dma_start(
                 scale_win[32 * quad : 32 * quad + 4, :].bitcast(I32),
                 keys_scales[0, 4 * quad : 4 * quad + 4, :].bitcast(I32),
             )
-
-        def load_vocab(c):
-            nc.sync.dma_start(v_raw[c][:], voc_r[:, :, c * CHUNK : (c + 1) * CHUNK])
-
-        nc.sync.dma_start(h_raw[:], hid.rearrange("(p j) w -> p j w", j=PACK))
         load_vocab(0)
         load_vocab(1)
         nc.sync.dma_start(lam_sb[:], lam)
@@ -78,140 +95,125 @@ def tile_attend_knnlm_kernel(tc, query, keys_words, keys_scales, kn, hid, voc, l
         nc.sync.dma_start(places[:], offs2)
         load_vocab(3)
 
-        def cast(engine, grouped, raw, lo, hi):
-            dst = grouped[:, lo:hi, :].rearrange("p (c i) t -> p c t i", i=4)
-            src = raw[:, :, lo:hi].rearrange("p t (c i) -> p c t i", i=4)
-            if engine == "scalar":
-                nc.scalar.copy(dst, src)
-            else:
-                nc.vector.tensor_copy(dst, src)
+        def cast(copy, grouped, raw):
+            copy(
+                grouped[:].rearrange("p (c i) t -> p c t i", i=4),
+                raw[:].rearrange("p t (c i) -> p c t i", i=4),
+            )
 
         def quantize(codes, scales, grouped):
             nc.vector.quantize_mx(out=codes.bitcast(FP8X4), scales=scales, in_=grouped[:].rearrange("p w j -> p (w j)"))
 
-        q_bf = tile([P, Q, PACK], BF16, "q_bf")
-        h_bf = tile([P, Q, PACK], BF16, "h_bf")
-        v_bf = [tile([P, CHUNK, PACK], BF16, "v_bf%d" % c) for c in range(n_chunks)]
-        q_codes = tile([P, Q], U32, "q_codes")
-        q_scales = tile([P, Q], U8, "q_scales")
-        h_codes = tile([P, Q], U32, "h_codes")
-        h_scales = tile([P, Q], U8, "h_scales")
-        v_scales = tile([P, V], U8, "v_scales")
-
-        v_codes = tile([P, V], U32, "v_codes")
-        kn_g = tile([P, I], F32, "kn_g")
+        kn_g = tile_at(at_col, [P, I], F32, "kn_g")
         nc.vector.tensor_copy(kn_g[:], kn_win[:].indirect(slots[:]))
-        word_g = tile([P, I], U16, "word_g")
+        q_bf = tile([P, Q, PACK], BF16, "q_bf")
+        cast(nc.scalar.copy, q_bf, q_raw)
+        q_codes = tile_at(at_kn + 2 * KIB, [P, Q], U32, "q_codes")
+        q_scales = tile([P, Q], U8, "q_scales")
+        quantize(q_codes[:], q_scales[:], q_bf)
+        word_g = tile_at(at_kn, [P, I], U16, "word_g")
         nc.vector.tensor_copy(word_g[:], word_win[:].indirect(slots[:]))
-        scale_g = tile([P, I], U8, "scale_g")
+        scale_g = tile_at(at_kn + KIB, [P, I], U8, "scale_g")
         nc.vector.tensor_copy(scale_g[:], scale_win[:].indirect(slots[:]))
 
-        kn_ps = ps.tile([P, 4, P], F32, name="kn_ps")
+        turn_ps = ps.tile([P, 4, P], F32, name="turn_ps", tag="slot_bank")
         for j in range(4):
-            nc.tensor.transpose(kn_ps[:, j, :], kn_g[:, j * P : (j + 1) * P], ident[:])
+            nc.tensor.transpose(turn_ps[:, j, :], kn_g[:, j * P : (j + 1) * P], ident[:])
         kn_col = tile([P, 4], F32, "kn_col")
-        cast("scalar", q_bf, q_raw, 0, Q)
-        nc.scalar.copy(kn_col[:], kn_ps[:, :, P - 1])
-        cast("scalar", h_bf, h_raw, 0, Q)
-        quantize(q_codes[:], q_scales[:], q_bf)
-        quantize(h_codes[:], h_scales[:], h_bf)
-        cast("scalar", v_bf[0], v_raw[0], 0, CHUNK // 2)
-        cast("vector", v_bf[0], v_raw[0], CHUNK // 2, CHUNK)
+        nc.scalar.copy(kn_col[:], turn_ps[:, :, P - 1])
+        h_bf = tile_at(at_col, [P, Q, PACK], BF16, "h_bf")
+        cast(nc.scalar.copy, h_bf, h_raw)
+        spread_ps = ps.tile([P, I], F32, name="spread_ps")
+        for j in range(4):
+            nc.tensor.transpose(spread_ps[:, j * P : (j + 1) * P], kn_col[:, j : j + 1].to_broadcast([P, P]), ident[:])
+        kn_rows = tile([P, I], F32, "kn_rows")
+        nc.scalar.copy(kn_rows[:], spread_ps[:])
 
-        a_ps = ps.tile([P, 4, Q], F32, name="a_ps")
-        word_bytes = word_g[:].bitcast(U8)
-        for j in range(4):
-            nc.tensor.matmul_mx(
-                out=a_ps[:, j, :],
-                lhsT=word_bytes[:, 2 * P * j : 2 * P * (j + 1)].bitcast(FP4X4),
-                lhsT_scale=scale_g[:, P * j : P * (j + 1)],
-                rhs=q_codes[:].bitcast(FP8X4),
-                rhs_scale=q_scales[:],
-                start=True,
-                stop=True,
-            )
-        neg_t = tile([P, 4, Q], F32, "neg_t")
-        neg_ps = ps.tile([P, I], F32, name="neg_ps")
-        for j in range(4):
-            nc.scalar.activation(neg_t[:, j, :], a_ps[:, j, :], ACT.Identity, bias=kn_col[:, j : j + 1], scale=-2.0)
-        for j in range(4):
-            nc.tensor.transpose(neg_ps[:, j * P : (j + 1) * P], neg_t[:, j, :], ident[:])
+        a_ps = ps.tile([P, I], F32, name="a_ps", tag="slot_bank")
+        nc.tensor.matmul_mx(
+            out=a_ps[:],
+            lhsT=q_codes[:].bitcast(FP8X4),
+            lhsT_scale=q_scales[:],
+            rhs=word_g[:].bitcast(U8).bitcast(FP4X4),
+            rhs_scale=scale_g[:],
+            start=True,
+            stop=True,
+        )
+        h_codes = tile_at(at_scales, [P, Q], U32, "h_codes")
+        h_scales = tile([P, Q], U8, "h_scales")
+        quantize(h_codes[:], h_scales[:], h_bf)
+        s_sb = tile_at(at_s, [P, I], F32, "s_sb")
+        nc.vector.scalar_tensor_tensor(s_sb[:], a_ps[:], 2.0, kn_rows[:], ALU.mult, ALU.subtract)
+        neg_s = tile([P, I], F32, "neg_s")
+        s_bias = tile_at(at_min, [P, 1], F32, "s_bias")
+        nc.vector.tensor_scalar(neg_s[:], s_sb[:], -1.0, None, ALU.mult, ALU.min, accum_out=s_bias[:])
 
         b_ps = [ps.tile([P, BANK], F32, name="b_ps%d" % h) for h in range(2)]
+        v_scales = tile([P, V], U8, "v_scales")
 
-        def quantize_vocab(c):
+        def vocab_scores(c, grouped, codes):
             cols = slice(c * CHUNK, (c + 1) * CHUNK)
-            quantize(v_codes[:, cols], v_scales[:, cols], v_bf[c])
-
-        def vocab_scores(c):
-            cols = slice(c * CHUNK, (c + 1) * CHUNK)
-            lo = (c % 2) * CHUNK
+            quantize(codes[:], v_scales[:, cols], grouped)
             nc.tensor.matmul_mx(
-                out=b_ps[c // 2][:, lo : lo + CHUNK],
+                out=b_ps[c // 2][:, (c % 2) * CHUNK : (c % 2 + 1) * CHUNK],
                 lhsT=h_codes[:].bitcast(FP8X4),
                 lhsT_scale=h_scales[:],
-                rhs=v_codes[:, cols].bitcast(FP8X4),
+                rhs=codes[:].bitcast(FP8X4),
                 rhs_scale=v_scales[:, cols],
                 start=True,
                 stop=True,
             )
 
-        quantize_vocab(0)
-        vocab_scores(0)
-        cast("scalar", v_bf[1], v_raw[1], 0, CHUNK // 2)
-        cast("vector", v_bf[1], v_raw[1], CHUNK // 2, CHUNK)
-        s_min = tile([P, 1], F32, "s_min")
-        nc.vector.tensor_reduce(s_min[:], neg_ps[:], AX.X, ALU.min)
-        p_sum = tile([P, 1], F32, "p_sum")
-        p_sb = tile([P, I], F32, "p_sb")
-        nc.scalar.activation(p_sb[:], neg_ps[:], ACT.Exp, bias=s_min[:], scale=-1.0, accum_out=p_sum[:])
-        quantize_vocab(1)
-        vocab_scores(1)
-        cast("vector", v_bf[2], v_raw[2], 0, CHUNK)
-        quantize_vocab(2)
-        vocab_scores(2)
-        cast("scalar", v_bf[3], v_raw[3], 0, CHUNK // 2)
-        cast("vector", v_bf[3], v_raw[3], CHUNK // 2, CHUNK)
-        b_neg0 = tile([P, 1], F32, "b_neg0")
-        nc.vector.tensor_reduce(b_neg0[:], b_ps[0][:], AX.X, ALU.max, negate=True)
-        quantize_vocab(3)
-        vocab_scores(3)
-
         share = tile([P, 2], F32, "share")
         minus_one = tile([P, 1], F32, "minus_one")
-        nc.gpsimd.memset(minus_one[:], -1.0)
+        nc.gpsimd.tensor_scalar(minus_one[:], one[:], -1.0, 0.0, ALU.mult, ALU.add)
         nc.gpsimd.tensor_scalar(share[:, 0:1], lam_sb[:], 512.0, 0.0, ALU.mult, ALU.add)
         nc.gpsimd.tensor_scalar(share[:, 1:2], lam_sb[:], -512.0, 512.0, ALU.mult, ALU.add)
 
-        def coefficient(total, col, name):
-            inv = tile([P, 1], F32, name + "_inv")
-            nc.gpsimd.tensor_tensor(inv[:], total[:], minus_one[:], ALU.pow)
-            coef = tile([P, 1], F32, name)
-            nc.gpsimd.tensor_tensor(coef[:], inv[:], share[:, col : col + 1], ALU.mult)
-            return coef
-
-        p_coef = coefficient(p_sum, 0, "p_coef")
+        v_bf0 = tile([P, CHUNK, PACK], BF16, "v_bf0")
+        cast(nc.scalar.copy, v_bf0, v_raw[0])
+        p_sum = tile([P, 1], F32, "p_sum")
+        p_sb = tile([P, I], F32, "p_sb")
+        nc.scalar.activation(p_sb[:], neg_s[:], ACT.Exp, bias=s_bias[:], scale=-1.0, accum_out=p_sum[:])
+        vocab_scores(0, v_bf0, tile_at(at_s, [P, CHUNK], U32, "v_codes0"))
+        v_bf1 = tile_at(at_s + KIB, [P, CHUNK, PACK], BF16, "v_bf1")
+        cast(nc.vector.tensor_copy, v_bf1, v_raw[1])
+        p_inv = tile([P, 1], F32, "p_inv")
+        nc.vector.reciprocal(p_inv[:], p_sum[:])
+        vocab_scores(1, v_bf1, tile([P, CHUNK], U32, "v_codes1"))
         w_head = tile([P, HEAD], F32, "w_head")
-        nc.scalar.activation(w_head[:], p_sb[:, 0:HEAD], ACT.Copy, scale=p_coef[:])
-        w_tail = tile([P, I - HEAD], F32, "w_tail", tag="v_bf3")
+        nc.vector.tensor_scalar(w_head[:], p_sb[:, 0:HEAD], p_inv[:], share[:, 0:1], ALU.mult, ALU.mult)
+        v_bf2 = tile_at(at_min, [P, CHUNK, PACK], BF16, "v_bf2")
+        cast(nc.scalar.copy, v_bf2, v_raw[2])
+        v_bf3 = tile_at(at_raw2, [P, CHUNK, PACK], BF16, "v_bf3")
+        cast(nc.scalar.copy, v_bf3, v_raw[3])
+
+        b_bias0 = tile([P, 1], F32, "b_bias0")
+        neg_b = tile([P, V], F32, "neg_b")
+        nc.vector.tensor_scalar(neg_b[:, 0:BANK], b_ps[0][:], -1.0, None, ALU.mult, ALU.min, accum_out=b_bias0[:])
+        vocab_scores(2, v_bf2, tile([P, CHUNK], U32, "v_codes2"))
+        nc.vector.tensor_copy(mixed[:].indirect(places[:, 0 : HEAD // 16]), w_head[:])
+        vocab_scores(3, v_bf3, tile_at(at_codes3, [P, CHUNK], U32, "v_codes3"))
+
+        p_coef = tile([P, 1], F32, "p_coef")
+        nc.gpsimd.tensor_tensor(p_coef[:], p_inv[:], share[:, 0:1], ALU.mult)
+        w_tail = tile_at(at_codes3, [P, I - HEAD], F32, "w_tail")
         nc.scalar.activation(w_tail[:], p_sb[:, HEAD:I], ACT.Copy, scale=p_coef[:])
 
-        nc.vector.tensor_copy(mixed[:].indirect(places[:, 0 : HEAD // 16]), w_head[:])
         b_bias = tile([P, 1], F32, "b_bias")
-        neg_b1 = tile([P, BANK], F32, "neg_b1")
-        nc.vector.tensor_scalar(neg_b1[:], b_ps[1][:], -1.0, b_neg0[:], ALU.mult, ALU.min, accum_out=b_bias[:])
+        nc.vector.tensor_scalar(neg_b[:, BANK:V], b_ps[1][:], -1.0, b_bias0[:], ALU.mult, ALU.min, accum_out=b_bias[:])
         nc.vector.tensor_copy(mixed[:].indirect(places[:, HEAD // 16 : I // 16]), w_tail[:])
 
-        r_sums = tile([P, 2], F32, "r_sums")
-        r_sb = [tile([P, BANK], F32, "r_sb%d" % h) for h in range(2)]
-        nc.scalar.activation(r_sb[0][:], b_ps[0][:], ACT.Exp, bias=b_bias[:], scale=1.0, accum_out=r_sums[:, 0:1])
-        nc.scalar.activation(r_sb[1][:], neg_b1[:], ACT.Exp, bias=b_bias[:], scale=-1.0, accum_out=r_sums[:, 1:2])
         r_sum = tile([P, 1], F32, "r_sum")
-        nc.scalar.activation(r_sum[:], r_sums[:, 0:1], ACT.Identity, bias=r_sums[:, 1:2], scale=1.0)
-        r_coef = coefficient(r_sum, 1, "r_coef")
+        r_sb = tile([P, V], F32, "r_sb")
+        nc.scalar.activation(r_sb[:], neg_b[:], ACT.Exp, bias=b_bias[:], scale=-1.0, accum_out=r_sum[:])
+        r_inv = tile([P, 1], F32, "r_inv")
+        nc.gpsimd.tensor_tensor(r_inv[:], r_sum[:], minus_one[:], ALU.pow)
+        r_coef = tile([P, 1], F32, "r_coef")
+        nc.gpsimd.tensor_tensor(r_coef[:], r_inv[:], share[:, 1:2], ALU.mult)
 
         for h in range(2):
             cols = slice(h * BANK, (h + 1) * BANK)
             res = tile([P, BANK], F32, "res%d" % h)
-            nc.vector.scalar_tensor_tensor(res[:], r_sb[h][:], r_coef[:], mixed[:, cols], ALU.mult, ALU.add)
+            nc.vector.scalar_tensor_tensor(res[:], r_sb[:, cols], r_coef[:], mixed[:, cols], ALU.mult, ALU.add)
             nc.sync.dma_start(out[:, cols], res[:])

@@ -19,9 +19,9 @@ ACT = mybir.ActivationFunctionType
 
 P = 128
 PACK = 4
-CHUNK = 256
+CHUNK = 512
+SCALAR_COLS = (320, 160)
 BANK = 512
-HEAD = 128
 KN_SPLIT = 896
 KIB = 1024
 
@@ -39,13 +39,12 @@ def tile_attend_knnlm_kernel(tc, query, keys_words, keys_scales, kn, hid, voc, l
         def tile_at(offset, shape, dtype, name):
             return reuse.tile(shape, dtype, name=name, align_bytes=64, offset=offset)
 
-        at_kn, at_words, at_scales, at_col, at_s, at_min, at_raw2, at_codes3 = (
-            0, 8 * KIB, 12 * KIB, 26 * KIB, 15 * KIB, 18 * KIB, 20 * KIB, 24 * KIB)
+        at_kn, at_scales, at_rows, at_min, at_codes1 = 0, 8 * KIB, 10 * KIB, 14 * KIB, 18 * KIB
 
         slots = tile([P, I // 16], U16, "slots")
         places = tile([P, I // 16], U16, "places")
         kn_win = tile_at(at_kn, [P, T], F32, "kn_win")
-        word_win = tile_at(at_words, [P, T], U16, "word_win")
+        word_win = tile([P, T], U16, "word_win")
         scale_win = tile_at(at_scales, [P, T], U8, "scale_win")
         mixed = tile([P, V], F32, "mixed")
         ident = tile([P, P], F32, "ident")
@@ -54,12 +53,7 @@ def tile_attend_knnlm_kernel(tc, query, keys_words, keys_scales, kn, hid, voc, l
         lam_sb = tile([P, 1], F32, "lam_sb")
         q_raw = tile([P, PACK, Q], F32, "q_raw")
         h_raw = tile([P, PACK, Q], F32, "h_raw")
-        v_raw = [
-            tile([P, PACK, CHUNK], F32, "v_raw0"),
-            tile([P, PACK, CHUNK], F32, "v_raw1"),
-            tile_at(at_raw2, [P, PACK, CHUNK], F32, "v_raw2"),
-            tile([P, PACK, CHUNK], F32, "v_raw3"),
-        ]
+        v_raw = [tile([P, PACK, CHUNK], F32, "v_raw%d" % c) for c in range(2)]
 
         nc.vector.memset(zero[:], 0.0)
         scale_words = scale_win[:].bitcast(I32)
@@ -82,29 +76,27 @@ def tile_attend_knnlm_kernel(tc, query, keys_words, keys_scales, kn, hid, voc, l
         nc.sync.dma_start(kn_win[P - 1 : P, :], kn[0:1, :])
         nc.sync.dma_start(q_raw[:], by_rows(query))
         nc.sync.dma_start(word_win[:].bitcast(I32), keys_words[0].bitcast(I32))
-        nc.sync.dma_start(h_raw[:], by_rows(hid))
         for quad in range(4):
             nc.sync.dma_start(
                 scale_win[32 * quad : 32 * quad + 4, :].bitcast(I32),
                 keys_scales[0, 4 * quad : 4 * quad + 4, :].bitcast(I32),
             )
+        nc.sync.dma_start(h_raw[:], by_rows(hid))
         load_vocab(0)
-        load_vocab(1)
         nc.sync.dma_start(lam_sb[:], lam)
-        load_vocab(2)
         nc.sync.dma_start(places[:], offs2)
-        load_vocab(3)
+        load_vocab(1)
 
-        def cast(copy, grouped, raw):
+        def cast(copy, grouped, raw, cols=slice(0, Q)):
             copy(
-                grouped[:].rearrange("p (c i) t -> p c t i", i=4),
-                raw[:].rearrange("p t (c i) -> p c t i", i=4),
+                grouped[:, cols, :].rearrange("p (c i) t -> p c t i", i=4),
+                raw[:, :, cols].rearrange("p t (c i) -> p c t i", i=4),
             )
 
         def quantize(codes, scales, grouped):
             nc.vector.quantize_mx(out=codes.bitcast(FP8X4), scales=scales, in_=grouped[:].rearrange("p w j -> p (w j)"))
 
-        kn_g = tile_at(at_col, [P, I], F32, "kn_g")
+        kn_g = tile_at(at_rows, [P, I], F32, "kn_g")
         nc.vector.tensor_copy(kn_g[:], kn_win[:].indirect(slots[:]))
         q_bf = tile([P, Q, PACK], BF16, "q_bf")
         cast(nc.scalar.copy, q_bf, q_raw)
@@ -121,7 +113,7 @@ def tile_attend_knnlm_kernel(tc, query, keys_words, keys_scales, kn, hid, voc, l
             nc.tensor.transpose(turn_ps[:, j, :], kn_g[:, j * P : (j + 1) * P], ident[:])
         kn_col = tile([P, 4], F32, "kn_col")
         nc.scalar.copy(kn_col[:], turn_ps[:, :, P - 1])
-        h_bf = tile_at(at_col, [P, Q, PACK], BF16, "h_bf")
+        h_bf = tile_at(at_rows, [P, Q, PACK], BF16, "h_bf")
         cast(nc.scalar.copy, h_bf, h_raw)
         spread_ps = ps.tile([P, I], F32, name="spread_ps")
         for j in range(4):
@@ -142,27 +134,43 @@ def tile_attend_knnlm_kernel(tc, query, keys_words, keys_scales, kn, hid, voc, l
         h_codes = tile_at(at_scales, [P, Q], U32, "h_codes")
         h_scales = tile([P, Q], U8, "h_scales")
         quantize(h_codes[:], h_scales[:], h_bf)
-        s_sb = tile_at(at_s, [P, I], F32, "s_sb")
+        s_sb = tile([P, I], F32, "s_sb")
         nc.vector.scalar_tensor_tensor(s_sb[:], a_ps[:], 2.0, kn_rows[:], ALU.mult, ALU.subtract)
-        neg_s = tile([P, I], F32, "neg_s")
-        s_bias = tile_at(at_min, [P, 1], F32, "s_bias")
-        nc.vector.tensor_scalar(neg_s[:], s_sb[:], -1.0, None, ALU.mult, ALU.min, accum_out=s_bias[:])
 
-        b_ps = [ps.tile([P, BANK], F32, name="b_ps%d" % h) for h in range(2)]
-        v_scales = tile([P, V], U8, "v_scales")
+        b_ps = [ps.tile([P, CHUNK], F32, name="b_ps%d" % c) for c in range(2)]
+
+        def cast_vocab(c, grouped):
+            cast(nc.scalar.copy, grouped, v_raw[c], slice(0, SCALAR_COLS[c]))
+            cast(nc.vector.tensor_copy, grouped, v_raw[c], slice(SCALAR_COLS[c], CHUNK))
 
         def vocab_scores(c, grouped, codes):
-            cols = slice(c * CHUNK, (c + 1) * CHUNK)
-            quantize(codes[:], v_scales[:, cols], grouped)
+            scales = tile([P, CHUNK], U8, "v_scales%d" % c)
+            quantize(codes[:], scales[:], grouped)
             nc.tensor.matmul_mx(
-                out=b_ps[c // 2][:, (c % 2) * CHUNK : (c % 2 + 1) * CHUNK],
+                out=b_ps[c][:],
                 lhsT=h_codes[:].bitcast(FP8X4),
                 lhsT_scale=h_scales[:],
                 rhs=codes[:].bitcast(FP8X4),
-                rhs_scale=v_scales[:, cols],
+                rhs_scale=scales[:],
                 start=True,
                 stop=True,
             )
+
+        v_bf0 = tile_at(at_rows, [P, CHUNK, PACK], BF16, "v_bf0")
+        cast_vocab(0, v_bf0)
+        neg_s = tile([P, I], F32, "neg_s")
+        s_bias = tile_at(at_min, [P, 1], F32, "s_bias")
+        nc.vector.tensor_scalar(neg_s[:], s_sb[:], -1.0, None, ALU.mult, ALU.min, accum_out=s_bias[:])
+        p_sum = tile([P, 1], F32, "p_sum")
+        p_sb = tile([P, I], F32, "p_sb")
+        nc.scalar.activation(p_sb[:], neg_s[:], ACT.Exp, bias=s_bias[:], scale=-1.0, accum_out=p_sum[:])
+        vocab_scores(0, v_bf0, tile([P, CHUNK], U32, "v_codes0"))
+        v_bf1 = tile_at(at_min, [P, CHUNK, PACK], BF16, "v_bf1")
+        cast_vocab(1, v_bf1)
+        vocab_scores(1, v_bf1, tile_at(at_codes1, [P, CHUNK], U32, "v_codes1"))
+        b_bias0 = tile([P, 1], F32, "b_bias0")
+        neg_b = tile_at(at_min, [P, V], F32, "neg_b")
+        nc.vector.tensor_scalar(neg_b[:, 0:BANK], b_ps[0][:], -1.0, None, ALU.mult, ALU.min, accum_out=b_bias0[:])
 
         share = tile([P, 2], F32, "share")
         minus_one = tile([P, 1], F32, "minus_one")
@@ -170,47 +178,25 @@ def tile_attend_knnlm_kernel(tc, query, keys_words, keys_scales, kn, hid, voc, l
         nc.gpsimd.tensor_scalar(share[:, 0:1], lam_sb[:], 512.0, 0.0, ALU.mult, ALU.add)
         nc.gpsimd.tensor_scalar(share[:, 1:2], lam_sb[:], -512.0, 512.0, ALU.mult, ALU.add)
 
-        v_bf0 = tile([P, CHUNK, PACK], BF16, "v_bf0")
-        cast(nc.scalar.copy, v_bf0, v_raw[0])
-        p_sum = tile([P, 1], F32, "p_sum")
-        p_sb = tile([P, I], F32, "p_sb")
-        nc.scalar.activation(p_sb[:], neg_s[:], ACT.Exp, bias=s_bias[:], scale=-1.0, accum_out=p_sum[:])
-        vocab_scores(0, v_bf0, tile_at(at_s, [P, CHUNK], U32, "v_codes0"))
-        v_bf1 = tile_at(at_s + KIB, [P, CHUNK, PACK], BF16, "v_bf1")
-        cast(nc.vector.tensor_copy, v_bf1, v_raw[1])
-        p_inv = tile([P, 1], F32, "p_inv")
-        nc.vector.reciprocal(p_inv[:], p_sum[:])
-        vocab_scores(1, v_bf1, tile([P, CHUNK], U32, "v_codes1"))
-        w_head = tile([P, HEAD], F32, "w_head")
-        nc.vector.tensor_scalar(w_head[:], p_sb[:, 0:HEAD], p_inv[:], share[:, 0:1], ALU.mult, ALU.mult)
-        v_bf2 = tile_at(at_min, [P, CHUNK, PACK], BF16, "v_bf2")
-        cast(nc.scalar.copy, v_bf2, v_raw[2])
-        v_bf3 = tile_at(at_raw2, [P, CHUNK, PACK], BF16, "v_bf3")
-        cast(nc.scalar.copy, v_bf3, v_raw[3])
+        def coefficient(total, col, name):
+            inverse = tile([P, 1], F32, name + "_inverse")
+            nc.gpsimd.tensor_tensor(inverse[:], total[:], minus_one[:], ALU.pow)
+            coef = tile([P, 1], F32, name)
+            nc.gpsimd.tensor_tensor(coef[:], inverse[:], share[:, col : col + 1], ALU.mult)
+            return coef
 
-        b_bias0 = tile([P, 1], F32, "b_bias0")
-        neg_b = tile([P, V], F32, "neg_b")
-        nc.vector.tensor_scalar(neg_b[:, 0:BANK], b_ps[0][:], -1.0, None, ALU.mult, ALU.min, accum_out=b_bias0[:])
-        vocab_scores(2, v_bf2, tile([P, CHUNK], U32, "v_codes2"))
-        nc.vector.tensor_copy(mixed[:].indirect(places[:, 0 : HEAD // 16]), w_head[:])
-        vocab_scores(3, v_bf3, tile_at(at_codes3, [P, CHUNK], U32, "v_codes3"))
-
-        p_coef = tile([P, 1], F32, "p_coef")
-        nc.gpsimd.tensor_tensor(p_coef[:], p_inv[:], share[:, 0:1], ALU.mult)
-        w_tail = tile_at(at_codes3, [P, I - HEAD], F32, "w_tail")
-        nc.scalar.activation(w_tail[:], p_sb[:, HEAD:I], ACT.Copy, scale=p_coef[:])
+        p_coef = coefficient(p_sum, 0, "p_coef")
+        w_sb = tile_at(at_codes1, [P, I], F32, "w_sb")
+        nc.scalar.activation(w_sb[:], p_sb[:], ACT.Copy, scale=p_coef[:])
 
         b_bias = tile([P, 1], F32, "b_bias")
         nc.vector.tensor_scalar(neg_b[:, BANK:V], b_ps[1][:], -1.0, b_bias0[:], ALU.mult, ALU.min, accum_out=b_bias[:])
-        nc.vector.tensor_copy(mixed[:].indirect(places[:, HEAD // 16 : I // 16]), w_tail[:])
+        nc.vector.tensor_copy(mixed[:].indirect(places[:]), w_sb[:])
 
         r_sum = tile([P, 1], F32, "r_sum")
         r_sb = tile([P, V], F32, "r_sb")
         nc.scalar.activation(r_sb[:], neg_b[:], ACT.Exp, bias=b_bias[:], scale=-1.0, accum_out=r_sum[:])
-        r_inv = tile([P, 1], F32, "r_inv")
-        nc.gpsimd.tensor_tensor(r_inv[:], r_sum[:], minus_one[:], ALU.pow)
-        r_coef = tile([P, 1], F32, "r_coef")
-        nc.gpsimd.tensor_tensor(r_coef[:], r_inv[:], share[:, 1:2], ALU.mult)
+        r_coef = coefficient(r_sum, 1, "r_coef")
 
         for h in range(2):
             cols = slice(h * BANK, (h + 1) * BANK)

@@ -20,7 +20,7 @@ ACT = mybir.ActivationFunctionType
 P = 128
 PACK = 4
 CHUNK = 512
-SCALAR_COLS = (320, 160)
+SCALAR_COLS = (256, 192)
 BANK = 512
 KN_SPLIT = 896
 KIB = 1024
@@ -83,9 +83,9 @@ def tile_attend_knnlm_kernel(tc, query, keys_words, keys_scales, kn, hid, voc, l
             )
         nc.sync.dma_start(h_raw[:], by_rows(hid))
         load_vocab(0)
+        load_vocab(1)
         nc.sync.dma_start(lam_sb[:], lam)
         nc.sync.dma_start(places[:], offs2)
-        load_vocab(1)
 
         def cast(copy, grouped, raw, cols=slice(0, Q)):
             copy(
@@ -134,14 +134,17 @@ def tile_attend_knnlm_kernel(tc, query, keys_words, keys_scales, kn, hid, voc, l
         h_codes = tile_at(at_scales, [P, Q], U32, "h_codes")
         h_scales = tile([P, Q], U8, "h_scales")
         quantize(h_codes[:], h_scales[:], h_bf)
-        s_sb = tile([P, I], F32, "s_sb")
+        s_sb = tile_at(at_min, [P, I], F32, "s_sb")
         nc.vector.scalar_tensor_tensor(s_sb[:], a_ps[:], 2.0, kn_rows[:], ALU.mult, ALU.subtract)
 
         b_ps = [ps.tile([P, CHUNK], F32, name="b_ps%d" % c) for c in range(2)]
 
+        def gpsimd_copy(dst, src):
+            nc.gpsimd.tensor_scalar(dst, src, 1.0, 0.0, ALU.mult, ALU.add)
+
         def cast_vocab(c, grouped):
             cast(nc.scalar.copy, grouped, v_raw[c], slice(0, SCALAR_COLS[c]))
-            cast(nc.vector.tensor_copy, grouped, v_raw[c], slice(SCALAR_COLS[c], CHUNK))
+            cast((gpsimd_copy, nc.vector.tensor_copy)[c], grouped, v_raw[c], slice(SCALAR_COLS[c], CHUNK))
 
         def vocab_scores(c, grouped, codes):
             scales = tile([P, CHUNK], U8, "v_scales%d" % c)
@@ -159,7 +162,7 @@ def tile_attend_knnlm_kernel(tc, query, keys_words, keys_scales, kn, hid, voc, l
         v_bf0 = tile_at(at_rows, [P, CHUNK, PACK], BF16, "v_bf0")
         cast_vocab(0, v_bf0)
         neg_s = tile([P, I], F32, "neg_s")
-        s_bias = tile_at(at_min, [P, 1], F32, "s_bias")
+        s_bias = tile([P, 1], F32, "s_bias")
         nc.vector.tensor_scalar(neg_s[:], s_sb[:], -1.0, None, ALU.mult, ALU.min, accum_out=s_bias[:])
         p_sum = tile([P, 1], F32, "p_sum")
         p_sb = tile([P, I], F32, "p_sb")

@@ -20,8 +20,8 @@ ACT = mybir.ActivationFunctionType
 P = 128
 PACK = 4
 CHUNK = 512
-SCALAR_COLS = (256, 192)
-BANK = 512
+OUT_SCALE = 512.0
+SCALAR_COLS = (320, 160)
 KN_SPLIT = 896
 KIB = 1024
 
@@ -39,7 +39,7 @@ def tile_attend_knnlm_kernel(tc, query, keys_words, keys_scales, kn, hid, voc, l
         def tile_at(offset, shape, dtype, name):
             return reuse.tile(shape, dtype, name=name, align_bytes=64, offset=offset)
 
-        at_kn, at_scales, at_rows, at_min, at_codes1 = 0, 8 * KIB, 10 * KIB, 14 * KIB, 18 * KIB
+        at_kn, at_scales, at_kn_g, at_s, at_codes1 = 0, 8 * KIB, 10 * KIB, 14 * KIB, 18 * KIB
 
         slots = tile([P, I // 16], U16, "slots")
         places = tile([P, I // 16], U16, "places")
@@ -53,24 +53,22 @@ def tile_attend_knnlm_kernel(tc, query, keys_words, keys_scales, kn, hid, voc, l
         lam_sb = tile([P, 1], F32, "lam_sb")
         q_raw = tile([P, PACK, Q], F32, "q_raw")
         h_raw = tile([P, PACK, Q], F32, "h_raw")
-        v_raw = [tile([P, PACK, CHUNK], F32, "v_raw%d" % c) for c in range(2)]
+        v_raw = [tile([P, PACK, CHUNK], F32, "v_raw%d" % c) for c in range(V // CHUNK)]
+
+        def zero_on_vector(ap, columns, value):
+            nc.vector.memset(ap[:, 0 : columns - 1], value)
+            nc.vector.memset(ap[:, columns - 1 : columns], value)
 
         nc.vector.memset(zero[:], 0.0)
-        scale_words = scale_win[:].bitcast(I32)
-        nc.vector.memset(scale_words[:, 0 : T // 4 - 1], 0)
-        nc.vector.memset(scale_words[:, T // 4 - 1 : T // 4], 0)
+        zero_on_vector(scale_win[:].bitcast(I32), T // 4, 0)
         make_identity(nc, ident[:])
-        nc.vector.memset(kn_win[0 : P - 1, 0 : KN_SPLIT - 1], 0.0)
-        nc.vector.memset(kn_win[0 : P - 1, KN_SPLIT - 1 : KN_SPLIT], 0.0)
+        zero_on_vector(kn_win[0 : P - 1, :], KN_SPLIT, 0.0)
         nc.gpsimd.memset(kn_win[0 : P - 1, KN_SPLIT:T], 0.0)
         nc.gpsimd.memset(mixed[:], 0.0)
         nc.scalar.activation(one[:], zero[:], ACT.Exp)
 
         def by_rows(x):
             return x.rearrange("(p j) w -> p j w", j=PACK)
-
-        def load_vocab(c):
-            nc.sync.dma_start(v_raw[c][:], by_rows(voc)[:, :, c * CHUNK : (c + 1) * CHUNK])
 
         nc.sync.dma_start(slots[:], offs)
         nc.sync.dma_start(kn_win[P - 1 : P, :], kn[0:1, :])
@@ -82,8 +80,8 @@ def tile_attend_knnlm_kernel(tc, query, keys_words, keys_scales, kn, hid, voc, l
                 keys_scales[0, 4 * quad : 4 * quad + 4, :].bitcast(I32),
             )
         nc.sync.dma_start(h_raw[:], by_rows(hid))
-        load_vocab(0)
-        load_vocab(1)
+        for c in range(V // CHUNK):
+            nc.sync.dma_start(v_raw[c][:], by_rows(voc)[:, :, c * CHUNK : (c + 1) * CHUNK])
         nc.sync.dma_start(lam_sb[:], lam)
         nc.sync.dma_start(places[:], offs2)
 
@@ -96,7 +94,7 @@ def tile_attend_knnlm_kernel(tc, query, keys_words, keys_scales, kn, hid, voc, l
         def quantize(codes, scales, grouped):
             nc.vector.quantize_mx(out=codes.bitcast(FP8X4), scales=scales, in_=grouped[:].rearrange("p w j -> p (w j)"))
 
-        kn_g = tile_at(at_rows, [P, I], F32, "kn_g")
+        kn_g = tile_at(at_kn_g, [P, I], F32, "kn_g")
         nc.vector.tensor_copy(kn_g[:], kn_win[:].indirect(slots[:]))
         q_bf = tile([P, Q, PACK], BF16, "q_bf")
         cast(nc.scalar.copy, q_bf, q_raw)
@@ -108,15 +106,16 @@ def tile_attend_knnlm_kernel(tc, query, keys_words, keys_scales, kn, hid, voc, l
         scale_g = tile_at(at_kn + KIB, [P, I], U8, "scale_g")
         nc.vector.tensor_copy(scale_g[:], scale_win[:].indirect(slots[:]))
 
-        turn_ps = ps.tile([P, 4, P], F32, name="turn_ps", tag="slot_bank")
-        for j in range(4):
+        blocks = I // P
+        turn_ps = ps.tile([P, blocks, P], F32, name="turn_ps", tag="slot_bank")
+        for j in range(blocks):
             nc.tensor.transpose(turn_ps[:, j, :], kn_g[:, j * P : (j + 1) * P], ident[:])
-        kn_col = tile([P, 4], F32, "kn_col")
+        kn_col = tile([P, blocks], F32, "kn_col")
         nc.scalar.copy(kn_col[:], turn_ps[:, :, P - 1])
-        h_bf = tile_at(at_rows, [P, Q, PACK], BF16, "h_bf")
+        h_bf = tile_at(at_kn_g, [P, Q, PACK], BF16, "h_bf")
         cast(nc.scalar.copy, h_bf, h_raw)
         spread_ps = ps.tile([P, I], F32, name="spread_ps")
-        for j in range(4):
+        for j in range(blocks):
             nc.tensor.transpose(spread_ps[:, j * P : (j + 1) * P], kn_col[:, j : j + 1].to_broadcast([P, P]), ident[:])
         kn_rows = tile([P, I], F32, "kn_rows")
         nc.scalar.copy(kn_rows[:], spread_ps[:])
@@ -134,17 +133,17 @@ def tile_attend_knnlm_kernel(tc, query, keys_words, keys_scales, kn, hid, voc, l
         h_codes = tile_at(at_scales, [P, Q], U32, "h_codes")
         h_scales = tile([P, Q], U8, "h_scales")
         quantize(h_codes[:], h_scales[:], h_bf)
-        s_sb = tile_at(at_min, [P, I], F32, "s_sb")
+        s_sb = tile_at(at_s, [P, I], F32, "s_sb")
         nc.vector.scalar_tensor_tensor(s_sb[:], a_ps[:], 2.0, kn_rows[:], ALU.mult, ALU.subtract)
 
-        b_ps = [ps.tile([P, CHUNK], F32, name="b_ps%d" % c) for c in range(2)]
+        b_ps = [ps.tile([P, CHUNK], F32, name="b_ps%d" % c) for c in range(V // CHUNK)]
 
         def gpsimd_copy(dst, src):
             nc.gpsimd.tensor_scalar(dst, src, 1.0, 0.0, ALU.mult, ALU.add)
 
-        def cast_vocab(c, grouped):
+        def cast_vocab(c, grouped, partner_copy):
             cast(nc.scalar.copy, grouped, v_raw[c], slice(0, SCALAR_COLS[c]))
-            cast((gpsimd_copy, nc.vector.tensor_copy)[c], grouped, v_raw[c], slice(SCALAR_COLS[c], CHUNK))
+            cast(partner_copy, grouped, v_raw[c], slice(SCALAR_COLS[c], CHUNK))
 
         def vocab_scores(c, grouped, codes):
             scales = tile([P, CHUNK], U8, "v_scales%d" % c)
@@ -159,27 +158,30 @@ def tile_attend_knnlm_kernel(tc, query, keys_words, keys_scales, kn, hid, voc, l
                 stop=True,
             )
 
-        v_bf0 = tile_at(at_rows, [P, CHUNK, PACK], BF16, "v_bf0")
-        cast_vocab(0, v_bf0)
+        def negate_with_minimum(negated, scores, start, minimum):
+            nc.vector.tensor_scalar(negated, scores, -1.0, start, ALU.mult, ALU.min, accum_out=minimum)
+
+        v_bf0 = tile_at(at_kn_g, [P, CHUNK, PACK], BF16, "v_bf0")
+        cast_vocab(0, v_bf0, gpsimd_copy)
         neg_s = tile([P, I], F32, "neg_s")
         s_bias = tile([P, 1], F32, "s_bias")
-        nc.vector.tensor_scalar(neg_s[:], s_sb[:], -1.0, None, ALU.mult, ALU.min, accum_out=s_bias[:])
+        negate_with_minimum(neg_s[:], s_sb[:], None, s_bias[:])
         p_sum = tile([P, 1], F32, "p_sum")
         p_sb = tile([P, I], F32, "p_sb")
         nc.scalar.activation(p_sb[:], neg_s[:], ACT.Exp, bias=s_bias[:], scale=-1.0, accum_out=p_sum[:])
         vocab_scores(0, v_bf0, tile([P, CHUNK], U32, "v_codes0"))
-        v_bf1 = tile_at(at_min, [P, CHUNK, PACK], BF16, "v_bf1")
-        cast_vocab(1, v_bf1)
+        v_bf1 = tile_at(at_s, [P, CHUNK, PACK], BF16, "v_bf1")
+        cast_vocab(1, v_bf1, nc.vector.tensor_copy)
         vocab_scores(1, v_bf1, tile_at(at_codes1, [P, CHUNK], U32, "v_codes1"))
         b_bias0 = tile([P, 1], F32, "b_bias0")
-        neg_b = tile_at(at_min, [P, V], F32, "neg_b")
-        nc.vector.tensor_scalar(neg_b[:, 0:BANK], b_ps[0][:], -1.0, None, ALU.mult, ALU.min, accum_out=b_bias0[:])
+        neg_b = tile_at(at_s, [P, V], F32, "neg_b")
+        negate_with_minimum(neg_b[:, 0:CHUNK], b_ps[0][:], None, b_bias0[:])
 
         share = tile([P, 2], F32, "share")
         minus_one = tile([P, 1], F32, "minus_one")
         nc.gpsimd.tensor_scalar(minus_one[:], one[:], -1.0, 0.0, ALU.mult, ALU.add)
-        nc.gpsimd.tensor_scalar(share[:, 0:1], lam_sb[:], 512.0, 0.0, ALU.mult, ALU.add)
-        nc.gpsimd.tensor_scalar(share[:, 1:2], lam_sb[:], -512.0, 512.0, ALU.mult, ALU.add)
+        nc.gpsimd.tensor_scalar(share[:, 0:1], lam_sb[:], OUT_SCALE, 0.0, ALU.mult, ALU.add)
+        nc.gpsimd.tensor_scalar(share[:, 1:2], lam_sb[:], -OUT_SCALE, OUT_SCALE, ALU.mult, ALU.add)
 
         def coefficient(total, col, name):
             inverse = tile([P, 1], F32, name + "_inverse")
@@ -193,7 +195,7 @@ def tile_attend_knnlm_kernel(tc, query, keys_words, keys_scales, kn, hid, voc, l
         nc.scalar.activation(w_sb[:], p_sb[:], ACT.Copy, scale=p_coef[:])
 
         b_bias = tile([P, 1], F32, "b_bias")
-        nc.vector.tensor_scalar(neg_b[:, BANK:V], b_ps[1][:], -1.0, b_bias0[:], ALU.mult, ALU.min, accum_out=b_bias[:])
+        negate_with_minimum(neg_b[:, CHUNK:V], b_ps[1][:], b_bias0[:], b_bias[:])
         nc.vector.tensor_copy(mixed[:].indirect(places[:]), w_sb[:])
 
         r_sum = tile([P, 1], F32, "r_sum")
@@ -201,8 +203,8 @@ def tile_attend_knnlm_kernel(tc, query, keys_words, keys_scales, kn, hid, voc, l
         nc.scalar.activation(r_sb[:], neg_b[:], ACT.Exp, bias=b_bias[:], scale=-1.0, accum_out=r_sum[:])
         r_coef = coefficient(r_sum, 1, "r_coef")
 
-        for h in range(2):
-            cols = slice(h * BANK, (h + 1) * BANK)
-            res = tile([P, BANK], F32, "res%d" % h)
+        for c in range(V // CHUNK):
+            cols = slice(c * CHUNK, (c + 1) * CHUNK)
+            res = tile([P, CHUNK], F32, "res%d" % c)
             nc.vector.scalar_tensor_tensor(res[:], r_sb[:, cols], r_coef[:], mixed[:, cols], ALU.mult, ALU.add)
             nc.sync.dma_start(out[:, cols], res[:])

@@ -19,10 +19,11 @@ ACT = mybir.ActivationFunctionType
 
 P = 128
 PACK = 4
-CHUNK = 512
+CHUNK = 256
+CHUNKS = V // CHUNK
 OUT_SCALE = 512.0
-SCALAR_COLS = (320, 160)
-KN_SPLIT = 896
+KN_SPLIT = 1152
+GROUPS = ((0, 512), (512, 768), (768, 1024))
 KIB = 1024
 
 
@@ -39,30 +40,26 @@ def tile_attend_knnlm_kernel(tc, query, keys_words, keys_scales, kn, hid, voc, l
         def tile_at(offset, shape, dtype, name):
             return reuse.tile(shape, dtype, name=name, align_bytes=64, offset=offset)
 
-        at_kn, at_scales, at_kn_g, at_s, at_codes1 = 0, 8 * KIB, 10 * KIB, 14 * KIB, 18 * KIB
-
         slots = tile([P, I // 16], U16, "slots")
         places = tile([P, I // 16], U16, "places")
-        kn_win = tile_at(at_kn, [P, T], F32, "kn_win")
-        word_win = tile([P, T], U16, "word_win")
-        scale_win = tile_at(at_scales, [P, T], U8, "scale_win")
+        kn_win = tile_at(36 * KIB, [P, T], F32, "kn_win")
+        word_win = tile_at(0, [P, T], U16, "word_win")
+        scale_win = tile([P, T], U8, "scale_win")
         mixed = tile([P, V], F32, "mixed")
         ident = tile([P, P], F32, "ident")
         zero = tile([P, 1], F32, "zero")
         one = tile([P, 1], F32, "one")
-        lam_sb = tile([P, 1], F32, "lam_sb")
-        q_raw = tile([P, PACK, Q], F32, "q_raw")
-        h_raw = tile([P, PACK, Q], F32, "h_raw")
-        v_raw = [tile([P, PACK, CHUNK], F32, "v_raw%d" % c) for c in range(V // CHUNK)]
-
-        def zero_on_vector(ap, columns, value):
-            nc.vector.memset(ap[:, 0 : columns - 1], value)
-            nc.vector.memset(ap[:, columns - 1 : columns], value)
+        lam_sb = tile_at(24 * KIB, [P, 1], F32, "lam_sb")
+        q_raw = tile_at(4 * KIB, [P, PACK, Q], F32, "q_raw")
+        h_raw = tile_at(6 * KIB, [P, PACK, Q], F32, "h_raw")
+        v_raw = [tile_at((8 + 4 * c) * KIB, [P, PACK, CHUNK], F32, "v_raw%d" % c) for c in range(CHUNKS)]
 
         nc.vector.memset(zero[:], 0.0)
-        zero_on_vector(scale_win[:].bitcast(I32), T // 4, 0)
-        make_identity(nc, ident[:])
-        zero_on_vector(kn_win[0 : P - 1, :], KN_SPLIT, 0.0)
+        nc.gpsimd.memset(ident[:], 0.0)
+        nc.gpsimd.memset(scale_win[:].bitcast(I32), 0)
+        make_identity(nc, ident[:], nomemset=True)
+        nc.vector.memset(kn_win[0 : P - 1, 0 : KN_SPLIT - 1], 0.0)
+        nc.vector.memset(kn_win[0 : P - 1, KN_SPLIT - 1 : KN_SPLIT], 0.0)
         nc.gpsimd.memset(kn_win[0 : P - 1, KN_SPLIT:T], 0.0)
         nc.gpsimd.memset(mixed[:], 0.0)
         nc.scalar.activation(one[:], zero[:], ACT.Exp)
@@ -70,20 +67,24 @@ def tile_attend_knnlm_kernel(tc, query, keys_words, keys_scales, kn, hid, voc, l
         def by_rows(x):
             return x.rearrange("(p j) w -> p j w", j=PACK)
 
+        def load_vocab(c):
+            nc.sync.dma_start(v_raw[c][:], by_rows(voc)[:, :, c * CHUNK : (c + 1) * CHUNK])
+
         nc.sync.dma_start(slots[:], offs)
         nc.sync.dma_start(kn_win[P - 1 : P, :], kn[0:1, :])
-        nc.sync.dma_start(q_raw[:], by_rows(query))
         nc.sync.dma_start(word_win[:].bitcast(I32), keys_words[0].bitcast(I32))
+        nc.sync.dma_start(q_raw[:], by_rows(query))
         for quad in range(4):
             nc.sync.dma_start(
                 scale_win[32 * quad : 32 * quad + 4, :].bitcast(I32),
                 keys_scales[0, 4 * quad : 4 * quad + 4, :].bitcast(I32),
             )
+        load_vocab(0)
         nc.sync.dma_start(h_raw[:], by_rows(hid))
-        for c in range(V // CHUNK):
-            nc.sync.dma_start(v_raw[c][:], by_rows(voc)[:, :, c * CHUNK : (c + 1) * CHUNK])
         nc.sync.dma_start(lam_sb[:], lam)
         nc.sync.dma_start(places[:], offs2)
+        for c in range(1, CHUNKS):
+            load_vocab(c)
 
         def cast(copy, grouped, raw, cols=slice(0, Q)):
             copy(
@@ -92,119 +93,159 @@ def tile_attend_knnlm_kernel(tc, query, keys_words, keys_scales, kn, hid, voc, l
             )
 
         def quantize(codes, scales, grouped):
-            nc.vector.quantize_mx(out=codes.bitcast(FP8X4), scales=scales, in_=grouped[:].rearrange("p w j -> p (w j)"))
-
-        kn_g = tile_at(at_kn_g, [P, I], F32, "kn_g")
-        nc.vector.tensor_copy(kn_g[:], kn_win[:].indirect(slots[:]))
-        q_bf = tile([P, Q, PACK], BF16, "q_bf")
-        cast(nc.scalar.copy, q_bf, q_raw)
-        q_codes = tile_at(at_kn + 2 * KIB, [P, Q], U32, "q_codes")
-        q_scales = tile([P, Q], U8, "q_scales")
-        quantize(q_codes[:], q_scales[:], q_bf)
-        word_g = tile_at(at_kn, [P, I], U16, "word_g")
-        nc.vector.tensor_copy(word_g[:], word_win[:].indirect(slots[:]))
-        scale_g = tile_at(at_kn + KIB, [P, I], U8, "scale_g")
-        nc.vector.tensor_copy(scale_g[:], scale_win[:].indirect(slots[:]))
-
-        blocks = I // P
-        turn_ps = ps.tile([P, blocks, P], F32, name="turn_ps", tag="slot_bank")
-        for j in range(blocks):
-            nc.tensor.transpose(turn_ps[:, j, :], kn_g[:, j * P : (j + 1) * P], ident[:])
-        kn_col = tile([P, blocks], F32, "kn_col")
-        nc.scalar.copy(kn_col[:], turn_ps[:, :, P - 1])
-        h_bf = tile_at(at_kn_g, [P, Q, PACK], BF16, "h_bf")
-        cast(nc.scalar.copy, h_bf, h_raw)
-        spread_ps = ps.tile([P, I], F32, name="spread_ps")
-        for j in range(blocks):
-            nc.tensor.transpose(spread_ps[:, j * P : (j + 1) * P], kn_col[:, j : j + 1].to_broadcast([P, P]), ident[:])
-        kn_rows = tile([P, I], F32, "kn_rows")
-        nc.scalar.copy(kn_rows[:], spread_ps[:])
-
-        a_ps = ps.tile([P, I], F32, name="a_ps", tag="slot_bank")
-        nc.tensor.matmul_mx(
-            out=a_ps[:],
-            lhsT=q_codes[:].bitcast(FP8X4),
-            lhsT_scale=q_scales[:],
-            rhs=word_g[:].bitcast(U8).bitcast(FP4X4),
-            rhs_scale=scale_g[:],
-            start=True,
-            stop=True,
-        )
-        h_codes = tile_at(at_scales, [P, Q], U32, "h_codes")
-        h_scales = tile([P, Q], U8, "h_scales")
-        quantize(h_codes[:], h_scales[:], h_bf)
-        s_sb = tile_at(at_s, [P, I], F32, "s_sb")
-        nc.vector.scalar_tensor_tensor(s_sb[:], a_ps[:], 2.0, kn_rows[:], ALU.mult, ALU.subtract)
-
-        b_ps = [ps.tile([P, CHUNK], F32, name="b_ps%d" % c) for c in range(V // CHUNK)]
+            nc.vector.quantize_mx(out=codes.bitcast(FP8X4), scales=scales, in_=grouped.rearrange("p w j -> p (w j)"))
 
         def gpsimd_copy(dst, src):
             nc.gpsimd.tensor_scalar(dst, src, 1.0, 0.0, ALU.mult, ALU.add)
 
-        def cast_vocab(c, grouped, partner_copy):
-            cast(nc.scalar.copy, grouped, v_raw[c], slice(0, SCALAR_COLS[c]))
-            cast(partner_copy, grouped, v_raw[c], slice(SCALAR_COLS[c], CHUNK))
+        half = I // 2
+        kn_g = [tile([P, half], F32, "kn_g0"), tile_at(28 * KIB, [P, half], F32, "kn_g1")]
+        nc.vector.tensor_copy(kn_g[0][:], kn_win[:].indirect(slots[:, 0 : half // 16]))
+        nc.scalar.activation(kn_g[1][:], kn_win[:].indirect(slots[:, half // 16 : I // 16]), ACT.Copy)
+        word_g = tile_at(36 * KIB, [P, I], U16, "word_g")
+        nc.vector.tensor_copy(word_g[:], word_win[:].indirect(slots[:]))
+        scale_g = [tile_at(37 * KIB, [P, half], U8, "scale_g0")]
+        nc.vector.tensor_copy(scale_g[0][:], scale_win[:].indirect(slots[:, 0 : half // 16]))
 
-        def vocab_scores(c, grouped, codes):
-            scales = tile([P, CHUNK], U8, "v_scales%d" % c)
-            quantize(codes[:], scales[:], grouped)
+        blocks = I // P
+        turn_ps = ps.tile([P, blocks, P], F32, name="turn_ps", tag="slot_bank")
+        for j in range(blocks):
+            nc.tensor.transpose(turn_ps[:, j, :], kn_g[j // 2][:, (j % 2) * P : (j % 2 + 1) * P], ident[:])
+        kn_col = tile_at(45 * KIB, [P, 2 * KIB // 4], F32, "kn_col")
+        nc.scalar.copy(kn_col[:, 0:blocks], turn_ps[:, :, P - 1])
+        spread_ps = ps.tile([P, I], F32, name="spread_ps")
+        for j in range(blocks):
+            nc.tensor.transpose(spread_ps[:, j * P : (j + 1) * P], kn_col[:, j : j + 1].to_broadcast([P, P]), ident[:])
+        q_bf = tile_at(28 * KIB, [P, Q, PACK], BF16, "q_bf")
+        cast(nc.scalar.copy, q_bf, q_raw)
+        q_codes = tile([P, Q], U32, "q_codes")
+        q_scales = tile_at(45 * KIB, [P, Q], U8, "q_scales")
+        quantize(q_codes[:], q_scales[:], q_bf[:])
+        scale_g.append(tile_at(28 * KIB, [P, half], U8, "scale_g1"))
+        nc.vector.tensor_copy(scale_g[1][:], scale_win[:].indirect(slots[:, half // 16 : I // 16]))
+        kn_rows = tile_at(50 * KIB, [P, 11 * KIB // 4], F32, "kn_rows")
+        nc.scalar.copy(kn_rows[:, 0:I], spread_ps[:])
+
+        neg_s = tile([P, I], F32, "neg_s")
+        for h, bank in enumerate(("slot_bank", "slot_bank2")):
+            cols = slice(h * half, (h + 1) * half)
+            a_ps = ps.tile([P, half], F32, name="a_ps%d" % h, tag=bank)
             nc.tensor.matmul_mx(
-                out=b_ps[c][:],
-                lhsT=h_codes[:].bitcast(FP8X4),
-                lhsT_scale=h_scales[:],
-                rhs=codes[:].bitcast(FP8X4),
-                rhs_scale=scales[:],
+                out=a_ps[:],
+                lhsT=q_codes[:].bitcast(FP8X4),
+                lhsT_scale=q_scales[:],
+                rhs=word_g[:, cols].bitcast(U8).bitcast(FP4X4),
+                rhs_scale=scale_g[h][:],
                 start=True,
                 stop=True,
             )
+            nc.vector.scalar_tensor_tensor(neg_s[:, cols], a_ps[:], -2.0, kn_rows[:, cols], ALU.mult, ALU.add)
 
         def negate_with_minimum(negated, scores, start, minimum):
             nc.vector.tensor_scalar(negated, scores, -1.0, start, ALU.mult, ALU.min, accum_out=minimum)
 
-        v_bf0 = tile_at(at_kn_g, [P, CHUNK, PACK], BF16, "v_bf0")
-        cast_vocab(0, v_bf0, gpsimd_copy)
-        neg_s = tile([P, I], F32, "neg_s")
         s_bias = tile([P, 1], F32, "s_bias")
-        negate_with_minimum(neg_s[:], s_sb[:], None, s_bias[:])
-        p_sum = tile([P, 1], F32, "p_sum")
-        p_sb = tile([P, I], F32, "p_sb")
-        nc.scalar.activation(p_sb[:], neg_s[:], ACT.Exp, bias=s_bias[:], scale=-1.0, accum_out=p_sum[:])
-        vocab_scores(0, v_bf0, tile([P, CHUNK], U32, "v_codes0"))
-        v_bf1 = tile_at(at_s, [P, CHUNK, PACK], BF16, "v_bf1")
-        cast_vocab(1, v_bf1, nc.vector.tensor_copy)
-        vocab_scores(1, v_bf1, tile_at(at_codes1, [P, CHUNK], U32, "v_codes1"))
-        b_bias0 = tile([P, 1], F32, "b_bias0")
-        neg_b = tile_at(at_s, [P, V], F32, "neg_b")
-        negate_with_minimum(neg_b[:, 0:CHUNK], b_ps[0][:], None, b_bias0[:])
+        nc.vector.tensor_reduce(s_bias[:], neg_s[:], mybir.AxisListType.X, ALU.min)
 
-        share = tile([P, 2], F32, "share")
+        h_bf = tile_at(45 * KIB + 256, [P, Q, PACK], BF16, "h_bf")
+        h_codes = tile_at(60 * KIB, [P, Q], U32, "h_codes")
+        h_scales = tile([P, Q], U8, "h_scales")
+        v_bf0 = tile_at(46 * KIB + 512, [P, CHUNK, PACK], BF16, "v_bf0")
+        v_rest = tile_at(50 * KIB, [P, V - CHUNK, PACK], BF16, "v_rest")
+        v_bf = [v_bf0[:]] + [v_rest[:, c * CHUNK : (c + 1) * CHUNK, :] for c in range(CHUNKS - 1)]
+        v_codes = tile_at(56 * KIB, [P, V], U32, "v_codes")
+        v_scales = tile([P, V], U8, "v_scales")
+        b_bias = tile([P, len(GROUPS)], F32, "b_bias")
+        neg_b = tile_at(30 * KIB, [P, V], F32, "neg_b")
+        b_ps = [ps.tile([P, hi - lo], F32, name="b_ps%d" % lo) for lo, hi in GROUPS]
+
+        def cast_vocab(c, copy, lo, hi):
+            cast(copy, v_bf[c], v_raw[c], slice(lo, hi))
+
+        def quantize_vocab(c):
+            cols = slice(c * CHUNK, (c + 1) * CHUNK)
+            quantize(v_codes[:, cols], v_scales[:, cols], v_bf[c])
+
+        def vocab_scores(g):
+            lo, hi = GROUPS[g]
+            nc.tensor.matmul_mx(
+                out=b_ps[g][:],
+                lhsT=h_codes[:].bitcast(FP8X4),
+                lhsT_scale=h_scales[:],
+                rhs=v_codes[:, lo:hi].bitcast(FP8X4),
+                rhs_scale=v_scales[:, lo:hi],
+                start=True,
+                stop=True,
+            )
+
+        def vocab_minimum(g):
+            lo, hi = GROUPS[g]
+            start = b_bias[:, g - 1 : g] if g else None
+            negate_with_minimum(neg_b[:, lo:hi], b_ps[g][:], start, b_bias[:, g : g + 1])
+
+        cast_vocab(0, nc.scalar.copy, 0, 128)
+        cast_vocab(0, gpsimd_copy, 128, CHUNK)
+        cast(nc.scalar.copy, h_bf, h_raw)
+        cast_vocab(1, gpsimd_copy, 0, 96)
+        p_sum = tile([P, 1], F32, "p_sum")
+        p_all = tile_at(6 * KIB, [P, I], F32, "p_all")
+        nc.scalar.activation(p_all[:], neg_s[:], ACT.Exp, bias=s_bias[:], scale=-1.0, accum_out=p_sum[:])
+        for h in range(2):
+            nc.scalar.activation(
+                mixed[:].indirect(places[:, h * half // 16 : (h + 1) * half // 16]),
+                p_all[:, h * half : (h + 1) * half],
+                ACT.Copy,
+            )
+        quantize(h_codes[:], h_scales[:], h_bf[:])
+        cast_vocab(1, nc.vector.tensor_copy, 96, CHUNK)
+        quantize_vocab(0)
+        quantize_vocab(1)
+        vocab_scores(0)
+        cast_vocab(2, nc.vector.tensor_copy, 0, CHUNK)
+        vocab_minimum(0)
+        quantize_vocab(2)
+        vocab_scores(1)
+        cast_vocab(3, nc.vector.tensor_copy, 0, CHUNK)
+        quantize_vocab(3)
+        vocab_scores(2)
+        vocab_minimum(1)
+        vocab_minimum(2)
+        share = tile_at(12 * KIB, [P, 3], F32, "share")
         minus_one = tile([P, 1], F32, "minus_one")
         nc.gpsimd.tensor_scalar(minus_one[:], one[:], -1.0, 0.0, ALU.mult, ALU.add)
         nc.gpsimd.tensor_scalar(share[:, 0:1], lam_sb[:], OUT_SCALE, 0.0, ALU.mult, ALU.add)
-        nc.gpsimd.tensor_scalar(share[:, 1:2], lam_sb[:], -OUT_SCALE, OUT_SCALE, ALU.mult, ALU.add)
+        nc.gpsimd.tensor_scalar(share[:, 2:3], lam_sb[:], -OUT_SCALE, OUT_SCALE, ALU.mult, ALU.add)
+        p_inverse = tile([P, 1], F32, "p_inverse")
+        nc.gpsimd.tensor_tensor(p_inverse[:], p_sum[:], minus_one[:], ALU.pow)
+        p_coef = tile([P, 1], F32, "p_coef")
+        nc.gpsimd.tensor_tensor(p_coef[:], p_inverse[:], share[:, 0:1], ALU.mult)
 
-        def coefficient(total, col, name):
-            inverse = tile([P, 1], F32, name + "_inverse")
-            nc.gpsimd.tensor_tensor(inverse[:], total[:], minus_one[:], ALU.pow)
-            coef = tile([P, 1], F32, name)
-            nc.gpsimd.tensor_tensor(coef[:], inverse[:], share[:, col : col + 1], ALU.mult)
-            return coef
-
-        p_coef = coefficient(p_sum, 0, "p_coef")
-        w_sb = tile_at(at_codes1, [P, I], F32, "w_sb")
-        nc.scalar.activation(w_sb[:], p_sb[:], ACT.Copy, scale=p_coef[:])
-
-        b_bias = tile([P, 1], F32, "b_bias")
-        negate_with_minimum(neg_b[:, CHUNK:V], b_ps[1][:], b_bias0[:], b_bias[:])
-        nc.vector.tensor_copy(mixed[:].indirect(places[:]), w_sb[:])
-
-        r_sum = tile([P, 1], F32, "r_sum")
+        mid = V // 2
+        r_sum = tile([P, 2], F32, "r_sum")
         r_sb = tile([P, V], F32, "r_sb")
-        nc.scalar.activation(r_sb[:], neg_b[:], ACT.Exp, bias=b_bias[:], scale=-1.0, accum_out=r_sum[:])
-        r_coef = coefficient(r_sum, 1, "r_coef")
+        nc.scalar.activation(
+            r_sb[:, 0:mid], neg_b[:, 0:mid], ACT.Exp, bias=b_bias[:, 0:1], scale=-1.0, accum_out=r_sum[:, 0:1]
+        )
+        fall = tile([P, 1], F32, "fall")
+        nc.scalar.activation(fall[:], b_bias[:, 0:1], ACT.Exp, bias=b_bias[:, 2:3], scale=-1.0)
+        nc.scalar.activation(
+            r_sb[:, mid:V], neg_b[:, mid:V], ACT.Exp, bias=b_bias[:, 2:3], scale=-1.0, accum_out=r_sum[:, 1:2]
+        )
+        head_sum = tile([P, 1], F32, "head_sum")
+        nc.vector.tensor_scalar(head_sum[:], fall[:], r_sum[:, 0:1], None, ALU.mult)
+        nc.vector.tensor_scalar(share[:, 1:2], fall[:], share[:, 2:3], None, ALU.mult)
+        r_total = tile([P, 1], F32, "r_total")
+        nc.vector.tensor_scalar(r_total[:], r_sum[:, 1:2], head_sum[:], None, ALU.add)
+        r_inverse = tile([P, 1], F32, "r_inverse")
+        nc.vector.reciprocal(r_inverse[:], r_total[:])
+        r_coef = tile([P, 2], F32, "r_coef")
+        nc.vector.tensor_scalar(r_coef[:], share[:, 1:3], r_inverse[:], None, ALU.mult)
 
-        for c in range(V // CHUNK):
+        for c in range(CHUNKS):
             cols = slice(c * CHUNK, (c + 1) * CHUNK)
+            g = c * CHUNK // mid
+            weights = tile_at((30 + c) * KIB, [P, CHUNK], F32, "weights%d" % c)
+            nc.scalar.activation(weights[:], mixed[:, cols], ACT.Copy, scale=p_coef[:])
             res = tile([P, CHUNK], F32, "res%d" % c)
-            nc.vector.scalar_tensor_tensor(res[:], r_sb[:, cols], r_coef[:], mixed[:, cols], ALU.mult, ALU.add)
+            nc.vector.scalar_tensor_tensor(res[:], r_sb[:, cols], r_coef[:, g : g + 1], weights[:], ALU.mult, ALU.add)
             nc.sync.dma_start(out[:, cols], res[:])

@@ -23,6 +23,7 @@ CHUNK = 256
 CHUNKS = V // CHUNK
 OUT_SCALE = 512.0
 KN_SPLIT = 1152
+KN_SLOTS = 320
 GROUPS = ((0, 512), (512, 768), (768, 1024))
 KIB = 1024
 
@@ -81,10 +82,11 @@ def tile_attend_knnlm_kernel(tc, query, keys_words, keys_scales, kn, hid, voc, l
             )
         load_vocab(0)
         nc.sync.dma_start(h_raw[:], by_rows(hid))
-        nc.sync.dma_start(lam_sb[:], lam)
+        load_vocab(1)
+        load_vocab(2)
         nc.sync.dma_start(places[:], offs2)
-        for c in range(1, CHUNKS):
-            load_vocab(c)
+        load_vocab(3)
+        nc.sync.dma_start(lam_sb[:], lam)
 
         def cast(copy, grouped, raw, cols=slice(0, Q)):
             copy(
@@ -95,13 +97,10 @@ def tile_attend_knnlm_kernel(tc, query, keys_words, keys_scales, kn, hid, voc, l
         def quantize(codes, scales, grouped):
             nc.vector.quantize_mx(out=codes.bitcast(FP8X4), scales=scales, in_=grouped.rearrange("p w j -> p (w j)"))
 
-        def gpsimd_copy(dst, src):
-            nc.gpsimd.tensor_scalar(dst, src, 1.0, 0.0, ALU.mult, ALU.add)
-
         half = I // 2
-        kn_g = [tile([P, half], F32, "kn_g0"), tile_at(28 * KIB, [P, half], F32, "kn_g1")]
-        nc.vector.tensor_copy(kn_g[0][:], kn_win[:].indirect(slots[:, 0 : half // 16]))
-        nc.scalar.activation(kn_g[1][:], kn_win[:].indirect(slots[:, half // 16 : I // 16]), ACT.Copy)
+        kn_g = tile_at(28 * KIB, [P, I], F32, "kn_g")
+        nc.vector.tensor_copy(kn_g[:, 0:KN_SLOTS], kn_win[:].indirect(slots[:, 0 : KN_SLOTS // 16]))
+        nc.scalar.activation(kn_g[:, KN_SLOTS:I], kn_win[:].indirect(slots[:, KN_SLOTS // 16 : I // 16]), ACT.Copy)
         word_g = tile_at(36 * KIB, [P, I], U16, "word_g")
         nc.vector.tensor_copy(word_g[:], word_win[:].indirect(slots[:]))
         scale_g = [tile_at(37 * KIB, [P, half], U8, "scale_g0")]
@@ -110,7 +109,7 @@ def tile_attend_knnlm_kernel(tc, query, keys_words, keys_scales, kn, hid, voc, l
         blocks = I // P
         turn_ps = ps.tile([P, blocks, P], F32, name="turn_ps", tag="slot_bank")
         for j in range(blocks):
-            nc.tensor.transpose(turn_ps[:, j, :], kn_g[j // 2][:, (j % 2) * P : (j % 2 + 1) * P], ident[:])
+            nc.tensor.transpose(turn_ps[:, j, :], kn_g[:, j * P : (j + 1) * P], ident[:])
         kn_col = tile_at(45 * KIB, [P, 2 * KIB // 4], F32, "kn_col")
         nc.scalar.copy(kn_col[:, 0:blocks], turn_ps[:, :, P - 1])
         spread_ps = ps.tile([P, I], F32, name="spread_ps")
@@ -119,14 +118,19 @@ def tile_attend_knnlm_kernel(tc, query, keys_words, keys_scales, kn, hid, voc, l
         q_bf = tile_at(28 * KIB, [P, Q, PACK], BF16, "q_bf")
         cast(nc.scalar.copy, q_bf, q_raw)
         q_codes = tile([P, Q], U32, "q_codes")
-        q_scales = tile_at(45 * KIB, [P, Q], U8, "q_scales")
+        q_scales = tile([P, Q], U8, "q_scales")
         quantize(q_codes[:], q_scales[:], q_bf[:])
         scale_g.append(tile_at(28 * KIB, [P, half], U8, "scale_g1"))
         nc.vector.tensor_copy(scale_g[1][:], scale_win[:].indirect(slots[:, half // 16 : I // 16]))
         kn_rows = tile_at(50 * KIB, [P, 11 * KIB // 4], F32, "kn_rows")
         nc.scalar.copy(kn_rows[:, 0:I], spread_ps[:])
 
+        def negate_with_minimum(negated, scores, start, minimum):
+            nc.vector.tensor_scalar(negated, scores, -1.0, start, ALU.mult, ALU.min, accum_out=minimum)
+
+        s_sb = tile([P, I], F32, "s_sb")
         neg_s = tile([P, I], F32, "neg_s")
+        s_bias = tile([P, 2], F32, "s_bias")
         for h, bank in enumerate(("slot_bank", "slot_bank2")):
             cols = slice(h * half, (h + 1) * half)
             a_ps = ps.tile([P, half], F32, name="a_ps%d" % h, tag=bank)
@@ -139,13 +143,8 @@ def tile_attend_knnlm_kernel(tc, query, keys_words, keys_scales, kn, hid, voc, l
                 start=True,
                 stop=True,
             )
-            nc.vector.scalar_tensor_tensor(neg_s[:, cols], a_ps[:], -2.0, kn_rows[:, cols], ALU.mult, ALU.add)
-
-        def negate_with_minimum(negated, scores, start, minimum):
-            nc.vector.tensor_scalar(negated, scores, -1.0, start, ALU.mult, ALU.min, accum_out=minimum)
-
-        s_bias = tile([P, 1], F32, "s_bias")
-        nc.vector.tensor_reduce(s_bias[:], neg_s[:], mybir.AxisListType.X, ALU.min)
+            nc.vector.scalar_tensor_tensor(s_sb[:, cols], a_ps[:], 2.0, kn_rows[:, cols], ALU.mult, ALU.subtract)
+            negate_with_minimum(neg_s[:, cols], s_sb[:, cols], s_bias[:, 0:1] if h else None, s_bias[:, h : h + 1])
 
         h_bf = tile_at(45 * KIB + 256, [P, Q, PACK], BF16, "h_bf")
         h_codes = tile_at(60 * KIB, [P, Q], U32, "h_codes")
@@ -183,13 +182,11 @@ def tile_attend_knnlm_kernel(tc, query, keys_words, keys_scales, kn, hid, voc, l
             start = b_bias[:, g - 1 : g] if g else None
             negate_with_minimum(neg_b[:, lo:hi], b_ps[g][:], start, b_bias[:, g : g + 1])
 
-        cast_vocab(0, nc.scalar.copy, 0, 128)
-        cast_vocab(0, gpsimd_copy, 128, CHUNK)
+        cast_vocab(0, nc.scalar.copy, 0, CHUNK)
         cast(nc.scalar.copy, h_bf, h_raw)
-        cast_vocab(1, gpsimd_copy, 0, 96)
         p_sum = tile([P, 1], F32, "p_sum")
         p_all = tile_at(6 * KIB, [P, I], F32, "p_all")
-        nc.scalar.activation(p_all[:], neg_s[:], ACT.Exp, bias=s_bias[:], scale=-1.0, accum_out=p_sum[:])
+        nc.scalar.activation(p_all[:], neg_s[:], ACT.Exp, bias=s_bias[:, 1:2], scale=-1.0, accum_out=p_sum[:])
         for h in range(2):
             nc.scalar.activation(
                 mixed[:].indirect(places[:, h * half // 16 : (h + 1) * half // 16]),
@@ -197,7 +194,7 @@ def tile_attend_knnlm_kernel(tc, query, keys_words, keys_scales, kn, hid, voc, l
                 ACT.Copy,
             )
         quantize(h_codes[:], h_scales[:], h_bf[:])
-        cast_vocab(1, nc.vector.tensor_copy, 96, CHUNK)
+        cast_vocab(1, nc.vector.tensor_copy, 0, CHUNK)
         quantize_vocab(0)
         quantize_vocab(1)
         vocab_scores(0)

@@ -19,12 +19,13 @@ ACT = mybir.ActivationFunctionType
 
 P = 128
 PACK = 4
-CHUNK = 256
-CHUNKS = V // CHUNK
+LOADS = ((0, 256), (256, 512), (512, 1024))
+PIECE = 256
 OUT_SCALE = 512.0
 KN_SPLIT = 1152
 KN_SLOTS = 320
-GROUPS = ((0, 512), (512, 768), (768, 1024))
+GROUPS = ((0, 512), (512, 1024))
+SCATTERS = ((0, 128), (128, 256), (256, 512))
 KIB = 1024
 
 
@@ -53,7 +54,7 @@ def tile_attend_knnlm_kernel(tc, query, keys_words, keys_scales, kn, hid, voc, l
         lam_sb = tile_at(24 * KIB, [P, 1], F32, "lam_sb")
         q_raw = tile_at(4 * KIB, [P, PACK, Q], F32, "q_raw")
         h_raw = tile_at(6 * KIB, [P, PACK, Q], F32, "h_raw")
-        v_raw = [tile_at((8 + 4 * c) * KIB, [P, PACK, CHUNK], F32, "v_raw%d" % c) for c in range(CHUNKS)]
+        v_raw = [tile_at(8 * KIB + 16 * lo, [P, PACK, hi - lo], F32, "v_raw%d" % lo) for lo, hi in LOADS]
 
         nc.vector.memset(zero[:], 0.0)
         nc.gpsimd.memset(ident[:], 0.0)
@@ -69,7 +70,7 @@ def tile_attend_knnlm_kernel(tc, query, keys_words, keys_scales, kn, hid, voc, l
             return x.rearrange("(p j) w -> p j w", j=PACK)
 
         def load_vocab(c):
-            nc.sync.dma_start(v_raw[c][:], by_rows(voc)[:, :, c * CHUNK : (c + 1) * CHUNK])
+            nc.sync.dma_start(v_raw[c][:], by_rows(voc)[:, :, LOADS[c][0] : LOADS[c][1]])
 
         nc.sync.dma_start(slots[:], offs)
         nc.sync.dma_start(kn_win[P - 1 : P, :], kn[0:1, :])
@@ -83,9 +84,8 @@ def tile_attend_knnlm_kernel(tc, query, keys_words, keys_scales, kn, hid, voc, l
         load_vocab(0)
         nc.sync.dma_start(h_raw[:], by_rows(hid))
         load_vocab(1)
-        load_vocab(2)
         nc.sync.dma_start(places[:], offs2)
-        load_vocab(3)
+        load_vocab(2)
         nc.sync.dma_start(lam_sb[:], lam)
 
         def cast(copy, grouped, raw, cols=slice(0, Q)):
@@ -96,6 +96,9 @@ def tile_attend_knnlm_kernel(tc, query, keys_words, keys_scales, kn, hid, voc, l
 
         def quantize(codes, scales, grouped):
             nc.vector.quantize_mx(out=codes.bitcast(FP8X4), scales=scales, in_=grouped.rearrange("p w j -> p (w j)"))
+
+        def gpsimd_copy(dst, src):
+            nc.gpsimd.tensor_scalar(dst, src, 1.0, 0.0, ALU.mult, ALU.add)
 
         half = I // 2
         kn_g = tile_at(28 * KIB, [P, I], F32, "kn_g")
@@ -149,21 +152,26 @@ def tile_attend_knnlm_kernel(tc, query, keys_words, keys_scales, kn, hid, voc, l
         h_bf = tile_at(45 * KIB + 256, [P, Q, PACK], BF16, "h_bf")
         h_codes = tile_at(60 * KIB, [P, Q], U32, "h_codes")
         h_scales = tile([P, Q], U8, "h_scales")
-        v_bf0 = tile_at(46 * KIB + 512, [P, CHUNK, PACK], BF16, "v_bf0")
-        v_rest = tile_at(50 * KIB, [P, V - CHUNK, PACK], BF16, "v_rest")
-        v_bf = [v_bf0[:]] + [v_rest[:, c * CHUNK : (c + 1) * CHUNK, :] for c in range(CHUNKS - 1)]
-        v_codes = tile_at(56 * KIB, [P, V], U32, "v_codes")
+        v_bf = [
+            tile_at(46 * KIB + 512, [P, 256, PACK], BF16, "v_bf0"),
+            tile_at(42 * KIB + 1024 + 64, [P, 256, PACK], BF16, "v_bf1"),
+            tile_at(50 * KIB, [P, 512, PACK], BF16, "v_bf2"),
+        ]
+        v_codes = [tile_at(56 * KIB + 4 * lo, [P, hi - lo], U32, "v_codes%d" % lo) for lo, hi in GROUPS]
         v_scales = tile([P, V], U8, "v_scales")
         b_bias = tile([P, len(GROUPS)], F32, "b_bias")
         neg_b = tile_at(30 * KIB, [P, V], F32, "neg_b")
         b_ps = [ps.tile([P, hi - lo], F32, name="b_ps%d" % lo) for lo, hi in GROUPS]
 
-        def cast_vocab(c, copy, lo, hi):
-            cast(copy, v_bf[c], v_raw[c], slice(lo, hi))
+        def cast_vocab(c, split):
+            lo, hi = LOADS[c]
+            cast(nc.scalar.copy, v_bf[c], v_raw[c], slice(0, split))
+            cast(gpsimd_copy, v_bf[c], v_raw[c], slice(split, hi - lo))
 
         def quantize_vocab(c):
-            cols = slice(c * CHUNK, (c + 1) * CHUNK)
-            quantize(v_codes[:, cols], v_scales[:, cols], v_bf[c])
+            lo, hi = LOADS[c]
+            g = lo // 512
+            quantize(v_codes[g][:, lo - 512 * g : hi - 512 * g], v_scales[:, lo:hi], v_bf[c][:])
 
         def vocab_scores(g):
             lo, hi = GROUPS[g]
@@ -171,7 +179,7 @@ def tile_attend_knnlm_kernel(tc, query, keys_words, keys_scales, kn, hid, voc, l
                 out=b_ps[g][:],
                 lhsT=h_codes[:].bitcast(FP8X4),
                 lhsT_scale=h_scales[:],
-                rhs=v_codes[:, lo:hi].bitcast(FP8X4),
+                rhs=v_codes[g][:].bitcast(FP8X4),
                 rhs_scale=v_scales[:, lo:hi],
                 start=True,
                 stop=True,
@@ -182,67 +190,60 @@ def tile_attend_knnlm_kernel(tc, query, keys_words, keys_scales, kn, hid, voc, l
             start = b_bias[:, g - 1 : g] if g else None
             negate_with_minimum(neg_b[:, lo:hi], b_ps[g][:], start, b_bias[:, g : g + 1])
 
-        cast_vocab(0, nc.scalar.copy, 0, CHUNK)
-        cast(nc.scalar.copy, h_bf, h_raw)
-        p_sum = tile([P, 1], F32, "p_sum")
-        p_all = tile_at(6 * KIB, [P, I], F32, "p_all")
-        nc.scalar.activation(p_all[:], neg_s[:], ACT.Exp, bias=s_bias[:, 1:2], scale=-1.0, accum_out=p_sum[:])
-        for h in range(2):
+        p_sum = tile([P, len(SCATTERS)], F32, "p_sum")
+
+        def scatter(n, offset):
+            lo, hi = SCATTERS[n]
+            p_sb = tile_at(offset, [P, hi - lo], F32, "p_sb%d" % n)
             nc.scalar.activation(
-                mixed[:].indirect(places[:, h * half // 16 : (h + 1) * half // 16]),
-                p_all[:, h * half : (h + 1) * half],
-                ACT.Copy,
+                p_sb[:], neg_s[:, lo:hi], ACT.Exp, bias=s_bias[:, 1:2], scale=-1.0, accum_out=p_sum[:, n : n + 1]
             )
+            nc.vector.tensor_copy(mixed[:].indirect(places[:, lo // 16 : hi // 16]), p_sb[:])
+
+        cast_vocab(0, 128)
+        cast(nc.scalar.copy, h_bf, h_raw)
+        cast_vocab(1, 128)
         quantize(h_codes[:], h_scales[:], h_bf[:])
-        cast_vocab(1, nc.vector.tensor_copy, 0, CHUNK)
         quantize_vocab(0)
         quantize_vocab(1)
         vocab_scores(0)
-        cast_vocab(2, nc.vector.tensor_copy, 0, CHUNK)
+        scatter(0, 12 * KIB)
         vocab_minimum(0)
+        cast_vocab(2, 256)
         quantize_vocab(2)
         vocab_scores(1)
-        cast_vocab(3, nc.vector.tensor_copy, 0, CHUNK)
-        quantize_vocab(3)
-        vocab_scores(2)
+        scatter(1, 16 * KIB)
         vocab_minimum(1)
-        vocab_minimum(2)
-        share = tile_at(12 * KIB, [P, 3], F32, "share")
+        scatter(2, 58 * KIB)
+
+        share = tile_at(13 * KIB, [P, 2], F32, "share")
         minus_one = tile([P, 1], F32, "minus_one")
         nc.gpsimd.tensor_scalar(minus_one[:], one[:], -1.0, 0.0, ALU.mult, ALU.add)
         nc.gpsimd.tensor_scalar(share[:, 0:1], lam_sb[:], OUT_SCALE, 0.0, ALU.mult, ALU.add)
-        nc.gpsimd.tensor_scalar(share[:, 2:3], lam_sb[:], -OUT_SCALE, OUT_SCALE, ALU.mult, ALU.add)
-        p_inverse = tile([P, 1], F32, "p_inverse")
-        nc.gpsimd.tensor_tensor(p_inverse[:], p_sum[:], minus_one[:], ALU.pow)
-        p_coef = tile([P, 1], F32, "p_coef")
-        nc.gpsimd.tensor_tensor(p_coef[:], p_inverse[:], share[:, 0:1], ALU.mult)
+        nc.gpsimd.tensor_scalar(share[:, 1:2], lam_sb[:], -OUT_SCALE, OUT_SCALE, ALU.mult, ALU.add)
 
-        mid = V // 2
-        r_sum = tile([P, 2], F32, "r_sum")
+        def coefficient(total, col, name):
+            inverse = tile([P, 1], F32, name + "_inverse")
+            nc.gpsimd.tensor_tensor(inverse[:], total[:], minus_one[:], ALU.pow)
+            coef = tile([P, 1], F32, name)
+            nc.gpsimd.tensor_tensor(coef[:], inverse[:], share[:, col : col + 1], ALU.mult)
+            return coef
+
+        p_head = tile([P, 1], F32, "p_head")
+        nc.gpsimd.tensor_tensor(p_head[:], p_sum[:, 0:1], p_sum[:, 1:2], ALU.add)
+        p_total = tile([P, 1], F32, "p_total")
+        nc.gpsimd.tensor_tensor(p_total[:], p_head[:], p_sum[:, 2:3], ALU.add)
+        p_coef = coefficient(p_total, 0, "p_coef")
+
+        r_sum = tile([P, 1], F32, "r_sum")
         r_sb = tile([P, V], F32, "r_sb")
-        nc.scalar.activation(
-            r_sb[:, 0:mid], neg_b[:, 0:mid], ACT.Exp, bias=b_bias[:, 0:1], scale=-1.0, accum_out=r_sum[:, 0:1]
-        )
-        fall = tile([P, 1], F32, "fall")
-        nc.scalar.activation(fall[:], b_bias[:, 0:1], ACT.Exp, bias=b_bias[:, 2:3], scale=-1.0)
-        nc.scalar.activation(
-            r_sb[:, mid:V], neg_b[:, mid:V], ACT.Exp, bias=b_bias[:, 2:3], scale=-1.0, accum_out=r_sum[:, 1:2]
-        )
-        head_sum = tile([P, 1], F32, "head_sum")
-        nc.vector.tensor_scalar(head_sum[:], fall[:], r_sum[:, 0:1], None, ALU.mult)
-        nc.vector.tensor_scalar(share[:, 1:2], fall[:], share[:, 2:3], None, ALU.mult)
-        r_total = tile([P, 1], F32, "r_total")
-        nc.vector.tensor_scalar(r_total[:], r_sum[:, 1:2], head_sum[:], None, ALU.add)
-        r_inverse = tile([P, 1], F32, "r_inverse")
-        nc.vector.reciprocal(r_inverse[:], r_total[:])
-        r_coef = tile([P, 2], F32, "r_coef")
-        nc.vector.tensor_scalar(r_coef[:], share[:, 1:3], r_inverse[:], None, ALU.mult)
+        nc.scalar.activation(r_sb[:], neg_b[:], ACT.Exp, bias=b_bias[:, 1:2], scale=-1.0, accum_out=r_sum[:])
+        r_coef = coefficient(r_sum, 1, "r_coef")
 
-        for c in range(CHUNKS):
-            cols = slice(c * CHUNK, (c + 1) * CHUNK)
-            g = c * CHUNK // mid
-            weights = tile_at((30 + c) * KIB, [P, CHUNK], F32, "weights%d" % c)
+        for c in range(V // PIECE):
+            cols = slice(c * PIECE, (c + 1) * PIECE)
+            weights = tile_at((30 + c) * KIB, [P, PIECE], F32, "weights%d" % c)
             nc.scalar.activation(weights[:], mixed[:, cols], ACT.Copy, scale=p_coef[:])
-            res = tile([P, CHUNK], F32, "res%d" % c)
-            nc.vector.scalar_tensor_tensor(res[:], r_sb[:, cols], r_coef[:, g : g + 1], weights[:], ALU.mult, ALU.add)
+            res = tile([P, PIECE], F32, "res%d" % c)
+            nc.vector.scalar_tensor_tensor(res[:], r_sb[:, cols], r_coef[:], weights[:], ALU.mult, ALU.add)
             nc.sync.dma_start(out[:, cols], res[:])

@@ -25,7 +25,7 @@ OUT_SCALE = 512.0
 KN_SPLIT = 1152
 KN_SLOTS = 320
 GROUPS = ((0, 512), (512, 1024))
-SCATTERS = ((0, 128), (128, 256), (256, 512))
+SCATTER_CUTS = (192, 320)
 KIB = 1024
 
 
@@ -190,16 +190,17 @@ def tile_attend_knnlm_kernel(tc, query, keys_words, keys_scales, kn, hid, voc, l
             start = b_bias[:, g - 1 : g] if g else None
             negate_with_minimum(neg_b[:, lo:hi], b_ps[g][:], start, b_bias[:, g : g + 1])
 
-        p_sum = tile([P, len(SCATTERS)], F32, "p_sum")
+        p_sum = tile([P, 2], F32, "p_sum")
 
-        def scatter(n, offset):
-            lo, hi = SCATTERS[n]
-            p_sb = tile_at(offset, [P, hi - lo], F32, "p_sb%d" % n)
+        def weigh(n, p_sb, lo, hi):
             nc.scalar.activation(
                 p_sb[:], neg_s[:, lo:hi], ACT.Exp, bias=s_bias[:, 1:2], scale=-1.0, accum_out=p_sum[:, n : n + 1]
             )
-            nc.vector.tensor_copy(mixed[:].indirect(places[:, lo // 16 : hi // 16]), p_sb[:])
 
+        def scatter(lo, hi, values):
+            nc.vector.tensor_copy(mixed[:].indirect(places[:, lo // 16 : hi // 16]), values)
+
+        head, mid = SCATTER_CUTS
         cast_vocab(0, 128)
         cast(nc.scalar.copy, h_bf, h_raw)
         cast_vocab(1, 128)
@@ -207,14 +208,20 @@ def tile_attend_knnlm_kernel(tc, query, keys_words, keys_scales, kn, hid, voc, l
         quantize_vocab(0)
         quantize_vocab(1)
         vocab_scores(0)
-        scatter(0, 12 * KIB)
+        p_head = tile_at(12 * KIB, [P, head], F32, "p_head")
+        weigh(0, p_head, 0, head)
+        scatter(0, head, p_head[:])
         vocab_minimum(0)
-        cast_vocab(2, 256)
+        cast_vocab(2, 288)
         quantize_vocab(2)
         vocab_scores(1)
-        scatter(1, 16 * KIB)
+        p_rest = tile_at(16 * KIB, [P, I - head], F32, "p_rest")
+        weigh(1, p_rest, head, I)
+        scatter(head, mid, p_rest[:, 0 : mid - head])
         vocab_minimum(1)
-        scatter(2, 58 * KIB)
+        p_tail = tile_at(58 * KIB, [P, I - mid], F32, "p_tail")
+        nc.scalar.copy(p_tail[:], p_rest[:, mid - head : I - head])
+        scatter(mid, I, p_tail[:])
 
         share = tile_at(13 * KIB, [P, 2], F32, "share")
         minus_one = tile([P, 1], F32, "minus_one")
@@ -222,23 +229,20 @@ def tile_attend_knnlm_kernel(tc, query, keys_words, keys_scales, kn, hid, voc, l
         nc.gpsimd.tensor_scalar(share[:, 0:1], lam_sb[:], OUT_SCALE, 0.0, ALU.mult, ALU.add)
         nc.gpsimd.tensor_scalar(share[:, 1:2], lam_sb[:], -OUT_SCALE, OUT_SCALE, ALU.mult, ALU.add)
 
-        def coefficient(total, col, name):
-            inverse = tile([P, 1], F32, name + "_inverse")
-            nc.gpsimd.tensor_tensor(inverse[:], total[:], minus_one[:], ALU.pow)
-            coef = tile([P, 1], F32, name)
-            nc.gpsimd.tensor_tensor(coef[:], inverse[:], share[:, col : col + 1], ALU.mult)
-            return coef
-
-        p_head = tile([P, 1], F32, "p_head")
-        nc.gpsimd.tensor_tensor(p_head[:], p_sum[:, 0:1], p_sum[:, 1:2], ALU.add)
         p_total = tile([P, 1], F32, "p_total")
-        nc.gpsimd.tensor_tensor(p_total[:], p_head[:], p_sum[:, 2:3], ALU.add)
-        p_coef = coefficient(p_total, 0, "p_coef")
+        nc.gpsimd.tensor_tensor(p_total[:], p_sum[:, 0:1], p_sum[:, 1:2], ALU.add)
+        p_inverse = tile([P, 1], F32, "p_inverse")
+        nc.gpsimd.tensor_tensor(p_inverse[:], p_total[:], minus_one[:], ALU.pow)
+        p_coef = tile([P, 1], F32, "p_coef")
+        nc.gpsimd.tensor_tensor(p_coef[:], p_inverse[:], share[:, 0:1], ALU.mult)
 
         r_sum = tile([P, 1], F32, "r_sum")
         r_sb = tile([P, V], F32, "r_sb")
         nc.scalar.activation(r_sb[:], neg_b[:], ACT.Exp, bias=b_bias[:, 1:2], scale=-1.0, accum_out=r_sum[:])
-        r_coef = coefficient(r_sum, 1, "r_coef")
+        r_inverse = tile([P, 1], F32, "r_inverse")
+        nc.vector.reciprocal(r_inverse[:], r_sum[:])
+        r_coef = tile([P, 1], F32, "r_coef")
+        nc.vector.tensor_scalar(r_coef[:], r_inverse[:], share[:, 1:2], None, ALU.mult)
 
         for c in range(V // PIECE):
             cols = slice(c * PIECE, (c + 1) * PIECE)

@@ -9,8 +9,8 @@ FLOPS = 2 * D * Q * I + 2 * K * Q * V
 F32 = mybir.dt.float32
 BF16 = mybir.dt.bfloat16
 I32 = mybir.dt.int32
-U32 = mybir.dt.uint32
 U16 = mybir.dt.uint16
+U32 = mybir.dt.uint32
 U8 = mybir.dt.uint8
 FP8X4 = mybir.dt.float8_e4m3fn_x4
 FP4X4 = mybir.dt.float4_e2m1fn_x4
@@ -19,13 +19,13 @@ ACT = mybir.ActivationFunctionType
 
 P = 128
 PACK = 4
-LOADS = ((0, 256), (256, 512), (512, 1024))
-PIECE = 256
+CHUNK = 256
+GROUP = 512
 OUT_SCALE = 512.0
-KN_SPLIT = 1152
+KN_SPLIT = 1536
 KN_SLOTS = 320
-GROUPS = ((0, 512), (512, 1024))
-SCATTER_CUTS = (192, 320)
+SCALAR_COLS = (192, 128, 256, 128)
+HEAD, MID = 128, 384
 KIB = 1024
 
 
@@ -42,27 +42,28 @@ def tile_attend_knnlm_kernel(tc, query, keys_words, keys_scales, kn, hid, voc, l
         def tile_at(offset, shape, dtype, name):
             return reuse.tile(shape, dtype, name=name, align_bytes=64, offset=offset)
 
+        chunks = V // CHUNK
         slots = tile([P, I // 16], U16, "slots")
         places = tile([P, I // 16], U16, "places")
-        kn_win = tile_at(36 * KIB, [P, T], F32, "kn_win")
+        kn_win = tile_at(40 * KIB, [P, T], F32, "kn_win")
         word_win = tile_at(0, [P, T], U16, "word_win")
         scale_win = tile([P, T], U8, "scale_win")
         mixed = tile([P, V], F32, "mixed")
         ident = tile([P, P], F32, "ident")
         zero = tile([P, 1], F32, "zero")
         one = tile([P, 1], F32, "one")
-        lam_sb = tile_at(24 * KIB, [P, 1], F32, "lam_sb")
-        q_raw = tile_at(4 * KIB, [P, PACK, Q], F32, "q_raw")
-        h_raw = tile_at(6 * KIB, [P, PACK, Q], F32, "h_raw")
-        v_raw = [tile_at(8 * KIB + 16 * lo, [P, PACK, hi - lo], F32, "v_raw%d" % lo) for lo, hi in LOADS]
+        lam_sb = tile([P, 1], F32, "lam_sb")
+        q_raw = tile([P, PACK, Q], F32, "q_raw")
+        h_raw = tile([P, PACK, Q], F32, "h_raw")
+        v_raw = [tile_at(at * KIB, [P, PACK, CHUNK], F32, "v_raw%d" % at) for at in (24, 28, 32, 12)]
 
-        nc.vector.memset(zero[:], 0.0)
         nc.gpsimd.memset(ident[:], 0.0)
         nc.gpsimd.memset(scale_win[:].bitcast(I32), 0)
+        nc.vector.memset(zero[:], 0.0)
         make_identity(nc, ident[:], nomemset=True)
+        nc.gpsimd.memset(kn_win[0 : P - 1, KN_SPLIT:T], 0.0)
         nc.vector.memset(kn_win[0 : P - 1, 0 : KN_SPLIT - 1], 0.0)
         nc.vector.memset(kn_win[0 : P - 1, KN_SPLIT - 1 : KN_SPLIT], 0.0)
-        nc.gpsimd.memset(kn_win[0 : P - 1, KN_SPLIT:T], 0.0)
         nc.gpsimd.memset(mixed[:], 0.0)
         nc.scalar.activation(one[:], zero[:], ACT.Exp)
 
@@ -70,184 +71,184 @@ def tile_attend_knnlm_kernel(tc, query, keys_words, keys_scales, kn, hid, voc, l
             return x.rearrange("(p j) w -> p j w", j=PACK)
 
         def load_vocab(c):
-            nc.sync.dma_start(v_raw[c][:], by_rows(voc)[:, :, LOADS[c][0] : LOADS[c][1]])
+            nc.sync.dma_start(v_raw[c][:], by_rows(voc)[:, :, c * CHUNK : (c + 1) * CHUNK])
 
         nc.sync.dma_start(slots[:], offs)
         nc.sync.dma_start(kn_win[P - 1 : P, :], kn[0:1, :])
-        nc.sync.dma_start(word_win[:].bitcast(I32), keys_words[0].bitcast(I32))
         nc.sync.dma_start(q_raw[:], by_rows(query))
-        for quad in range(4):
-            nc.sync.dma_start(
-                scale_win[32 * quad : 32 * quad + 4, :].bitcast(I32),
-                keys_scales[0, 4 * quad : 4 * quad + 4, :].bitcast(I32),
-            )
-        load_vocab(0)
+        for r in range(4):
+            nc.sync.dma_start(scale_win[r:P:32, :].bitcast(I32), keys_scales[0, r:16:4, :].bitcast(I32))
+        nc.sync.dma_start(word_win[:].bitcast(I32), keys_words[0].bitcast(I32))
         nc.sync.dma_start(h_raw[:], by_rows(hid))
+        load_vocab(0)
         load_vocab(1)
         nc.sync.dma_start(places[:], offs2)
         load_vocab(2)
+        load_vocab(3)
         nc.sync.dma_start(lam_sb[:], lam)
 
-        def cast(copy, grouped, raw, cols=slice(0, Q)):
+        def cast(copy, grouped, raw, cols=slice(None)):
             copy(
                 grouped[:, cols, :].rearrange("p (c i) t -> p c t i", i=4),
                 raw[:, :, cols].rearrange("p t (c i) -> p c t i", i=4),
             )
 
-        def quantize(codes, scales, grouped):
-            nc.vector.quantize_mx(out=codes.bitcast(FP8X4), scales=scales, in_=grouped.rearrange("p w j -> p (w j)"))
-
         def gpsimd_copy(dst, src):
             nc.gpsimd.tensor_scalar(dst, src, 1.0, 0.0, ALU.mult, ALU.add)
 
+        def quantize(codes, scales, grouped):
+            nc.vector.quantize_mx(out=codes.bitcast(FP8X4), scales=scales, in_=grouped.rearrange("p w j -> p (w j)"))
+
         half = I // 2
-        kn_g = tile_at(28 * KIB, [P, I], F32, "kn_g")
+        kn_g = tile([P, I], F32, "kn_g")
         nc.vector.tensor_copy(kn_g[:, 0:KN_SLOTS], kn_win[:].indirect(slots[:, 0 : KN_SLOTS // 16]))
         nc.scalar.activation(kn_g[:, KN_SLOTS:I], kn_win[:].indirect(slots[:, KN_SLOTS // 16 : I // 16]), ACT.Copy)
-        word_g = tile_at(36 * KIB, [P, I], U16, "word_g")
-        nc.vector.tensor_copy(word_g[:], word_win[:].indirect(slots[:]))
-        scale_g = [tile_at(37 * KIB, [P, half], U8, "scale_g0")]
-        nc.vector.tensor_copy(scale_g[0][:], scale_win[:].indirect(slots[:, 0 : half // 16]))
-
-        blocks = I // P
-        turn_ps = ps.tile([P, blocks, P], F32, name="turn_ps", tag="slot_bank")
-        for j in range(blocks):
-            nc.tensor.transpose(turn_ps[:, j, :], kn_g[:, j * P : (j + 1) * P], ident[:])
-        kn_col = tile_at(45 * KIB, [P, 2 * KIB // 4], F32, "kn_col")
-        nc.scalar.copy(kn_col[:, 0:blocks], turn_ps[:, :, P - 1])
-        spread_ps = ps.tile([P, I], F32, name="spread_ps")
-        for j in range(blocks):
-            nc.tensor.transpose(spread_ps[:, j * P : (j + 1) * P], kn_col[:, j : j + 1].to_broadcast([P, P]), ident[:])
-        q_bf = tile_at(28 * KIB, [P, Q, PACK], BF16, "q_bf")
-        cast(nc.scalar.copy, q_bf, q_raw)
+        q_bf = tile_at(40 * KIB, [P, Q, PACK], BF16, "q_bf")
+        cast(nc.vector.tensor_copy, q_bf, q_raw)
+        scale_g = tile_at(41 * KIB, [P, I], U8, "scale_g")
+        nc.vector.tensor_copy(scale_g[:], scale_win[:].indirect(slots[:]))
         q_codes = tile([P, Q], U32, "q_codes")
         q_scales = tile([P, Q], U8, "q_scales")
         quantize(q_codes[:], q_scales[:], q_bf[:])
-        scale_g.append(tile_at(28 * KIB, [P, half], U8, "scale_g1"))
-        nc.vector.tensor_copy(scale_g[1][:], scale_win[:].indirect(slots[:, half // 16 : I // 16]))
-        kn_rows = tile_at(50 * KIB, [P, 11 * KIB // 4], F32, "kn_rows")
-        nc.scalar.copy(kn_rows[:, 0:I], spread_ps[:])
+        word_g = [tile_at((42 + h) * KIB, [P, half], U16, "word_g%d" % h) for h in range(2)]
+        for h in range(2):
+            nc.vector.tensor_copy(word_g[h][:], word_win[:].indirect(slots[:, h * half // 16 : (h + 1) * half // 16]))
+
+        kn_col = [tile_at(4 * KIB, [P, 2], F32, "kn_col0"), tile_at(45 * KIB, [P, 2], F32, "kn_col1")]
+        for h in range(2):
+            turn_ps = ps.tile([P, 2, P], F32, name="turn_ps%d" % h, tag="slot_bank%d" % h)
+            for j in range(2):
+                nc.tensor.transpose(turn_ps[:, j, :], kn_g[:, (2 * h + j) * P : (2 * h + j + 1) * P], ident[:])
+            nc.scalar.copy(kn_col[h][:], turn_ps[:, :, P - 1])
+        kn_rows = tile([P, I], F32, "kn_rows")
+        for h in range(2):
+            spread_ps = ps.tile([P, half], F32, name="spread_ps%d" % h)
+            for j in range(2):
+                column = kn_col[h][:, j : j + 1]
+                nc.tensor.transpose(spread_ps[:, j * P : (j + 1) * P], column.to_broadcast([P, P]), ident[:])
+            nc.scalar.copy(kn_rows[:, h * half : (h + 1) * half], spread_ps[:])
 
         def negate_with_minimum(negated, scores, start, minimum):
             nc.vector.tensor_scalar(negated, scores, -1.0, start, ALU.mult, ALU.min, accum_out=minimum)
 
-        s_sb = tile([P, I], F32, "s_sb")
-        neg_s = tile([P, I], F32, "neg_s")
-        s_bias = tile([P, 2], F32, "s_bias")
-        for h, bank in enumerate(("slot_bank", "slot_bank2")):
+        s_sb = tile_at(6 * KIB, [P, 6 * KIB // 4], F32, "s_sb")
+
+        def key_scores(h):
             cols = slice(h * half, (h + 1) * half)
-            a_ps = ps.tile([P, half], F32, name="a_ps%d" % h, tag=bank)
+            a_ps = ps.tile([P, half], F32, name="a_ps%d" % h, tag="slot_bank%d" % h)
             nc.tensor.matmul_mx(
                 out=a_ps[:],
                 lhsT=q_codes[:].bitcast(FP8X4),
                 lhsT_scale=q_scales[:],
-                rhs=word_g[:, cols].bitcast(U8).bitcast(FP4X4),
-                rhs_scale=scale_g[h][:],
+                rhs=word_g[h][:].bitcast(U8).bitcast(FP4X4),
+                rhs_scale=scale_g[:, cols],
                 start=True,
                 stop=True,
             )
             nc.vector.scalar_tensor_tensor(s_sb[:, cols], a_ps[:], 2.0, kn_rows[:, cols], ALU.mult, ALU.subtract)
-            negate_with_minimum(neg_s[:, cols], s_sb[:, cols], s_bias[:, 0:1] if h else None, s_bias[:, h : h + 1])
 
-        h_bf = tile_at(45 * KIB + 256, [P, Q, PACK], BF16, "h_bf")
-        h_codes = tile_at(60 * KIB, [P, Q], U32, "h_codes")
+        key_scores(0)
+        h_bf = tile_at(44 * KIB, [P, Q, PACK], BF16, "h_bf")
+        cast(nc.vector.tensor_copy, h_bf, h_raw)
+        key_scores(1)
+        h_codes = tile([P, Q], U32, "h_codes")
         h_scales = tile([P, Q], U8, "h_scales")
-        v_bf = [
-            tile_at(46 * KIB + 512, [P, 256, PACK], BF16, "v_bf0"),
-            tile_at(42 * KIB + 1024 + 64, [P, 256, PACK], BF16, "v_bf1"),
-            tile_at(50 * KIB, [P, 512, PACK], BF16, "v_bf2"),
-        ]
-        v_codes = [tile_at(56 * KIB + 4 * lo, [P, hi - lo], U32, "v_codes%d" % lo) for lo, hi in GROUPS]
-        v_scales = tile([P, V], U8, "v_scales")
-        b_bias = tile([P, len(GROUPS)], F32, "b_bias")
-        neg_b = tile_at(30 * KIB, [P, V], F32, "neg_b")
-        b_ps = [ps.tile([P, hi - lo], F32, name="b_ps%d" % lo) for lo, hi in GROUPS]
+        quantize(h_codes[:], h_scales[:], h_bf[:])
+        neg_s = tile([P, I], F32, "neg_s")
+        s_bias = tile([P, 1], F32, "s_bias")
+        negate_with_minimum(neg_s[:], s_sb[:, 0:I], None, s_bias[:])
 
-        def cast_vocab(c, split):
-            lo, hi = LOADS[c]
-            cast(nc.scalar.copy, v_bf[c], v_raw[c], slice(0, split))
-            cast(gpsimd_copy, v_bf[c], v_raw[c], slice(split, hi - lo))
+        v_bf = [
+            tile_at(at, [P, CHUNK, PACK], BF16, "v_bf%d" % c)
+            for c, at in enumerate((2 * KIB + 64, 44 * KIB, 6 * KIB, 32 * KIB))
+        ]
+        for c in range(2):
+            cast(nc.scalar.copy, v_bf[c], v_raw[c], slice(0, SCALAR_COLS[c]))
+            cast(gpsimd_copy, v_bf[c], v_raw[c], slice(SCALAR_COLS[c], CHUNK))
+
+        early_codes = tile_at(10 * KIB, [P, GROUP], U32, "early_codes")
+        v_codes = [
+            early_codes[:, 0:CHUNK],
+            early_codes[:, CHUNK:GROUP],
+            tile([P, CHUNK], U32, "v_codes2")[:],
+            tile_at(20 * KIB, [P, CHUNK], U32, "v_codes3")[:],
+        ]
+        v_scales = tile([P, V], U8, "v_scales")
 
         def quantize_vocab(c):
-            lo, hi = LOADS[c]
-            g = lo // 512
-            quantize(v_codes[g][:, lo - 512 * g : hi - 512 * g], v_scales[:, lo:hi], v_bf[c][:])
+            quantize(v_codes[c], v_scales[:, c * CHUNK : (c + 1) * CHUNK], v_bf[c][:])
 
-        def vocab_scores(g):
-            lo, hi = GROUPS[g]
+        def vocab_scores(b_ps, codes, lo, hi):
             nc.tensor.matmul_mx(
-                out=b_ps[g][:],
+                out=b_ps,
                 lhsT=h_codes[:].bitcast(FP8X4),
                 lhsT_scale=h_scales[:],
-                rhs=v_codes[g][:].bitcast(FP8X4),
+                rhs=codes.bitcast(FP8X4),
                 rhs_scale=v_scales[:, lo:hi],
                 start=True,
                 stop=True,
             )
 
-        def vocab_minimum(g):
-            lo, hi = GROUPS[g]
-            start = b_bias[:, g - 1 : g] if g else None
-            negate_with_minimum(neg_b[:, lo:hi], b_ps[g][:], start, b_bias[:, g : g + 1])
-
         p_sum = tile([P, 2], F32, "p_sum")
 
         def weigh(n, p_sb, lo, hi):
             nc.scalar.activation(
-                p_sb[:], neg_s[:, lo:hi], ACT.Exp, bias=s_bias[:, 1:2], scale=-1.0, accum_out=p_sum[:, n : n + 1]
+                p_sb[:], neg_s[:, lo:hi], ACT.Exp, bias=s_bias[:], scale=-1.0, accum_out=p_sum[:, n : n + 1]
             )
 
         def scatter(lo, hi, values):
             nc.vector.tensor_copy(mixed[:].indirect(places[:, lo // 16 : hi // 16]), values)
 
-        head, mid = SCATTER_CUTS
-        cast_vocab(0, 128)
-        cast(nc.scalar.copy, h_bf, h_raw)
-        cast_vocab(1, 128)
-        quantize(h_codes[:], h_scales[:], h_bf[:])
         quantize_vocab(0)
+        p_head = tile([P, HEAD], F32, "p_head")
+        weigh(0, p_head, 0, HEAD)
+        scatter(0, HEAD, p_head[:])
         quantize_vocab(1)
-        vocab_scores(0)
-        p_head = tile_at(12 * KIB, [P, head], F32, "p_head")
-        weigh(0, p_head, 0, head)
-        scatter(0, head, p_head[:])
-        vocab_minimum(0)
-        cast_vocab(2, 288)
-        quantize_vocab(2)
-        vocab_scores(1)
-        p_rest = tile_at(16 * KIB, [P, I - head], F32, "p_rest")
-        weigh(1, p_rest, head, I)
-        scatter(head, mid, p_rest[:, 0 : mid - head])
-        vocab_minimum(1)
-        p_tail = tile_at(58 * KIB, [P, I - mid], F32, "p_tail")
-        nc.scalar.copy(p_tail[:], p_rest[:, mid - head : I - head])
-        scatter(mid, I, p_tail[:])
-
-        share = tile_at(13 * KIB, [P, 2], F32, "share")
-        minus_one = tile([P, 1], F32, "minus_one")
-        nc.gpsimd.tensor_scalar(minus_one[:], one[:], -1.0, 0.0, ALU.mult, ALU.add)
-        nc.gpsimd.tensor_scalar(share[:, 0:1], lam_sb[:], OUT_SCALE, 0.0, ALU.mult, ALU.add)
-        nc.gpsimd.tensor_scalar(share[:, 1:2], lam_sb[:], -OUT_SCALE, OUT_SCALE, ALU.mult, ALU.add)
-
-        p_total = tile([P, 1], F32, "p_total")
-        nc.gpsimd.tensor_tensor(p_total[:], p_sum[:, 0:1], p_sum[:, 1:2], ALU.add)
-        p_inverse = tile([P, 1], F32, "p_inverse")
-        nc.gpsimd.tensor_tensor(p_inverse[:], p_total[:], minus_one[:], ALU.pow)
-        p_coef = tile([P, 1], F32, "p_coef")
-        nc.gpsimd.tensor_tensor(p_coef[:], p_inverse[:], share[:, 0:1], ALU.mult)
+        b_ps = [ps.tile([P, GROUP], F32, name="b_ps%d" % g) for g in range(2)]
+        vocab_scores(b_ps[0][:], early_codes[:], 0, GROUP)
+        cast(nc.scalar.copy, v_bf[2], v_raw[2])
+        cast(nc.scalar.copy, v_bf[3], v_raw[3], slice(0, SCALAR_COLS[3]))
+        cast(nc.vector.tensor_copy, v_bf[3], v_raw[3], slice(SCALAR_COLS[3], CHUNK))
+        for c in (2, 3):
+            quantize_vocab(c)
+            vocab_scores(b_ps[1][:, (c - 2) * CHUNK : (c - 1) * CHUNK], v_codes[c], c * CHUNK, (c + 1) * CHUNK)
+        b_bias = tile([P, 2], F32, "b_bias")
+        neg_b = tile_at(12 * KIB, [P, V], F32, "neg_b")
+        for g in range(2):
+            start = b_bias[:, 0:1] if g else None
+            negate_with_minimum(neg_b[:, g * GROUP : (g + 1) * GROUP], b_ps[g][:], start, b_bias[:, g : g + 1])
+        p_rest = tile_at(20 * KIB, [P, I - HEAD], F32, "p_rest")
+        weigh(1, p_rest, HEAD, I)
+        scatter(HEAD, MID, p_rest[:, 0 : MID - HEAD])
 
         r_sum = tile([P, 1], F32, "r_sum")
         r_sb = tile([P, V], F32, "r_sb")
         nc.scalar.activation(r_sb[:], neg_b[:], ACT.Exp, bias=b_bias[:, 1:2], scale=-1.0, accum_out=r_sum[:])
         r_inverse = tile([P, 1], F32, "r_inverse")
         nc.vector.reciprocal(r_inverse[:], r_sum[:])
-        r_coef = tile([P, 1], F32, "r_coef")
-        nc.vector.tensor_scalar(r_coef[:], r_inverse[:], share[:, 1:2], None, ALU.mult)
+        p_tail = tile_at(12 * KIB, [P, I - MID], F32, "p_tail")
+        nc.scalar.copy(p_tail[:], p_rest[:, MID - HEAD : I - HEAD])
+        scatter(MID, I, p_tail[:])
 
-        for c in range(V // PIECE):
-            cols = slice(c * PIECE, (c + 1) * PIECE)
-            weights = tile_at((30 + c) * KIB, [P, PIECE], F32, "weights%d" % c)
-            nc.scalar.activation(weights[:], mixed[:, cols], ACT.Copy, scale=p_coef[:])
-            res = tile([P, PIECE], F32, "res%d" % c)
-            nc.vector.scalar_tensor_tensor(res[:], r_sb[:, cols], r_coef[:], weights[:], ALU.mult, ALU.add)
+        share = tile([P, 2], F32, "share")
+        minus_one = tile([P, 1], F32, "minus_one")
+        nc.gpsimd.tensor_scalar(minus_one[:], one[:], -1.0, 0.0, ALU.mult, ALU.add)
+        p_total = tile([P, 1], F32, "p_total")
+        nc.gpsimd.tensor_tensor(p_total[:], p_sum[:, 0:1], p_sum[:, 1:2], ALU.add)
+        p_inverse = tile([P, 1], F32, "p_inverse")
+        nc.gpsimd.tensor_tensor(p_inverse[:], p_total[:], minus_one[:], ALU.pow)
+        nc.gpsimd.tensor_scalar(share[:, 0:1], lam_sb[:], OUT_SCALE, 0.0, ALU.mult, ALU.add)
+        nc.gpsimd.tensor_scalar(share[:, 1:2], lam_sb[:], -OUT_SCALE, OUT_SCALE, ALU.mult, ALU.add)
+        p_coef = tile([P, 1], F32, "p_coef")
+        nc.gpsimd.tensor_tensor(p_coef[:], p_inverse[:], share[:, 0:1], ALU.mult)
+
+        r_coef = tile([P, 1], F32, "r_coef")
+        nc.scalar.activation(r_coef[:], share[:, 1:2], ACT.Copy, scale=r_inverse[:])
+
+        for c in range(chunks):
+            cols = slice(c * CHUNK, (c + 1) * CHUNK)
+            model = tile([P, CHUNK], F32, "model%d" % c)
+            nc.scalar.activation(model[:], r_sb[:, cols], ACT.Copy, scale=r_coef[:])
+            res = tile([P, CHUNK], F32, "res%d" % c)
+            nc.vector.scalar_tensor_tensor(res[:], mixed[:, cols], p_coef[:], model[:], ALU.mult, ALU.add)
             nc.sync.dma_start(out[:, cols], res[:])

@@ -22,7 +22,7 @@ PACK = 4
 CHUNK = 256
 GROUP = 512
 OUT_SCALE = 512.0
-KN_SPLIT = 1536
+KN_SPLIT = 1856
 KN_SLOTS = 320
 SCALAR_COLS = (192, 128, 256, 128)
 HEAD, MID = 128, 384
@@ -66,6 +66,8 @@ def tile_attend_knnlm_kernel(tc, query, keys_words, keys_scales, kn, hid, voc, l
         nc.vector.memset(kn_win[0 : P - 1, KN_SPLIT - 1 : KN_SPLIT], 0.0)
         nc.gpsimd.memset(mixed[:], 0.0)
         nc.scalar.activation(one[:], zero[:], ACT.Exp)
+        full = tile([P, 1], F32, "full")
+        nc.gpsimd.tensor_scalar(full[:], one[:], OUT_SCALE, 0.0, ALU.mult, ALU.add)
 
         def by_rows(x):
             return x.rearrange("(p j) w -> p j w", j=PACK)
@@ -213,7 +215,7 @@ def tile_attend_knnlm_kernel(tc, query, keys_words, keys_scales, kn, hid, voc, l
             quantize_vocab(c)
             vocab_scores(b_ps[1][:, (c - 2) * CHUNK : (c - 1) * CHUNK], v_codes[c], c * CHUNK, (c + 1) * CHUNK)
         b_bias = tile([P, 2], F32, "b_bias")
-        neg_b = tile_at(12 * KIB, [P, V], F32, "neg_b")
+        neg_b = tile_at(12 * KIB - 64, [P, V], F32, "neg_b")
         for g in range(2):
             start = b_bias[:, 0:1] if g else None
             negate_with_minimum(neg_b[:, g * GROUP : (g + 1) * GROUP], b_ps[g][:], start, b_bias[:, g : g + 1])
@@ -221,29 +223,22 @@ def tile_attend_knnlm_kernel(tc, query, keys_words, keys_scales, kn, hid, voc, l
         weigh(1, p_rest, HEAD, I)
         scatter(HEAD, MID, p_rest[:, 0 : MID - HEAD])
 
-        r_sum = tile([P, 1], F32, "r_sum")
+        share = tile_at(16 * KIB - 64, [P, 2], F32, "share")
+        nc.scalar.activation(share[:, 0:1], lam_sb[:], ACT.Copy, scale=OUT_SCALE)
+        nc.scalar.activation(share[:, 1:2], lam_sb[:], ACT.Identity, bias=full[:], scale=-OUT_SCALE)
+        sums = tile([P, 2], F32, "sums")
+        nc.scalar.activation(sums[:, 0:1], p_sum[:, 0:1], ACT.Identity, bias=p_sum[:, 1:2])
         r_sb = tile([P, V], F32, "r_sb")
-        nc.scalar.activation(r_sb[:], neg_b[:], ACT.Exp, bias=b_bias[:, 1:2], scale=-1.0, accum_out=r_sum[:])
-        r_inverse = tile([P, 1], F32, "r_inverse")
-        nc.vector.reciprocal(r_inverse[:], r_sum[:])
+        nc.scalar.activation(r_sb[:], neg_b[:], ACT.Exp, bias=b_bias[:, 1:2], scale=-1.0, accum_out=sums[:, 1:2])
+        inverse = tile([P, 2], F32, "inverse")
+        nc.vector.reciprocal(inverse[:], sums[:])
         p_tail = tile_at(12 * KIB, [P, I - MID], F32, "p_tail")
         nc.scalar.copy(p_tail[:], p_rest[:, MID - HEAD : I - HEAD])
         scatter(MID, I, p_tail[:])
-
-        share = tile([P, 2], F32, "share")
-        minus_one = tile([P, 1], F32, "minus_one")
-        nc.gpsimd.tensor_scalar(minus_one[:], one[:], -1.0, 0.0, ALU.mult, ALU.add)
-        p_total = tile([P, 1], F32, "p_total")
-        nc.gpsimd.tensor_tensor(p_total[:], p_sum[:, 0:1], p_sum[:, 1:2], ALU.add)
-        p_inverse = tile([P, 1], F32, "p_inverse")
-        nc.gpsimd.tensor_tensor(p_inverse[:], p_total[:], minus_one[:], ALU.pow)
-        nc.gpsimd.tensor_scalar(share[:, 0:1], lam_sb[:], OUT_SCALE, 0.0, ALU.mult, ALU.add)
-        nc.gpsimd.tensor_scalar(share[:, 1:2], lam_sb[:], -OUT_SCALE, OUT_SCALE, ALU.mult, ALU.add)
-        p_coef = tile([P, 1], F32, "p_coef")
-        nc.gpsimd.tensor_tensor(p_coef[:], p_inverse[:], share[:, 0:1], ALU.mult)
-
         r_coef = tile([P, 1], F32, "r_coef")
-        nc.scalar.activation(r_coef[:], share[:, 1:2], ACT.Copy, scale=r_inverse[:])
+        nc.scalar.activation(r_coef[:], share[:, 1:2], ACT.Copy, scale=inverse[:, 1:2])
+        p_coef = tile([P, 1], F32, "p_coef")
+        nc.scalar.activation(p_coef[:], share[:, 0:1], ACT.Copy, scale=inverse[:, 0:1])
 
         for c in range(chunks):
             cols = slice(c * CHUNK, (c + 1) * CHUNK)

@@ -22,10 +22,10 @@ PACK = 4
 CHUNK = 256
 GROUP = 512
 OUT_SCALE = 512.0
-KN_SPLIT = 1856
+KN_SPLIT = 1536
 KN_SLOTS = 320
-SCALAR_COLS = (192, 128, 256, 128)
-HEAD, MID = 128, 384
+SCALAR_COLS = 128
+HEAD, MID = 192, 320
 KIB = 1024
 
 
@@ -46,14 +46,14 @@ def tile_attend_knnlm_kernel(tc, query, keys_words, keys_scales, kn, hid, voc, l
         slots = tile([P, I // 16], U16, "slots")
         places = tile([P, I // 16], U16, "places")
         kn_win = tile_at(40 * KIB, [P, T], F32, "kn_win")
-        word_win = tile_at(0, [P, T], U16, "word_win")
+        word_win = tile([P, T], U16, "word_win")
         scale_win = tile([P, T], U8, "scale_win")
         mixed = tile([P, V], F32, "mixed")
         ident = tile([P, P], F32, "ident")
         zero = tile([P, 1], F32, "zero")
         one = tile([P, 1], F32, "one")
         lam_sb = tile([P, 1], F32, "lam_sb")
-        q_raw = tile([P, PACK, Q], F32, "q_raw")
+        q_raw = tile_at(52 * KIB, [P, PACK, Q], F32, "q_raw")
         h_raw = tile([P, PACK, Q], F32, "h_raw")
         v_raw = [tile_at(at * KIB, [P, PACK, CHUNK], F32, "v_raw%d" % at) for at in (24, 28, 32, 12)]
 
@@ -66,8 +66,6 @@ def tile_attend_knnlm_kernel(tc, query, keys_words, keys_scales, kn, hid, voc, l
         nc.vector.memset(kn_win[0 : P - 1, KN_SPLIT - 1 : KN_SPLIT], 0.0)
         nc.gpsimd.memset(mixed[:], 0.0)
         nc.scalar.activation(one[:], zero[:], ACT.Exp)
-        full = tile([P, 1], F32, "full")
-        nc.gpsimd.tensor_scalar(full[:], one[:], OUT_SCALE, 0.0, ALU.mult, ALU.add)
 
         def by_rows(x):
             return x.rearrange("(p j) w -> p j w", j=PACK)
@@ -95,9 +93,6 @@ def tile_attend_knnlm_kernel(tc, query, keys_words, keys_scales, kn, hid, voc, l
                 raw[:, :, cols].rearrange("p t (c i) -> p c t i", i=4),
             )
 
-        def gpsimd_copy(dst, src):
-            nc.gpsimd.tensor_scalar(dst, src, 1.0, 0.0, ALU.mult, ALU.add)
-
         def quantize(codes, scales, grouped):
             nc.vector.quantize_mx(out=codes.bitcast(FP8X4), scales=scales, in_=grouped.rearrange("p w j -> p (w j)"))
 
@@ -106,34 +101,34 @@ def tile_attend_knnlm_kernel(tc, query, keys_words, keys_scales, kn, hid, voc, l
         nc.vector.tensor_copy(kn_g[:, 0:KN_SLOTS], kn_win[:].indirect(slots[:, 0 : KN_SLOTS // 16]))
         nc.scalar.activation(kn_g[:, KN_SLOTS:I], kn_win[:].indirect(slots[:, KN_SLOTS // 16 : I // 16]), ACT.Copy)
         q_bf = tile_at(40 * KIB, [P, Q, PACK], BF16, "q_bf")
-        cast(nc.vector.tensor_copy, q_bf, q_raw)
+        cast(nc.scalar.copy, q_bf, q_raw)
         scale_g = tile_at(41 * KIB, [P, I], U8, "scale_g")
         nc.vector.tensor_copy(scale_g[:], scale_win[:].indirect(slots[:]))
         q_codes = tile([P, Q], U32, "q_codes")
         q_scales = tile([P, Q], U8, "q_scales")
         quantize(q_codes[:], q_scales[:], q_bf[:])
-        word_g = [tile_at((42 + h) * KIB, [P, half], U16, "word_g%d" % h) for h in range(2)]
+        word_g = [tile_at(52 * KIB + h * 2 * half, [P, half], U16, "word_g%d" % h) for h in range(2)]
         for h in range(2):
             nc.vector.tensor_copy(word_g[h][:], word_win[:].indirect(slots[:, h * half // 16 : (h + 1) * half // 16]))
 
-        kn_col = [tile_at(4 * KIB, [P, 2], F32, "kn_col0"), tile_at(45 * KIB, [P, 2], F32, "kn_col1")]
+        blocks = I // P
+        turn_ps = ps.tile([P, blocks, P], F32, name="turn_ps")
+        for j in range(blocks):
+            nc.tensor.transpose(turn_ps[:, j, :], kn_g[:, j * P : (j + 1) * P], ident[:])
+        kn_col = tile_at(4 * KIB, [P, blocks], F32, "kn_col")
+        nc.scalar.copy(kn_col[:], turn_ps[:, :, P - 1])
+        kn_rows = [tile([P, half], F32, "kn_rows0"), tile_at(46 * KIB, [P, half], F32, "kn_rows1")]
         for h in range(2):
-            turn_ps = ps.tile([P, 2, P], F32, name="turn_ps%d" % h, tag="slot_bank%d" % h)
+            spread_ps = ps.tile([P, half], F32, name="spread_ps%d" % h, tag="slot_bank%d" % h)
             for j in range(2):
-                nc.tensor.transpose(turn_ps[:, j, :], kn_g[:, (2 * h + j) * P : (2 * h + j + 1) * P], ident[:])
-            nc.scalar.copy(kn_col[h][:], turn_ps[:, :, P - 1])
-        kn_rows = tile([P, I], F32, "kn_rows")
-        for h in range(2):
-            spread_ps = ps.tile([P, half], F32, name="spread_ps%d" % h)
-            for j in range(2):
-                column = kn_col[h][:, j : j + 1]
+                column = kn_col[:, 2 * h + j : 2 * h + j + 1]
                 nc.tensor.transpose(spread_ps[:, j * P : (j + 1) * P], column.to_broadcast([P, P]), ident[:])
-            nc.scalar.copy(kn_rows[:, h * half : (h + 1) * half], spread_ps[:])
+            nc.scalar.copy(kn_rows[h][:, 0:half], spread_ps[:])
 
         def negate_with_minimum(negated, scores, start, minimum):
             nc.vector.tensor_scalar(negated, scores, -1.0, start, ALU.mult, ALU.min, accum_out=minimum)
 
-        s_sb = tile_at(6 * KIB, [P, 6 * KIB // 4], F32, "s_sb")
+        s_sb = tile_at(8 * KIB, [P, I], F32, "s_sb")
 
         def key_scores(h):
             cols = slice(h * half, (h + 1) * half)
@@ -147,28 +142,21 @@ def tile_attend_knnlm_kernel(tc, query, keys_words, keys_scales, kn, hid, voc, l
                 start=True,
                 stop=True,
             )
-            nc.vector.scalar_tensor_tensor(s_sb[:, cols], a_ps[:], 2.0, kn_rows[:, cols], ALU.mult, ALU.subtract)
+            nc.vector.scalar_tensor_tensor(s_sb[:, cols], a_ps[:], 2.0, kn_rows[h][:, 0:half], ALU.mult, ALU.subtract)
 
-        key_scores(0)
-        h_bf = tile_at(44 * KIB, [P, Q, PACK], BF16, "h_bf")
+        h_bf = tile_at(53 * KIB, [P, Q, PACK], BF16, "h_bf")
         cast(nc.vector.tensor_copy, h_bf, h_raw)
-        key_scores(1)
+        v_bf = {c: tile_at(at * KIB, [P, CHUNK, PACK], BF16, "v_bf%d" % c) for c, at in ((0, 4), (2, 28), (3, 32))}
+        v_bf_halves = [tile_at(at * KIB, [P, SCALAR_COLS, PACK], BF16, "v_bf_half%d" % at) for at in (24, 8)]
+        cast(nc.scalar.copy, v_bf[0], v_raw[0])
+        key_scores(0)
         h_codes = tile([P, Q], U32, "h_codes")
         h_scales = tile([P, Q], U8, "h_scales")
         quantize(h_codes[:], h_scales[:], h_bf[:])
-        neg_s = tile([P, I], F32, "neg_s")
-        s_bias = tile([P, 1], F32, "s_bias")
-        negate_with_minimum(neg_s[:], s_sb[:, 0:I], None, s_bias[:])
+        key_scores(1)
+        cast(nc.scalar.copy, v_bf_halves[0], v_raw[1][:, :, 0:SCALAR_COLS])
 
-        v_bf = [
-            tile_at(at, [P, CHUNK, PACK], BF16, "v_bf%d" % c)
-            for c, at in enumerate((2 * KIB + 64, 44 * KIB, 6 * KIB, 32 * KIB))
-        ]
-        for c in range(2):
-            cast(nc.scalar.copy, v_bf[c], v_raw[c], slice(0, SCALAR_COLS[c]))
-            cast(gpsimd_copy, v_bf[c], v_raw[c], slice(SCALAR_COLS[c], CHUNK))
-
-        early_codes = tile_at(10 * KIB, [P, GROUP], U32, "early_codes")
+        early_codes = tile_at(46 * KIB, [P, GROUP], U32, "early_codes")
         v_codes = [
             early_codes[:, 0:CHUNK],
             early_codes[:, CHUNK:GROUP],
@@ -202,48 +190,60 @@ def tile_attend_knnlm_kernel(tc, query, keys_words, keys_scales, kn, hid, voc, l
             nc.vector.tensor_copy(mixed[:].indirect(places[:, lo // 16 : hi // 16]), values)
 
         quantize_vocab(0)
+        neg_s = tile([P, I], F32, "neg_s")
+        s_bias = tile([P, 1], F32, "s_bias")
+        negate_with_minimum(neg_s[:], s_sb[:, 0:I], None, s_bias[:])
+        cast(nc.vector.tensor_copy, v_bf_halves[1], v_raw[1][:, :, SCALAR_COLS:CHUNK])
+        for h in range(2):
+            cols = slice(CHUNK + h * SCALAR_COLS, CHUNK + (h + 1) * SCALAR_COLS)
+            quantize(early_codes[:, cols], v_scales[:, cols], v_bf_halves[h][:])
+        b_ps = [ps.tile([P, GROUP], F32, name="b_ps%d" % g) for g in range(2)]
+        vocab_scores(b_ps[0][:], early_codes[:], 0, GROUP)
         p_head = tile([P, HEAD], F32, "p_head")
         weigh(0, p_head, 0, HEAD)
         scatter(0, HEAD, p_head[:])
-        quantize_vocab(1)
-        b_ps = [ps.tile([P, GROUP], F32, name="b_ps%d" % g) for g in range(2)]
-        vocab_scores(b_ps[0][:], early_codes[:], 0, GROUP)
-        cast(nc.scalar.copy, v_bf[2], v_raw[2])
-        cast(nc.scalar.copy, v_bf[3], v_raw[3], slice(0, SCALAR_COLS[3]))
-        cast(nc.vector.tensor_copy, v_bf[3], v_raw[3], slice(SCALAR_COLS[3], CHUNK))
-        for c in (2, 3):
-            quantize_vocab(c)
-            vocab_scores(b_ps[1][:, (c - 2) * CHUNK : (c - 1) * CHUNK], v_codes[c], c * CHUNK, (c + 1) * CHUNK)
         b_bias = tile([P, 2], F32, "b_bias")
-        neg_b = tile_at(12 * KIB - 64, [P, V], F32, "neg_b")
-        for g in range(2):
-            start = b_bias[:, 0:1] if g else None
-            negate_with_minimum(neg_b[:, g * GROUP : (g + 1) * GROUP], b_ps[g][:], start, b_bias[:, g : g + 1])
-        p_rest = tile_at(20 * KIB, [P, I - HEAD], F32, "p_rest")
+        neg_b = tile_at(16 * KIB, [P, V], F32, "neg_b")
+        negate_with_minimum(neg_b[:, 0:GROUP], b_ps[0][:], None, b_bias[:, 0:1])
+        cast(nc.scalar.copy, v_bf[2], v_raw[2])
+        cast(nc.scalar.copy, v_bf[3], v_raw[3], slice(0, SCALAR_COLS))
+        quantize_vocab(2)
+        vocab_scores(b_ps[1][:, 0:CHUNK], v_codes[2], 2 * CHUNK, 3 * CHUNK)
+        cast(nc.vector.tensor_copy, v_bf[3], v_raw[3], slice(SCALAR_COLS, CHUNK))
+        quantize_vocab(3)
+        vocab_scores(b_ps[1][:, CHUNK:GROUP], v_codes[3], 3 * CHUNK, V)
+        p_rest = tile_at(28 * KIB, [P, I - HEAD], F32, "p_rest")
         weigh(1, p_rest, HEAD, I)
         scatter(HEAD, MID, p_rest[:, 0 : MID - HEAD])
-
-        share = tile_at(16 * KIB - 64, [P, 2], F32, "share")
-        nc.scalar.activation(share[:, 0:1], lam_sb[:], ACT.Copy, scale=OUT_SCALE)
-        nc.scalar.activation(share[:, 1:2], lam_sb[:], ACT.Identity, bias=full[:], scale=-OUT_SCALE)
-        sums = tile([P, 2], F32, "sums")
-        nc.scalar.activation(sums[:, 0:1], p_sum[:, 0:1], ACT.Identity, bias=p_sum[:, 1:2])
-        r_sb = tile([P, V], F32, "r_sb")
-        nc.scalar.activation(r_sb[:], neg_b[:], ACT.Exp, bias=b_bias[:, 1:2], scale=-1.0, accum_out=sums[:, 1:2])
-        inverse = tile([P, 2], F32, "inverse")
-        nc.vector.reciprocal(inverse[:], sums[:])
-        p_tail = tile_at(12 * KIB, [P, I - MID], F32, "p_tail")
+        negate_with_minimum(neg_b[:, GROUP:V], b_ps[1][:], b_bias[:, 0:1], b_bias[:, 1:2])
+        p_tail = tile_at(20 * KIB, [P, I - MID], F32, "p_tail")
         nc.scalar.copy(p_tail[:], p_rest[:, MID - HEAD : I - HEAD])
         scatter(MID, I, p_tail[:])
-        r_coef = tile([P, 1], F32, "r_coef")
-        nc.scalar.activation(r_coef[:], share[:, 1:2], ACT.Copy, scale=inverse[:, 1:2])
+
+        share = tile([P, 2], F32, "share")
+        minus_one = tile([P, 1], F32, "minus_one")
+        nc.gpsimd.tensor_scalar(minus_one[:], one[:], -1.0, 0.0, ALU.mult, ALU.add)
+        nc.gpsimd.tensor_scalar(share[:, 0:1], lam_sb[:], OUT_SCALE, 0.0, ALU.mult, ALU.add)
+        nc.gpsimd.tensor_scalar(share[:, 1:2], lam_sb[:], -OUT_SCALE, OUT_SCALE, ALU.mult, ALU.add)
+        p_total = tile([P, 1], F32, "p_total")
+        nc.gpsimd.tensor_tensor(p_total[:], p_sum[:, 0:1], p_sum[:, 1:2], ALU.add)
+        p_inverse = tile([P, 1], F32, "p_inverse")
+        nc.gpsimd.tensor_tensor(p_inverse[:], p_total[:], minus_one[:], ALU.pow)
         p_coef = tile([P, 1], F32, "p_coef")
-        nc.scalar.activation(p_coef[:], share[:, 0:1], ACT.Copy, scale=inverse[:, 0:1])
+        nc.gpsimd.tensor_tensor(p_coef[:], p_inverse[:], share[:, 0:1], ALU.mult)
+
+        r_sum = tile([P, 1], F32, "r_sum")
+        r_sb = tile([P, V], F32, "r_sb")
+        nc.scalar.activation(r_sb[:], neg_b[:], ACT.Exp, bias=b_bias[:, 1:2], scale=-1.0, accum_out=r_sum[:])
+        r_inverse = tile([P, 1], F32, "r_inverse")
+        nc.vector.reciprocal(r_inverse[:], r_sum[:])
+        r_coef = tile([P, 1], F32, "r_coef")
+        nc.vector.tensor_scalar(r_coef[:], r_inverse[:], share[:, 1:2], None, ALU.mult)
 
         for c in range(chunks):
             cols = slice(c * CHUNK, (c + 1) * CHUNK)
-            model = tile([P, CHUNK], F32, "model%d" % c)
-            nc.scalar.activation(model[:], r_sb[:, cols], ACT.Copy, scale=r_coef[:])
+            weights = tile_at((16 + c) * KIB, [P, CHUNK], F32, "weights%d" % c)
+            nc.scalar.activation(weights[:], mixed[:, cols], ACT.Copy, scale=p_coef[:])
             res = tile([P, CHUNK], F32, "res%d" % c)
-            nc.vector.scalar_tensor_tensor(res[:], mixed[:, cols], p_coef[:], model[:], ALU.mult, ALU.add)
+            nc.vector.scalar_tensor_tensor(res[:], r_sb[:, cols], r_coef[:], weights[:], ALU.mult, ALU.add)
             nc.sync.dma_start(out[:, cols], res[:])

@@ -24,8 +24,8 @@ GROUP = 512
 OUT_SCALE = 512.0
 KN_SPLIT = 1536
 KN_SLOTS = 320
-SCALAR_COLS = 128
-HEAD, MID = 192, 320
+SCALAR_COLS = {1: 160, 2: 128, 3: 176}
+HEAD, MID = 160, 288
 KIB = 1024
 
 
@@ -96,6 +96,9 @@ def tile_attend_knnlm_kernel(tc, query, keys_words, keys_scales, kn, hid, voc, l
         def quantize(codes, scales, grouped):
             nc.vector.quantize_mx(out=codes.bitcast(FP8X4), scales=scales, in_=grouped.rearrange("p w j -> p (w j)"))
 
+        def gpsimd_copy(dst, src):
+            nc.gpsimd.tensor_scalar(dst, src, 1.0, 0.0, ALU.mult, ALU.add)
+
         half = I // 2
         kn_g = tile([P, I], F32, "kn_g")
         nc.vector.tensor_copy(kn_g[:, 0:KN_SLOTS], kn_win[:].indirect(slots[:, 0 : KN_SLOTS // 16]))
@@ -146,15 +149,20 @@ def tile_attend_knnlm_kernel(tc, query, keys_words, keys_scales, kn, hid, voc, l
 
         h_bf = tile_at(53 * KIB, [P, Q, PACK], BF16, "h_bf")
         cast(nc.vector.tensor_copy, h_bf, h_raw)
-        v_bf = {c: tile_at(at * KIB, [P, CHUNK, PACK], BF16, "v_bf%d" % c) for c, at in ((0, 4), (2, 28), (3, 32))}
-        v_bf_halves = [tile_at(at * KIB, [P, SCALAR_COLS, PACK], BF16, "v_bf_half%d" % at) for at in (24, 8)]
+        v_bf = [
+            tile_at(at * KIB, [P, CHUNK, PACK], BF16, "v_bf%d" % c) for c, at in enumerate((4, 53, 53, 46))
+        ]
+
+        def cast_shared(c):
+            cast(nc.scalar.copy, v_bf[c], v_raw[c], slice(0, SCALAR_COLS[c]))
+            cast(gpsimd_copy, v_bf[c], v_raw[c], slice(SCALAR_COLS[c], CHUNK))
+
         cast(nc.scalar.copy, v_bf[0], v_raw[0])
         key_scores(0)
         h_codes = tile([P, Q], U32, "h_codes")
         h_scales = tile([P, Q], U8, "h_scales")
         quantize(h_codes[:], h_scales[:], h_bf[:])
         key_scores(1)
-        cast(nc.scalar.copy, v_bf_halves[0], v_raw[1][:, :, 0:SCALAR_COLS])
 
         early_codes = tile_at(46 * KIB, [P, GROUP], U32, "early_codes")
         v_codes = [
@@ -179,7 +187,7 @@ def tile_attend_knnlm_kernel(tc, query, keys_words, keys_scales, kn, hid, voc, l
                 stop=True,
             )
 
-        p_sum = tile([P, 2], F32, "p_sum")
+        p_sum = tile([P, 3], F32, "p_sum")
 
         def weigh(n, p_sb, lo, hi):
             nc.scalar.activation(
@@ -190,43 +198,40 @@ def tile_attend_knnlm_kernel(tc, query, keys_words, keys_scales, kn, hid, voc, l
             nc.vector.tensor_copy(mixed[:].indirect(places[:, lo // 16 : hi // 16]), values)
 
         quantize_vocab(0)
+        cast_shared(1)
         neg_s = tile([P, I], F32, "neg_s")
         s_bias = tile([P, 1], F32, "s_bias")
         negate_with_minimum(neg_s[:], s_sb[:, 0:I], None, s_bias[:])
-        cast(nc.vector.tensor_copy, v_bf_halves[1], v_raw[1][:, :, SCALAR_COLS:CHUNK])
-        for h in range(2):
-            cols = slice(CHUNK + h * SCALAR_COLS, CHUNK + (h + 1) * SCALAR_COLS)
-            quantize(early_codes[:, cols], v_scales[:, cols], v_bf_halves[h][:])
+        quantize_vocab(1)
         b_ps = [ps.tile([P, GROUP], F32, name="b_ps%d" % g) for g in range(2)]
         vocab_scores(b_ps[0][:], early_codes[:], 0, GROUP)
-        p_head = tile([P, HEAD], F32, "p_head")
+        p_head = tile_at(28 * KIB, [P, HEAD], F32, "p_head")
         weigh(0, p_head, 0, HEAD)
         scatter(0, HEAD, p_head[:])
         b_bias = tile([P, 2], F32, "b_bias")
         neg_b = tile_at(16 * KIB, [P, V], F32, "neg_b")
         negate_with_minimum(neg_b[:, 0:GROUP], b_ps[0][:], None, b_bias[:, 0:1])
-        cast(nc.scalar.copy, v_bf[2], v_raw[2])
-        cast(nc.scalar.copy, v_bf[3], v_raw[3], slice(0, SCALAR_COLS))
+        cast_shared(2)
+        cast_shared(3)
         quantize_vocab(2)
         vocab_scores(b_ps[1][:, 0:CHUNK], v_codes[2], 2 * CHUNK, 3 * CHUNK)
-        cast(nc.vector.tensor_copy, v_bf[3], v_raw[3], slice(SCALAR_COLS, CHUNK))
         quantize_vocab(3)
         vocab_scores(b_ps[1][:, CHUNK:GROUP], v_codes[3], 3 * CHUNK, V)
-        p_rest = tile_at(28 * KIB, [P, I - HEAD], F32, "p_rest")
-        weigh(1, p_rest, HEAD, I)
-        scatter(HEAD, MID, p_rest[:, 0 : MID - HEAD])
+        p_mid = tile_at(12 * KIB, [P, MID - HEAD], F32, "p_mid")
+        weigh(1, p_mid, HEAD, MID)
+        scatter(HEAD, MID, p_mid[:])
         negate_with_minimum(neg_b[:, GROUP:V], b_ps[1][:], b_bias[:, 0:1], b_bias[:, 1:2])
         p_tail = tile_at(20 * KIB, [P, I - MID], F32, "p_tail")
-        nc.scalar.copy(p_tail[:], p_rest[:, MID - HEAD : I - HEAD])
+        weigh(2, p_tail, MID, I)
         scatter(MID, I, p_tail[:])
 
-        share = tile([P, 2], F32, "share")
+        share = tile_at(14 * KIB, [P, 2], F32, "share")
         minus_one = tile([P, 1], F32, "minus_one")
         nc.gpsimd.tensor_scalar(minus_one[:], one[:], -1.0, 0.0, ALU.mult, ALU.add)
         nc.gpsimd.tensor_scalar(share[:, 0:1], lam_sb[:], OUT_SCALE, 0.0, ALU.mult, ALU.add)
         nc.gpsimd.tensor_scalar(share[:, 1:2], lam_sb[:], -OUT_SCALE, OUT_SCALE, ALU.mult, ALU.add)
         p_total = tile([P, 1], F32, "p_total")
-        nc.gpsimd.tensor_tensor(p_total[:], p_sum[:, 0:1], p_sum[:, 1:2], ALU.add)
+        nc.gpsimd.tensor_scalar(p_total[:], p_sum[:, 0:1], p_sum[:, 1:2], p_sum[:, 2:3], ALU.add, ALU.add)
         p_inverse = tile([P, 1], F32, "p_inverse")
         nc.gpsimd.tensor_tensor(p_inverse[:], p_total[:], minus_one[:], ALU.pow)
         p_coef = tile([P, 1], F32, "p_coef")
@@ -237,13 +242,15 @@ def tile_attend_knnlm_kernel(tc, query, keys_words, keys_scales, kn, hid, voc, l
         nc.scalar.activation(r_sb[:], neg_b[:], ACT.Exp, bias=b_bias[:, 1:2], scale=-1.0, accum_out=r_sum[:])
         r_inverse = tile([P, 1], F32, "r_inverse")
         nc.vector.reciprocal(r_inverse[:], r_sum[:])
+        scaled = [tile_at((16 + c) * KIB, [P, CHUNK], F32, "weights%d" % c) for c in range(chunks)]
+        nc.vector.tensor_scalar(scaled[0][:], mixed[:, 0:CHUNK], p_coef[:], None, ALU.mult)
         r_coef = tile([P, 1], F32, "r_coef")
         nc.vector.tensor_scalar(r_coef[:], r_inverse[:], share[:, 1:2], None, ALU.mult)
 
         for c in range(chunks):
             cols = slice(c * CHUNK, (c + 1) * CHUNK)
-            weights = tile_at((16 + c) * KIB, [P, CHUNK], F32, "weights%d" % c)
-            nc.scalar.activation(weights[:], mixed[:, cols], ACT.Copy, scale=p_coef[:])
+            if c:
+                nc.scalar.activation(scaled[c][:], mixed[:, cols], ACT.Copy, scale=p_coef[:])
             res = tile([P, CHUNK], F32, "res%d" % c)
-            nc.vector.scalar_tensor_tensor(res[:], r_sb[:, cols], r_coef[:], weights[:], ALU.mult, ALU.add)
+            nc.vector.scalar_tensor_tensor(res[:], r_sb[:, cols], r_coef[:], scaled[c][:], ALU.mult, ALU.add)
             nc.sync.dma_start(out[:, cols], res[:])

@@ -54,7 +54,10 @@ def tile_attend_knnlm_kernel(tc, query, keys_words, keys_scales, kn, hid, voc, l
         one = tile([P, 1], F32, "one")
         lam_sb = tile([P, 1], F32, "lam_sb")
         q_raw = tile_at(52 * KIB, [P, PACK, Q], F32, "q_raw")
-        h_raw = tile([P, PACK, Q], F32, "h_raw")
+        half = I // 2
+        score_row = tile([P, 4 * half - 32], F32, "score_row")
+        neg_s = score_row[:, 0:I]
+        h_raw = score_row[:, half - 16 : 3 * half - 16].rearrange("p (j w) -> p j w", j=PACK)
         v_raw = [tile_at(at * KIB, [P, PACK, CHUNK], F32, "v_raw%d" % at) for at in (24, 28, 32, 12)]
 
         nc.gpsimd.memset(ident[:], 0.0)
@@ -79,7 +82,7 @@ def tile_attend_knnlm_kernel(tc, query, keys_words, keys_scales, kn, hid, voc, l
         for r in range(4):
             nc.sync.dma_start(scale_win[r:P:32, :].bitcast(I32), keys_scales[0, r:16:4, :].bitcast(I32))
         nc.sync.dma_start(word_win[:].bitcast(I32), keys_words[0].bitcast(I32))
-        nc.sync.dma_start(h_raw[:], by_rows(hid))
+        nc.sync.dma_start(h_raw, by_rows(hid))
         load_vocab(0)
         load_vocab(1)
         nc.sync.dma_start(places[:], offs2)
@@ -99,13 +102,12 @@ def tile_attend_knnlm_kernel(tc, query, keys_words, keys_scales, kn, hid, voc, l
         def gpsimd_copy(dst, src):
             nc.gpsimd.tensor_scalar(dst, src, 1.0, 0.0, ALU.mult, ALU.add)
 
-        half = I // 2
         kn_g = tile([P, I], F32, "kn_g")
         nc.vector.tensor_copy(kn_g[:, 0:KN_SLOTS], kn_win[:].indirect(slots[:, 0 : KN_SLOTS // 16]))
         nc.scalar.activation(kn_g[:, KN_SLOTS:I], kn_win[:].indirect(slots[:, KN_SLOTS // 16 : I // 16]), ACT.Copy)
         q_bf = tile_at(40 * KIB, [P, Q, PACK], BF16, "q_bf")
         cast(nc.scalar.copy, q_bf, q_raw)
-        scale_g = tile_at(41 * KIB, [P, I], U8, "scale_g")
+        scale_g = tile_at(43 * KIB, [P, I], U8, "scale_g")
         nc.vector.tensor_copy(scale_g[:], scale_win[:].indirect(slots[:]))
         q_codes = tile([P, Q], U32, "q_codes")
         q_scales = tile([P, Q], U8, "q_scales")
@@ -131,7 +133,7 @@ def tile_attend_knnlm_kernel(tc, query, keys_words, keys_scales, kn, hid, voc, l
         def negate_with_minimum(negated, scores, start, minimum):
             nc.vector.tensor_scalar(negated, scores, -1.0, start, ALU.mult, ALU.min, accum_out=minimum)
 
-        s_sb = tile_at(8 * KIB, [P, I], F32, "s_sb")
+        s_sb = [tile([P, half], F32, "s_first")[:], score_row[:, 3 * half - 32 : 4 * half - 32]]
 
         def key_scores(h):
             cols = slice(h * half, (h + 1) * half)
@@ -145,12 +147,12 @@ def tile_attend_knnlm_kernel(tc, query, keys_words, keys_scales, kn, hid, voc, l
                 start=True,
                 stop=True,
             )
-            nc.vector.scalar_tensor_tensor(s_sb[:, cols], a_ps[:], 2.0, kn_rows[h][:, 0:half], ALU.mult, ALU.subtract)
+            nc.vector.scalar_tensor_tensor(s_sb[h], a_ps[:], 2.0, kn_rows[h][:, 0:half], ALU.mult, ALU.subtract)
 
-        h_bf = tile_at(53 * KIB, [P, Q, PACK], BF16, "h_bf")
-        cast(nc.vector.tensor_copy, h_bf, h_raw)
+        h_bf = tile_at(40 * KIB, [P, Q, PACK], BF16, "h_bf")
+        cast(gpsimd_copy, h_bf, h_raw)
         v_bf = [
-            tile_at(at * KIB, [P, CHUNK, PACK], BF16, "v_bf%d" % c) for c, at in enumerate((4, 53, 53, 46))
+            tile_at(at * KIB, [P, CHUNK, PACK], BF16, "v_bf%d" % c) for c, at in enumerate((4, 40, 40, 46))
         ]
 
         def cast_shared(c):
@@ -162,6 +164,8 @@ def tile_attend_knnlm_kernel(tc, query, keys_words, keys_scales, kn, hid, voc, l
         h_codes = tile([P, Q], U32, "h_codes")
         h_scales = tile([P, Q], U8, "h_scales")
         quantize(h_codes[:], h_scales[:], h_bf[:])
+        s_bias = tile([P, 2], F32, "s_bias")
+        negate_with_minimum(neg_s[:, 0:half], s_sb[0], None, s_bias[:, 0:1])
         key_scores(1)
 
         early_codes = tile_at(46 * KIB, [P, GROUP], U32, "early_codes")
@@ -191,7 +195,7 @@ def tile_attend_knnlm_kernel(tc, query, keys_words, keys_scales, kn, hid, voc, l
 
         def weigh(n, p_sb, lo, hi):
             nc.scalar.activation(
-                p_sb[:], neg_s[:, lo:hi], ACT.Exp, bias=s_bias[:], scale=-1.0, accum_out=p_sum[:, n : n + 1]
+                p_sb[:], neg_s[:, lo:hi], ACT.Exp, bias=s_bias[:, 1:2], scale=-1.0, accum_out=p_sum[:, n : n + 1]
             )
 
         def scatter(lo, hi, values):
@@ -199,9 +203,7 @@ def tile_attend_knnlm_kernel(tc, query, keys_words, keys_scales, kn, hid, voc, l
 
         quantize_vocab(0)
         cast_shared(1)
-        neg_s = tile([P, I], F32, "neg_s")
-        s_bias = tile([P, 1], F32, "s_bias")
-        negate_with_minimum(neg_s[:], s_sb[:, 0:I], None, s_bias[:])
+        negate_with_minimum(neg_s[:, half:I], s_sb[1], s_bias[:, 0:1], s_bias[:, 1:2])
         quantize_vocab(1)
         b_ps = [ps.tile([P, GROUP], F32, name="b_ps%d" % g) for g in range(2)]
         vocab_scores(b_ps[0][:], early_codes[:], 0, GROUP)

@@ -91,9 +91,10 @@ def tile_attend_knnlm_kernel(tc, query, keys_words, keys_scales, kn, hid, voc, l
         nc.sync.dma_start(lam_sb[:], lam)
 
         def cast(copy, grouped, raw, cols=slice(None)):
+            run = 8 if copy is gpsimd_copy else 4
             copy(
-                grouped[:, cols, :].rearrange("p (c i) t -> p c t i", i=4),
-                raw[:, :, cols].rearrange("p t (c i) -> p c t i", i=4),
+                grouped[:, cols, :].rearrange("p (c i) t -> p c t i", i=run),
+                raw[:, :, cols].rearrange("p t (c i) -> p c t i", i=run),
             )
 
         def quantize(codes, scales, grouped):

@@ -24,7 +24,7 @@ GROUP = 512
 OUT_SCALE = 512.0
 KN_SPLIT = 1536
 KN_SLOTS = 320
-SCALAR_COLS = {1: 160, 2: 128, 3: 176}
+SCALAR_COLS = {1: 128, 2: 128, 3: 176}
 HEAD, MID = 160, 288
 KIB = 1024
 
@@ -91,7 +91,7 @@ def tile_attend_knnlm_kernel(tc, query, keys_words, keys_scales, kn, hid, voc, l
         nc.sync.dma_start(lam_sb[:], lam)
 
         def cast(copy, grouped, raw, cols=slice(None)):
-            run = 8 if copy is gpsimd_copy else 4
+            run = 2 if copy is gpsimd_copy else 4
             copy(
                 grouped[:, cols, :].rearrange("p (c i) t -> p c t i", i=run),
                 raw[:, :, cols].rearrange("p t (c i) -> p c t i", i=run),

@@ -23,7 +23,7 @@ CHUNK = 256
 GROUP = 512
 OUT_SCALE = 512.0
 KN_SPLIT = 1536
-KN_SLOTS = 320
+KN_SLOTS = 288
 SCALAR_COLS = {1: 128, 2: 128, 3: 176}
 HEAD, MID = 160, 288
 KIB = 1024
@@ -152,9 +152,11 @@ def tile_attend_knnlm_kernel(tc, query, keys_words, keys_scales, kn, hid, voc, l
 
         h_bf = tile_at(40 * KIB, [P, Q, PACK], BF16, "h_bf")
         cast(gpsimd_copy, h_bf, h_raw)
-        v_bf = [
-            tile_at(at * KIB, [P, CHUNK, PACK], BF16, "v_bf%d" % c) for c, at in enumerate((4, 40, 40, 46))
-        ]
+        v_bf = [tile_at(at * KIB, [P, CHUNK, PACK], BF16, "v_bf%d" % c)[:] for c, at in enumerate((4, 40))]
+        late_row = tile_at(40 * KIB, [P, GROUP * PACK], BF16, "late_row")
+        for n in range(2):
+            words = late_row[:, n * CHUNK * PACK : (n + 1) * CHUNK * PACK]
+            v_bf.append(words.rearrange("p (w j) -> p w j", j=PACK))
 
         def cast_shared(c):
             cast(nc.scalar.copy, v_bf[c], v_raw[c], slice(0, SCALAR_COLS[c]))
@@ -179,7 +181,7 @@ def tile_attend_knnlm_kernel(tc, query, keys_words, keys_scales, kn, hid, voc, l
         v_scales = tile([P, V], U8, "v_scales")
 
         def quantize_vocab(c):
-            quantize(v_codes[c], v_scales[:, c * CHUNK : (c + 1) * CHUNK], v_bf[c][:])
+            quantize(v_codes[c], v_scales[:, c * CHUNK : (c + 1) * CHUNK], v_bf[c])
 
         def vocab_scores(b_ps, codes, lo, hi):
             nc.tensor.matmul_mx(

@@ -24,7 +24,7 @@ GROUP = 512
 OUT_SCALE = 512.0
 KN_SPLIT = 1536
 KN_SLOTS = 288
-SCALAR_COLS = {1: 128, 2: 128, 3: 176}
+SCALAR_COLS = {1: 128, 2: 128, 3: 144}
 HEAD, MID = 160, 288
 KIB = 1024
 

@@ -22,10 +22,10 @@ PACK = 4
 CHUNK = 256
 GROUP = 512
 OUT_SCALE = 512.0
-KN_SPLIT = 1536
+KN_SPLIT = 1408
 KN_SLOTS = 288
 SCALAR_COLS = {1: 128, 2: 128, 3: 144}
-HEAD, MID = 160, 288
+HEAD, MID = 160, 320
 KIB = 1024
 
 
@@ -49,26 +49,26 @@ def tile_attend_knnlm_kernel(tc, query, keys_words, keys_scales, kn, hid, voc, l
         word_win = tile([P, T], U16, "word_win")
         scale_win = tile([P, T], U8, "scale_win")
         mixed = tile([P, V], F32, "mixed")
-        ident = tile([P, P], F32, "ident")
-        zero = tile([P, 1], F32, "zero")
+        ident_row = tile([P, P + 1], F32, "ident_row")
+        ident = ident_row[:, 0:P]
+        zero = ident_row[:, P : P + 1]
         one = tile([P, 1], F32, "one")
         lam_sb = tile([P, 1], F32, "lam_sb")
         q_raw = tile_at(52 * KIB, [P, PACK, Q], F32, "q_raw")
         half = I // 2
-        score_row = tile([P, 4 * half - 32], F32, "score_row")
-        neg_s = score_row[:, 0:I]
-        h_raw = score_row[:, half - 16 : 3 * half - 16].rearrange("p (j w) -> p j w", j=PACK)
+        score_row = tile([P, 6 * half - 32], F32, "score_row")
+        neg_s = tile([P, I], F32, "neg_s")
+        h_raw = score_row[:, 2 * half - 16 : 4 * half - 16].rearrange("p (j w) -> p j w", j=PACK)
         v_raw = [tile_at(at * KIB, [P, PACK, CHUNK], F32, "v_raw%d" % at) for at in (24, 28, 32, 12)]
 
-        nc.gpsimd.memset(ident[:], 0.0)
         nc.gpsimd.memset(scale_win[:].bitcast(I32), 0)
-        nc.vector.memset(zero[:], 0.0)
-        make_identity(nc, ident[:], nomemset=True)
+        nc.vector.memset(ident_row[:], 0.0)
+        make_identity(nc, ident, nomemset=True)
         nc.gpsimd.memset(kn_win[0 : P - 1, KN_SPLIT:T], 0.0)
         nc.vector.memset(kn_win[0 : P - 1, 0 : KN_SPLIT - 1], 0.0)
         nc.vector.memset(kn_win[0 : P - 1, KN_SPLIT - 1 : KN_SPLIT], 0.0)
         nc.gpsimd.memset(mixed[:], 0.0)
-        nc.scalar.activation(one[:], zero[:], ACT.Exp)
+        nc.scalar.activation(one[:], zero, ACT.Exp)
 
         def by_rows(x):
             return x.rearrange("(p j) w -> p j w", j=PACK)
@@ -118,23 +118,24 @@ def tile_attend_knnlm_kernel(tc, query, keys_words, keys_scales, kn, hid, voc, l
             nc.vector.tensor_copy(word_g[h][:], word_win[:].indirect(slots[:, h * half // 16 : (h + 1) * half // 16]))
 
         blocks = I // P
-        turn_ps = ps.tile([P, blocks, P], F32, name="turn_ps")
-        for j in range(blocks):
-            nc.tensor.transpose(turn_ps[:, j, :], kn_g[:, j * P : (j + 1) * P], ident[:])
-        kn_col = tile_at(4 * KIB, [P, blocks], F32, "kn_col")
-        nc.scalar.copy(kn_col[:], turn_ps[:, :, P - 1])
-        kn_rows = [tile([P, half], F32, "kn_rows0"), tile_at(46 * KIB, [P, half], F32, "kn_rows1")]
+        kn_col = score_row[:, 6 * half - 32 - blocks : 6 * half - 32]
+        for h in range(2):
+            turn_ps = ps.tile([P, 2, P], F32, name="turn_ps%d" % h)
+            for j in range(2):
+                nc.tensor.transpose(turn_ps[:, j, :], kn_g[:, (2 * h + j) * P : (2 * h + j + 1) * P], ident)
+            nc.scalar.copy(kn_col[:, 2 * h : 2 * h + 2], turn_ps[:, :, P - 1])
+        kn_rows = [tile([P, half], F32, "kn_rows0"), tile([P, half], F32, "kn_rows1")]
         for h in range(2):
             spread_ps = ps.tile([P, half], F32, name="spread_ps%d" % h, tag="slot_bank%d" % h)
             for j in range(2):
                 column = kn_col[:, 2 * h + j : 2 * h + j + 1]
-                nc.tensor.transpose(spread_ps[:, j * P : (j + 1) * P], column.to_broadcast([P, P]), ident[:])
+                nc.tensor.transpose(spread_ps[:, j * P : (j + 1) * P], column.to_broadcast([P, P]), ident)
             nc.scalar.copy(kn_rows[h][:, 0:half], spread_ps[:])
 
         def negate_with_minimum(negated, scores, start, minimum):
             nc.vector.tensor_scalar(negated, scores, -1.0, start, ALU.mult, ALU.min, accum_out=minimum)
 
-        s_sb = [tile([P, half], F32, "s_first")[:], score_row[:, 3 * half - 32 : 4 * half - 32]]
+        s_sb = [score_row[:, 0:half], score_row[:, half:I]]
 
         def key_scores(h):
             cols = slice(h * half, (h + 1) * half)
@@ -152,7 +153,10 @@ def tile_attend_knnlm_kernel(tc, query, keys_words, keys_scales, kn, hid, voc, l
 
         h_bf = tile_at(40 * KIB, [P, Q, PACK], BF16, "h_bf")
         cast(gpsimd_copy, h_bf, h_raw)
-        v_bf = [tile_at(at * KIB, [P, CHUNK, PACK], BF16, "v_bf%d" % c)[:] for c, at in enumerate((4, 40))]
+        v_bf = [
+            score_row[:, 4 * half - 32 : 6 * half - 32].bitcast(BF16).rearrange("p (w j) -> p w j", j=PACK),
+            tile_at(40 * KIB, [P, CHUNK, PACK], BF16, "v_bf1")[:],
+        ]
         late_row = tile_at(40 * KIB, [P, GROUP * PACK], BF16, "late_row")
         for n in range(2):
             words = late_row[:, n * CHUNK * PACK : (n + 1) * CHUNK * PACK]
@@ -167,8 +171,7 @@ def tile_attend_knnlm_kernel(tc, query, keys_words, keys_scales, kn, hid, voc, l
         h_codes = tile([P, Q], U32, "h_codes")
         h_scales = tile([P, Q], U8, "h_scales")
         quantize(h_codes[:], h_scales[:], h_bf[:])
-        s_bias = tile([P, 2], F32, "s_bias")
-        negate_with_minimum(neg_s[:, 0:half], s_sb[0], None, s_bias[:, 0:1])
+        s_bias = tile([P, 1], F32, "s_bias")
         key_scores(1)
 
         early_codes = tile_at(46 * KIB, [P, GROUP], U32, "early_codes")
@@ -198,18 +201,19 @@ def tile_attend_knnlm_kernel(tc, query, keys_words, keys_scales, kn, hid, voc, l
 
         def weigh(n, p_sb, lo, hi):
             nc.scalar.activation(
-                p_sb[:], neg_s[:, lo:hi], ACT.Exp, bias=s_bias[:, 1:2], scale=-1.0, accum_out=p_sum[:, n : n + 1]
+                p_sb[:], neg_s[:, lo:hi], ACT.Exp, bias=s_bias[:], scale=-1.0, accum_out=p_sum[:, n : n + 1]
             )
 
         def scatter(lo, hi, values):
             nc.vector.tensor_copy(mixed[:].indirect(places[:, lo // 16 : hi // 16]), values)
 
-        quantize_vocab(0)
-        cast_shared(1)
-        negate_with_minimum(neg_s[:, half:I], s_sb[1], s_bias[:, 0:1], s_bias[:, 1:2])
-        quantize_vocab(1)
         b_ps = [ps.tile([P, GROUP], F32, name="b_ps%d" % g) for g in range(2)]
-        vocab_scores(b_ps[0][:], early_codes[:], 0, GROUP)
+        quantize_vocab(0)
+        vocab_scores(b_ps[0][:, 0:CHUNK], v_codes[0], 0, CHUNK)
+        cast_shared(1)
+        negate_with_minimum(neg_s[:], score_row[:, 0:I], None, s_bias[:])
+        quantize_vocab(1)
+        vocab_scores(b_ps[0][:, CHUNK:GROUP], v_codes[1], CHUNK, GROUP)
         p_head = tile_at(28 * KIB, [P, HEAD], F32, "p_head")
         weigh(0, p_head, 0, HEAD)
         scatter(0, HEAD, p_head[:])

from contextlib import ExitStack

import concourse.mybir as mybir
from concourse.masks import make_identity

D, K, T, I, V, Q = 512, 512, 2048, 512, 1024, 128
FLOPS = 2 * D * Q * I + 2 * K * Q * V

F32 = mybir.dt.float32
BF16 = mybir.dt.bfloat16
I32 = mybir.dt.int32
U16 = mybir.dt.uint16
U32 = mybir.dt.uint32
U8 = mybir.dt.uint8
FP8X4 = mybir.dt.float8_e4m3fn_x4
FP4X4 = mybir.dt.float4_e2m1fn_x4
ALU = mybir.AluOpType
ACT = mybir.ActivationFunctionType

P = 128
PACK = 4
CHUNK = 256
GROUP = 512
OUT_SCALE = 512.0
KN_SPLIT = 1408
KN_SLOTS = 288
SCALAR_COLS = {1: 128, 2: 128, 3: 144}
HEAD, MID = 160, 320
KIB = 1024


def tile_attend_knnlm_kernel(tc, query, keys_words, keys_scales, kn, hid, voc, lam, offs, offs2, out):
    nc = tc.nc
    with ExitStack() as ctx:
        sb = ctx.enter_context(tc.tile_pool(name="sb", bufs=1))
        reuse = ctx.enter_context(tc.tile_pool(name="reuse", bufs=1))
        ps = ctx.enter_context(tc.psum_pool(name="ps", bufs=1))

        def tile(shape, dtype, name):
            return sb.tile(shape, dtype, name=name, align_bytes=64)

        def tile_at(offset, shape, dtype, name):
            return reuse.tile(shape, dtype, name=name, align_bytes=64, offset=offset)

        chunks = V // CHUNK
        slots = tile([P, I // 16], U16, "slots")
        places = tile([P, I // 16], U16, "places")
        kn_win = tile_at(40 * KIB, [P, T], F32, "kn_win")
        word_win = tile([P, T], U16, "word_win")
        scale_win = tile([P, T], U8, "scale_win")
        mixed = tile([P, V], F32, "mixed")
        ident_row = tile([P, P + 1], F32, "ident_row")
        ident = ident_row[:, 0:P]
        zero = ident_row[:, P : P + 1]
        one = tile([P, 1], F32, "one")
        lam_sb = tile([P, 1], F32, "lam_sb")
        q_raw = tile_at(52 * KIB, [P, PACK, Q], F32, "q_raw")
        half = I // 2
        score_row = tile([P, 6 * half - 32], F32, "score_row")
        neg_s = tile([P, I], F32, "neg_s")
        h_raw = score_row[:, 2 * half - 16 : 4 * half - 16].rearrange("p (j w) -> p j w", j=PACK)
        v_raw = [tile_at(at * KIB, [P, PACK, CHUNK], F32, "v_raw%d" % at) for at in (24, 28, 32, 12)]

        nc.gpsimd.memset(scale_win[:].bitcast(I32), 0)
        nc.vector.memset(ident_row[:], 0.0)
        make_identity(nc, ident, nomemset=True)
        nc.gpsimd.memset(kn_win[0 : P - 1, KN_SPLIT:T], 0.0)
        nc.vector.memset(kn_win[0 : P - 1, 0 : KN_SPLIT - 1], 0.0)
        nc.vector.memset(kn_win[0 : P - 1, KN_SPLIT - 1 : KN_SPLIT], 0.0)
        nc.gpsimd.memset(mixed[:], 0.0)
        nc.scalar.activation(one[:], zero, ACT.Exp)

        def by_rows(x):
            return x.rearrange("(p j) w -> p j w", j=PACK)

        def load_vocab(c):
            nc.sync.dma_start(v_raw[c][:], by_rows(voc)[:, :, c * CHUNK : (c + 1) * CHUNK])

        nc.sync.dma_start(slots[:], offs)
        nc.sync.dma_start(kn_win[P - 1 : P, :], kn[0:1, :])
        nc.sync.dma_start(q_raw[:], by_rows(query))
        for r in range(4):
            nc.sync.dma_start(scale_win[r:P:32, :].bitcast(I32), keys_scales[0, r:16:4, :].bitcast(I32))
        nc.sync.dma_start(word_win[:].bitcast(I32), keys_words[0].bitcast(I32))
        nc.sync.dma_start(h_raw, by_rows(hid))
        load_vocab(0)
        load_vocab(1)
        nc.sync.dma_start(places[:], offs2)
        load_vocab(2)
        load_vocab(3)
        nc.sync.dma_start(lam_sb[:], lam)

        def cast(copy, grouped, raw, cols=slice(None)):
            run = 2 if copy is gpsimd_copy else 4
            copy(
                grouped[:, cols, :].rearrange("p (c i) t -> p c t i", i=run),
                raw[:, :, cols].rearrange("p t (c i) -> p c t i", i=run),
            )

        def quantize(codes, scales, grouped):
            nc.vector.quantize_mx(out=codes.bitcast(FP8X4), scales=scales, in_=grouped.rearrange("p w j -> p (w j)"))

        def gpsimd_copy(dst, src):
            nc.gpsimd.tensor_scalar(dst, src, 1.0, 0.0, ALU.mult, ALU.add)

        kn_g = tile([P, I], F32, "kn_g")
        nc.vector.tensor_copy(kn_g[:, 0:KN_SLOTS], kn_win[:].indirect(slots[:, 0 : KN_SLOTS // 16]))
        nc.scalar.activation(kn_g[:, KN_SLOTS:I], kn_win[:].indirect(slots[:, KN_SLOTS // 16 : I // 16]), ACT.Copy)
        q_bf = tile_at(40 * KIB, [P, Q, PACK], BF16, "q_bf")
        cast(nc.scalar.copy, q_bf, q_raw)
        scale_g = tile_at(43 * KIB, [P, I], U8, "scale_g")
        nc.vector.tensor_copy(scale_g[:], scale_win[:].indirect(slots[:]))
        q_codes = tile([P, Q], U32, "q_codes")
        q_scales = tile([P, Q], U8, "q_scales")
        quantize(q_codes[:], q_scales[:], q_bf[:])
        word_g = [tile_at(52 * KIB + h * 2 * half, [P, half], U16, "word_g%d" % h) for h in range(2)]
        for h in range(2):
            nc.vector.tensor_copy(word_g[h][:], word_win[:].indirect(slots[:, h * half // 16 : (h + 1) * half // 16]))

        blocks = I // P
        kn_col = score_row[:, 6 * half - 32 - blocks : 6 * half - 32]
        for h in range(2):
            turn_ps = ps.tile([P, 2, P], F32, name="turn_ps%d" % h)
            for j in range(2):
                nc.tensor.transpose(turn_ps[:, j, :], kn_g[:, (2 * h + j) * P : (2 * h + j + 1) * P], ident)
            nc.scalar.copy(kn_col[:, 2 * h : 2 * h + 2], turn_ps[:, :, P - 1])
        kn_rows = [tile([P, half], F32, "kn_rows0"), tile([P, half], F32, "kn_rows1")]
        for h in range(2):
            spread_ps = ps.tile([P, half], F32, name="spread_ps%d" % h, tag="slot_bank%d" % h)
            for j in range(2):
                column = kn_col[:, 2 * h + j : 2 * h + j + 1]
                nc.tensor.transpose(spread_ps[:, j * P : (j + 1) * P], column.to_broadcast([P, P]), ident)
            nc.scalar.copy(kn_rows[h][:, 0:half], spread_ps[:])

        def negate_with_minimum(negated, scores, start, minimum):
            nc.vector.tensor_scalar(negated, scores, -1.0, start, ALU.mult, ALU.min, accum_out=minimum)

        s_sb = [score_row[:, 0:half], score_row[:, half:I]]

        def key_scores(h):
            cols = slice(h * half, (h + 1) * half)
            a_ps = ps.tile([P, half], F32, name="a_ps%d" % h, tag="slot_bank%d" % h)
            nc.tensor.matmul_mx(
                out=a_ps[:],
                lhsT=q_codes[:].bitcast(FP8X4),
                lhsT_scale=q_scales[:],
                rhs=word_g[h][:].bitcast(U8).bitcast(FP4X4),
                rhs_scale=scale_g[:, cols],
                start=True,
                stop=True,
            )
            nc.vector.scalar_tensor_tensor(s_sb[h], a_ps[:], 2.0, kn_rows[h][:, 0:half], ALU.mult, ALU.subtract)

        h_bf = tile_at(40 * KIB, [P, Q, PACK], BF16, "h_bf")
        cast(gpsimd_copy, h_bf, h_raw)
        v_bf = [
            score_row[:, 4 * half - 32 : 6 * half - 32].bitcast(BF16).rearrange("p (w j) -> p w j", j=PACK),
            tile_at(40 * KIB, [P, CHUNK, PACK], BF16, "v_bf1")[:],
        ]
        late_row = tile_at(40 * KIB, [P, GROUP * PACK], BF16, "late_row")
        for n in range(2):
            words = late_row[:, n * CHUNK * PACK : (n + 1) * CHUNK * PACK]
            v_bf.append(words.rearrange("p (w j) -> p w j", j=PACK))

        def cast_shared(c):
            cast(nc.scalar.copy, v_bf[c], v_raw[c], slice(0, SCALAR_COLS[c]))
            cast(gpsimd_copy, v_bf[c], v_raw[c], slice(SCALAR_COLS[c], CHUNK))

        cast(nc.scalar.copy, v_bf[0], v_raw[0])
        key_scores(0)
        h_codes = tile([P, Q], U32, "h_codes")
        h_scales = tile([P, Q], U8, "h_scales")
        quantize(h_codes[:], h_scales[:], h_bf[:])
        s_bias = tile([P, 1], F32, "s_bias")
        key_scores(1)

        early_codes = tile_at(46 * KIB, [P, GROUP], U32, "early_codes")
        v_codes = [
            early_codes[:, 0:CHUNK],
            early_codes[:, CHUNK:GROUP],
            tile([P, CHUNK], U32, "v_codes2")[:],
            tile_at(20 * KIB, [P, CHUNK], U32, "v_codes3")[:],
        ]
        v_scales = tile([P, V], U8, "v_scales")

        def quantize_vocab(c):
            quantize(v_codes[c], v_scales[:, c * CHUNK : (c + 1) * CHUNK], v_bf[c])

        def vocab_scores(b_ps, codes, lo, hi):
            nc.tensor.matmul_mx(
                out=b_ps,
                lhsT=h_codes[:].bitcast(FP8X4),
                lhsT_scale=h_scales[:],
                rhs=codes.bitcast(FP8X4),
                rhs_scale=v_scales[:, lo:hi],
                start=True,
                stop=True,
            )

        p_sum = tile([P, 3], F32, "p_sum")

        def weigh(n, p_sb, lo, hi):
            nc.scalar.activation(
                p_sb[:], neg_s[:, lo:hi], ACT.Exp, bias=s_bias[:], scale=-1.0, accum_out=p_sum[:, n : n + 1]
            )

        def scatter(lo, hi, values):
            nc.vector.tensor_copy(mixed[:].indirect(places[:, lo // 16 : hi // 16]), values)

        b_ps = [ps.tile([P, GROUP], F32, name="b_ps%d" % g) for g in range(2)]
        quantize_vocab(0)
        vocab_scores(b_ps[0][:, 0:CHUNK], v_codes[0], 0, CHUNK)
        cast_shared(1)
        negate_with_minimum(neg_s[:], score_row[:, 0:I], None, s_bias[:])
        quantize_vocab(1)
        vocab_scores(b_ps[0][:, CHUNK:GROUP], v_codes[1], CHUNK, GROUP)
        p_head = tile_at(28 * KIB, [P, HEAD], F32, "p_head")
        weigh(0, p_head, 0, HEAD)
        scatter(0, HEAD, p_head[:])
        b_bias = tile([P, 2], F32, "b_bias")
        neg_b = tile_at(16 * KIB, [P, V], F32, "neg_b")
        negate_with_minimum(neg_b[:, 0:GROUP], b_ps[0][:], None, b_bias[:, 0:1])
        cast_shared(2)
        cast_shared(3)
        quantize_vocab(2)
        vocab_scores(b_ps[1][:, 0:CHUNK], v_codes[2], 2 * CHUNK, 3 * CHUNK)
        quantize_vocab(3)
        vocab_scores(b_ps[1][:, CHUNK:GROUP], v_codes[3], 3 * CHUNK, V)
        p_mid = tile_at(12 * KIB, [P, MID - HEAD], F32, "p_mid")
        weigh(1, p_mid, HEAD, MID)
        scatter(HEAD, MID, p_mid[:])
        negate_with_minimum(neg_b[:, GROUP:V], b_ps[1][:], b_bias[:, 0:1], b_bias[:, 1:2])
        p_tail = tile_at(20 * KIB, [P, I - MID], F32, "p_tail")
        weigh(2, p_tail, MID, I)
        scatter(MID, I, p_tail[:])

        share = tile_at(14 * KIB, [P, 2], F32, "share")
        minus_one = tile([P, 1], F32, "minus_one")
        nc.gpsimd.tensor_scalar(minus_one[:], one[:], -1.0, 0.0, ALU.mult, ALU.add)
        nc.gpsimd.tensor_scalar(share[:, 0:1], lam_sb[:], OUT_SCALE, 0.0, ALU.mult, ALU.add)
        nc.gpsimd.tensor_scalar(share[:, 1:2], lam_sb[:], -OUT_SCALE, OUT_SCALE, ALU.mult, ALU.add)
        p_total = tile([P, 1], F32, "p_total")
        nc.gpsimd.tensor_scalar(p_total[:], p_sum[:, 0:1], p_sum[:, 1:2], p_sum[:, 2:3], ALU.add, ALU.add)
        p_inverse = tile([P, 1], F32, "p_inverse")
        nc.gpsimd.tensor_tensor(p_inverse[:], p_total[:], minus_one[:], ALU.pow)
        p_coef = tile([P, 1], F32, "p_coef")
        nc.gpsimd.tensor_tensor(p_coef[:], p_inverse[:], share[:, 0:1], ALU.mult)

        r_sum = tile([P, 1], F32, "r_sum")
        r_sb = tile([P, V], F32, "r_sb")
        nc.scalar.activation(r_sb[:], neg_b[:], ACT.Exp, bias=b_bias[:, 1:2], scale=-1.0, accum_out=r_sum[:])
        r_inverse = tile([P, 1], F32, "r_inverse")
        nc.vector.reciprocal(r_inverse[:], r_sum[:])
        scaled = [tile_at((16 + c) * KIB, [P, CHUNK], F32, "weights%d" % c) for c in range(chunks)]
        nc.vector.tensor_scalar(scaled[0][:], mixed[:, 0:CHUNK], p_coef[:], None, ALU.mult)
        r_coef = tile([P, 1], F32, "r_coef")
        nc.vector.tensor_scalar(r_coef[:], r_inverse[:], share[:, 1:2], None, ALU.mult)

        for c in range(chunks):
            cols = slice(c * CHUNK, (c + 1) * CHUNK)
            if c:
                nc.scalar.activation(scaled[c][:], mixed[:, cols], ACT.Copy, scale=p_coef[:])
            res = tile([P, CHUNK], F32, "res%d" % c)
            nc.vector.scalar_tensor_tensor(res[:], r_sb[:, cols], r_coef[:], scaled[c][:], ALU.mult, ALU.add)
            nc.sync.dma_start(out[:, cols], res[:])
